import numpy as np
import ml_dtypes


def mxq(x, axis, fmt="e4m3"):
    dtype, down = {"e4m3": (ml_dtypes.float8_e4m3fn, 7), "e5m2": (ml_dtypes.float8_e5m2, 14)}[fmt]
    v = np.moveaxis(np.asarray(x, np.float32).astype(ml_dtypes.bfloat16).astype(np.float64), axis, -1)
    blocks = v.reshape(v.shape[:-1] + (-1, 32))
    amax = np.abs(blocks).max(-1, keepdims=True)
    byte = np.maximum(np.where(amax > 0, np.frexp(amax)[1] - 1 + 127, 0) - down, 1)
    scale = np.exp2(byte - 127.0)
    codes = (blocks / scale).astype(np.float32).astype(dtype).astype(np.float64)
    return np.moveaxis((codes * scale).reshape(v.shape), -1, axis)


WIDE = False


def mx_kscale(k):
    if not WIDE:
        return np.ones(k)
    levels = np.array([10, -10, 5, -5, 0])
    if k % 512:
        return np.exp2(np.random.permutation(np.resize(levels, k // 32))).repeat(32)
    a = np.empty((k // 512, 16))
    for p in range(k // 512):
        a[p, :8] = np.random.permutation(np.resize(levels, 8))
        for g in range(8):
            far = levels[np.abs(levels - a[p, g]) >= 10]
            a[p, g + 8] = far[np.random.randint(len(far))]
    return np.exp2(a.ravel()).repeat(32)


def f64(x):
    return np.asarray(x).astype(np.float64)


def striped(idx):
    return np.tile(idx.reshape(-1, 16).T, (8, 1)).astype(np.uint16)


def unstriped(offs):
    return offs[:16].T.reshape(-1).astype(np.int64)


E2M1 = np.array([0.0, 0.5, 1.0, 1.5, 2.0, 3.0, 4.0, 6.0, -0.0, -0.5, -1.0, -1.5, -2.0, -3.0, -4.0, -6.0])


def pack_weight(w, fmt):
    k, n = w.shape
    w = f64(np.asarray(w, np.float32).astype(ml_dtypes.bfloat16)).reshape(k // 32, 32, n)
    amax = np.abs(w).max(1)
    if fmt == "e4m3":
        byte = np.frexp(amax)[1] - 1 + 127 - 7
    else:
        mant, ex = np.frexp(amax / 6.0)
        byte = np.where(mant > 0.5, ex, ex - 1) + 127
    byte = np.clip(np.where(amax > 0, byte, 1), 1, 254)
    scaled = (w * np.exp2(127.0 - byte)[:, None, :]).reshape(k, n).astype(np.float32)
    by_word = np.ascontiguousarray(scaled.reshape(k // 512, 128, 4, n).transpose(0, 1, 3, 2))
    if fmt == "e4m3":
        words = by_word.astype(ml_dtypes.float8_e4m3fn).view(np.uint8)
    else:
        c = by_word.astype(ml_dtypes.float4_e2m1fn).view(np.uint8) & 0xF
        words = (c[..., 0::2] | (c[..., 1::2] << 4)).reshape(k // 512, 128, 2 * n)
    return np.ascontiguousarray(words), np.ascontiguousarray(byte.astype(np.uint8).reshape(k // 512, 16, n))


def unpack_weight(words, scales, fmt):
    g, _, n = scales.shape
    words = np.ascontiguousarray(words).reshape(g, 128, n, -1)
    if fmt == "e4m3":
        vals = words.view(ml_dtypes.float8_e4m3fn).astype(np.float64)
    else:
        nib = np.empty((g, 128, n, 4), np.uint8)
        nib[..., 0::2] = words & 0xF
        nib[..., 1::2] = words >> 4
        vals = E2M1[nib]
    vals = vals * np.repeat(np.exp2(scales.astype(np.float64) - 127.0), 8, axis=1)[..., None]
    return vals.transpose(0, 1, 3, 2).reshape(g * 512, n)


def gelu(v):
    return 0.5 * v * (1.0 + np.tanh(np.sqrt(2.0 / np.pi) * (v + 0.044715 * v**3)))


K, T, S, H, T2, P, N = 1024, 4096, 1024, 1024, 2048, 1024, 512

def setup_inputs():
    n = np.random.standard_normal
    s = mx_kscale(K)[:, None]
    u = mx_kscale(H)[:, None]
    tab_words, tab_scales = pack_weight(n((K, T)) * s, "e4m3")
    weg_words, weg_scales = pack_weight(n((K, H)) / np.sqrt(K) / s * u.T, "e2m1")
    wal_words, wal_scales = pack_weight(n((H, N)) / np.sqrt(H) / u, "e4m3")
    return {
        "tab_words": tab_words, "tab_scales": tab_scales,
        "offs": striped(np.random.permutation(T)[:S]),
        "win": (n((K, H)) / np.sqrt(K) / s * u.T).astype(np.float32),
        "weg_words": weg_words, "weg_scales": weg_scales,
        "drain": np.exp(0.3 * n(H)).astype(np.float32),
        "wgs": np.exp(0.3 * n((128, S))).astype(np.float32),
        "offs2": striped(np.random.permutation(T2)[:S]),
        "offs3": striped(np.random.permutation(T2)[:P]),
        "base": (np.exp(0.5 * n((H, P))) * u).astype(np.float32),
        "wal_words": wal_words, "wal_scales": wal_scales,
        "bias": (0.5 * n(N)).astype(np.float32),
    }

def reference(tab_words, tab_scales, offs, win, weg_words, weg_scales, drain, wgs, offs2, offs3, base, wal_words, wal_scales, bias):
    v = unpack_weight(tab_words, tab_scales, "e4m3")[:, unstriped(offs)]
    weg = unpack_weight(weg_words, weg_scales, "e2m1")
    ingress = mxq(f64(win), 0, "e4m3").T @ v
    egress = weg.T @ v
    h = np.abs(ingress - f64(drain)[:, None] * egress)
    page = np.zeros((H, T2))
    page[:, unstriped(offs2)] = np.tile(f64(wgs), (H // 128, 1)) * h
    x = page[:, unstriped(offs3)]
    z = mxq(f64(base) - x, 0, "e4m3")
    wal = unpack_weight(wal_words, wal_scales, "e4m3")
    y = wal.T @ z
    return y + f64(bias)[:, None]

@@ -1,0 +1,353 @@
+from contextlib import ExitStack
+
+import concourse.mybir as mybir
+from concourse.masks import make_identity
+
+K, T, S, H, T2, M, N = 1024, 4096, 1024, 1024, 2048, 1024, 512
+FLOPS = 2 * (2 * K * H * S + H * N * M)
+
+F32 = mybir.dt.float32
+BF16 = mybir.dt.bfloat16
+I32 = mybir.dt.int32
+U32 = mybir.dt.uint32
+U16 = mybir.dt.uint16
+U8 = mybir.dt.uint8
+FP8X4 = mybir.dt.float8_e4m3fn_x4
+FP4X4 = mybir.dt.float4_e2m1fn_x4
+ALU = mybir.AluOpType
+ACT = mybir.ActivationFunctionType
+
+P = 128
+PACK = 4
+PASS = P * PACK
+BANK = 512
+K_PASSES = K // PASS
+R_PASSES = H // PASS
+ROW_TILES = H // P
+TILES_PER_PASS = PASS // P
+N_TILES = N // P
+HALVES = S // BANK
+PER_COLUMN = 16
+QUARTER = 256
+WIN_CHUNKS = ((0, 1), (1, 2), (2, 4), (4, 8))
+WEG_CHUNKS = ((0, 2), (2, 8))
+
+
+def tile_list_router_queue_alarms_kernel(
+    tc, tab_words, tab_scales, offs, win, weg_words, weg_scales, drain, wgs, offs2, offs3, base,
+    wal_words, wal_scales, bias, out,
+):
+    nc = tc.nc
+    with ExitStack() as ctx:
+        held = ctx.enter_context(tc.tile_pool(name="held", bufs=1))
+        shared = ctx.enter_context(tc.tile_pool(name="shared", bufs=1))
+        psum = ctx.enter_context(tc.psum_pool(name="psum", bufs=1))
+
+        def sbuf(name, width, dtype):
+            return held.tile([P, width], dtype, name=name, align_bytes=64)
+
+        def tiles(name, count, width, dtype):
+            return [sbuf(f"{name}{i}", width, dtype) for i in range(count)]
+
+        def placed(name, width, dtype, offset):
+            return shared.tile([P, width], dtype, name=name, align_bytes=64, offset=offset)
+
+        banks = [psum.tile([P, BANK], F32, name=f"bank{i}") for i in range(8)]
+
+        idx = held.tile([P, S // PER_COLUMN], U16, name="idx")
+        idx2 = held.tile([P, S // PER_COLUMN], U16, name="idx2")
+        idx3 = held.tile([P, M // PER_COLUMN], U16, name="idx3")
+        table = [placed(f"table{a}", T, I32, 4 * T * a) for a in range(K_PASSES)]
+        table_scales = placed("table_scales", K_PASSES * T, U8, 8 * T)
+        picked = [
+            tiles("picked0_", HALVES, BANK, U32),
+            [placed(f"picked1_{half}", BANK, U32, 8 * T + 4 * BANK * half) for half in range(HALVES)],
+        ]
+        picked_scales = [placed(f"picked_scales{a}", S, U8, 4 * T2 + S * a) for a in range(K_PASSES)]
+        win_raw = [[sbuf(f"win_raw{lo}_{a}", PACK * P * (hi - lo), F32) for a in range(K_PASSES)] for lo, hi in WIN_CHUNKS]
+        win_bf = tiles("win_bf", 2, K_PASSES * P * PACK, BF16)
+        win_codes = [
+            placed("win_codes1", K_PASSES * P, U32, 4 * T + 4 * T2) if u == 1 else sbuf(f"win_codes{u}", K_PASSES * P, U32)
+            for u in range(ROW_TILES)
+        ]
+        win_scales = tiles("win_scales", ROW_TILES, K_PASSES * P, U8)
+        weg_codes = [sbuf(f"weg_codes{lo}", K_PASSES * 2 * P * (hi - lo), U8) for lo, hi in WEG_CHUNKS]
+        weg_sc = sbuf("weg_sc", K_PASSES * H, U8)
+        wal_codes = sbuf("wal_codes", R_PASSES * N, I32)
+        wal_sc = sbuf("wal_sc", R_PASSES * N, U8)
+        slot_weights = sbuf("slot_weights", S, F32)
+        baseline = tiles("baseline", TILES_PER_PASS, M, F32)
+        pages = tiles("page", 2, T2, F32)
+        pages.extend(placed(f"late_page{a}", T2, F32, 4 * T * a) for a in range(K_PASSES))
+        readings = tiles("readings", TILES_PER_PASS, S, F32)
+        polled = tiles("polled", TILES_PER_PASS, M, F32)
+        ingress = tiles("ingress", 2, BANK, F32)
+        drained = tiles("drained", 2, BANK, F32)
+        turned = tiles("turned", 4, BANK, F32)
+        z_rows = tiles("z_rows", 4, PASS, BF16)
+        z_bf = tiles("z_bf", 2, QUARTER * PACK, BF16)
+        z_codes = [tiles(f"z_codes{b}_", M // QUARTER, QUARTER, U32) for b in range(R_PASSES)]
+        z_scales = [tiles(f"z_scales{b}_", M // QUARTER, QUARTER, U8) for b in range(R_PASSES)]
+        result = tiles("result", 4, BANK, F32)
+        vectors = sbuf("vectors", P, F32)
+        minus_drain = sbuf("minus_drain", ROW_TILES, F32)
+        bias_col = sbuf("bias_col", N_TILES, F32)
+        identity = sbuf("identity", P, F32)
+
+        nc.vector.memset(table_scales[:].bitcast(I32), 0)
+        nc.vector.memset(weg_sc[:].bitcast(I32), 0)
+        nc.vector.memset(vectors[:], 0.0)
+        nc.vector.memset(wal_sc[:].bitcast(I32), 0)
+        for page in pages[:2]:
+            nc.vector.memset(page[:, 0 : T2 - 1], 0.0)
+            nc.vector.memset(page[:, T2 - 1 : T2], 0.0)
+        make_identity(nc, identity[:])
+
+        def load_scales(plane, scales):
+            for quad in range(4):
+                nc.gpsimd.dma_start(
+                    out=plane[32 * quad : 32 * quad + 4, :].bitcast(I32).rearrange("q (a c) -> q a c", a=2),
+                    in_=scales[:, 4 * quad : 4 * quad + 4, :].bitcast(I32).rearrange("a q c -> q a c"),
+                )
+
+        def load_table(a):
+            nc.sync.dma_start(out=table[a][:], in_=tab_words[a].rearrange("p t i -> p (t i)").bitcast(I32))
+
+        def load_win(chunk):
+            lo, hi = WIN_CHUNKS[chunk]
+            for a in range(K_PASSES):
+                nc.sync.dma_start(
+                    out=win_raw[chunk][a][:].rearrange("p (i r) -> p i r", i=PACK),
+                    in_=win[a * PASS : (a + 1) * PASS, lo * P : hi * P].rearrange("(p i) r -> p i r", i=PACK),
+                )
+
+        def load_weg(chunk):
+            lo, hi = WEG_CHUNKS[chunk]
+            nc.sync.dma_start(
+                out=weg_codes[chunk][:].bitcast(I32).rearrange("p (a c) -> p a c", a=K_PASSES),
+                in_=weg_words[:, :, 2 * lo * P : 2 * hi * P].bitcast(I32).rearrange("a p c -> p a c"),
+            )
+
+        def load_base(u):
+            nc.sync.dma_start(out=baseline[u % TILES_PER_PASS][:], in_=base[u * P : (u + 1) * P, :])
+
+        nc.sync.dma_start(idx[:], offs)
+        load_win(0)
+        load_table(0)
+        load_scales(table_scales, tab_scales)
+        load_weg(0)
+        load_table(1)
+        load_scales(weg_sc, weg_scales)
+        nc.gpsimd.dma_start(out=vectors[0:ROW_TILES, :], in_=drain.rearrange("(u p) -> u p", p=P))
+        nc.gpsimd.dma_start(out=vectors[ROW_TILES : ROW_TILES + N_TILES, :], in_=bias.rearrange("(c p) -> c p", p=P))
+        load_win(1)
+        nc.sync.dma_start(idx2[:], offs2)
+        nc.sync.dma_start(out=slot_weights[:], in_=wgs)
+        load_win(2)
+        load_weg(1)
+        nc.sync.dma_start(idx3[:], offs3)
+        load_base(0)
+        load_win(3)
+        for u in range(1, TILES_PER_PASS):
+            load_base(u)
+        nc.sync.dma_start(
+            out=wal_codes[:].rearrange("p (b c) -> p b c", b=R_PASSES),
+            in_=wal_words.rearrange("b p c i -> p b (c i)").bitcast(I32),
+        )
+        load_scales(wal_sc, wal_scales)
+
+        nc.tensor.transpose(banks[7][:, 0:P], vectors[:], identity[:])
+        nc.scalar.activation(minus_drain[:], banks[7][:, 0:ROW_TILES], ACT.Copy, scale=-1.0)
+        nc.scalar.copy(bias_col[:], banks[7][:, ROW_TILES : ROW_TILES + N_TILES])
+
+        def entries(offsets, start, count):
+            return offsets[:, start // PER_COLUMN : (start + count) // PER_COLUMN]
+
+        def chunk_of(chunks, u):
+            return [c for c, (lo, hi) in enumerate(chunks) if lo <= u < hi][0]
+
+        def quantize_win(u, staged):
+            chunk = chunk_of(WIN_CHUNKS, u)
+            first = (u - WIN_CHUNKS[chunk][0]) * P
+            for a in range(K_PASSES):
+                nc.scalar.copy(
+                    staged[:, a * PASS : (a + 1) * PASS].rearrange("p (r i) -> p r i", i=PACK),
+                    win_raw[chunk][a][:].rearrange("p (i r) -> p r i", i=PACK)[:, first : first + P, :],
+                )
+            nc.vector.quantize_mx(out=win_codes[u][:].bitcast(FP8X4), scales=win_scales[u][:], in_=staged)
+
+        def gather_words(a, half):
+            nc.vector.tensor_copy(picked[a][half][:], table[a][:].bitcast(U32).indirect(entries(idx, half * BANK, BANK)))
+
+        def gather_scales(a):
+            nc.vector.tensor_copy(picked_scales[a][:], table_scales[:, a * T : (a + 1) * T].indirect(idx[:]))
+
+        def project(u, half, ingress_bank, egress_bank):
+            chunk = chunk_of(WEG_CHUNKS, u)
+            lo, hi = WEG_CHUNKS[chunk]
+            for a in range(K_PASSES):
+                nc.tensor.matmul_mx(
+                    out=ingress_bank[:],
+                    lhsT=win_codes[u][:, a * P : (a + 1) * P].bitcast(FP8X4),
+                    lhsT_scale=win_scales[u][:, a * P : (a + 1) * P],
+                    rhs=picked[a][half][:].bitcast(FP8X4),
+                    rhs_scale=picked_scales[a][:, half * BANK : (half + 1) * BANK],
+                    start=a == 0,
+                    stop=a == K_PASSES - 1,
+                )
+            for a in range(K_PASSES):
+                first = 2 * P * (a * (hi - lo) + u - lo)
+                nc.tensor.matmul_mx(
+                    out=egress_bank[:],
+                    lhsT=weg_codes[chunk][:, first : first + 2 * P].bitcast(FP4X4),
+                    lhsT_scale=weg_sc[:, a * H + u * P : a * H + (u + 1) * P],
+                    rhs=picked[a][half][:].bitcast(FP8X4),
+                    rhs_scale=picked_scales[a][:, half * BANK : (half + 1) * BANK],
+                    start=a == 0,
+                    stop=a == K_PASSES - 1,
+                )
+
+        def columns(c):
+            return slice(c * P, (c + 1) * P)
+
+        def scatter(u, start, count):
+            nc.vector.tensor_tensor(
+                pages[u % TILES_PER_PASS][:].indirect(entries(idx2, start, count)),
+                readings[u % TILES_PER_PASS][:, start : start + count],
+                slot_weights[:, start : start + count],
+                ALU.mult,
+            )
+
+        def poll(u, start, count, dst):
+            nc.vector.tensor_tensor(
+                dst,
+                pages[u % TILES_PER_PASS][:].indirect(entries(idx3, start, count)),
+                baseline[u % TILES_PER_PASS][:, start : start + count],
+                ALU.subtract,
+            )
+
+        quantize_win(0, win_bf[0][:])
+        for half in range(HALVES):
+            gather_words(0, half)
+        for a in range(K_PASSES):
+            gather_scales(a)
+        for half in range(HALVES):
+            gather_words(1, half)
+        for page in pages[2:]:
+            for c in range(T2 // BANK):
+                nc.gpsimd.memset(page[:, c * BANK : (c + 1) * BANK], 0.0)
+        quantize_win(1, win_bf[1][:])
+        first_difference = [win_bf[1][:].bitcast(F32), win_bf[0][:].bitcast(F32)]
+        for half in range(HALVES):
+            ingress_bank, egress_bank = banks[4 * half], banks[4 * half + 1]
+            project(0, half, ingress_bank, egress_bank)
+            nc.scalar.copy(ingress[half][:], ingress_bank[:])
+            nc.vector.scalar_tensor_tensor(
+                first_difference[half], egress_bank[:], minus_drain[:, 0:1], ingress[half][:], ALU.mult, ALU.add
+            )
+            nc.scalar.activation(readings[0][:, half * BANK : (half + 1) * BANK], first_difference[half], ACT.Abs)
+        for half in range(HALVES):
+            scatter(0, half * BANK, BANK)
+        quantize_win(2, win_bf[0][:])
+        poll(0, 0, M, polled[0][:])
+        load_base(TILES_PER_PASS)
+
+        units = [(u, half) for u in range(1, ROW_TILES) for half in range(HALVES)]
+
+        def stage_products(n):
+            u, half = units[n]
+            project(u, half, banks[0], banks[1])
+            nc.scalar.copy(ingress[n % 2][:], banks[0][:])
+            nc.scalar.activation(drained[n % 2][:], banks[1][:], ACT.Copy, scale=minus_drain[:, u : u + 1])
+
+        def stage_difference(n):
+            for c in range(BANK // P):
+                nc.tensor.matmul(banks[2][:, columns(c)], ingress[n % 2][:, columns(c)], identity[:], start=True, stop=False, is_transpose=True)
+                nc.tensor.matmul(banks[2][:, columns(c)], drained[n % 2][:, columns(c)], identity[:], start=False, stop=True, is_transpose=True)
+            nc.scalar.activation(turned[n % 4][:], banks[2][:], ACT.Abs)
+
+        def stage_turn_back(n):
+            u, half = units[n]
+            for c in range(BANK // P):
+                nc.tensor.transpose(banks[3][:, columns(c)], turned[n % 4][:, columns(c)], identity[:])
+            nc.scalar.copy(readings[u % TILES_PER_PASS][:, half * BANK : (half + 1) * BANK], banks[3][:])
+
+        for step in range(-2, len(units)):
+            if step >= 0:
+                stage_turn_back(step)
+            if 0 <= step + 1 < len(units):
+                stage_difference(step + 1)
+            if step + 2 < len(units):
+                stage_products(step + 2)
+            if step >= 0 and step % 2 == 1:
+                u = units[step][0]
+                scatter(u, 0, S)
+                if u < TILES_PER_PASS:
+                    poll(u, 0, M, polled[u][:])
+                    load_base(u + TILES_PER_PASS)
+            if step >= 0 and step % 2 == 0 and step // 2 + 3 < ROW_TILES:
+                quantize_win(step // 2 + 3, turned[step % 4][:].bitcast(BF16))
+
+        def quantize_z(b, q, sources):
+            count = b * (M // QUARTER) + q
+            word_bank = banks[6 + count % 2]
+            for c in range(QUARTER // P):
+                for t in range(TILES_PER_PASS):
+                    nc.tensor.transpose(banks[2 + c][:, columns(t)], sources[t][:, columns(c)], identity[:])
+                rows = z_rows[(2 * count + c) % 4]
+                nc.scalar.activation(
+                    rows[:].rearrange("m (w p e) -> m w p e", w=2, e=2),
+                    banks[2 + c][:].rearrange("m (p w e) -> m w p e", w=2, e=2),
+                    ACT.Copy,
+                    scale=-1.0,
+                )
+            for c in range(QUARTER // P):
+                rows = z_rows[(2 * count + c) % 4]
+                for w in range(2):
+                    nc.tensor.transpose(word_bank[:, columns(2 * c + w)], rows[:].bitcast(F32)[:, columns(w)], identity[:])
+            staged = z_bf[count % 2]
+            nc.scalar.copy(
+                staged[:].bitcast(F32).rearrange("p (c m w) -> p c m w", c=2, w=2),
+                word_bank[:].rearrange("p (c w m) -> p c m w", c=2, w=2),
+            )
+            nc.vector.quantize_mx(out=z_codes[b][q][:].bitcast(FP8X4), scales=z_scales[b][q][:], in_=staged[:])
+
+        for q in range(M // QUARTER):
+            quantize_z(0, q, [polled[t][:, q * QUARTER : (q + 1) * QUARTER] for t in range(TILES_PER_PASS)])
+
+        def alarm_pass(b, q):
+            pair = (banks[0], banks[1]) if q % 2 == 0 else (banks[4], banks[5])
+            for c in range(N_TILES):
+                nc.tensor.matmul_mx(
+                    out=pair[c // 2][:, (c % 2) * QUARTER : (c % 2 + 1) * QUARTER],
+                    lhsT=wal_codes[:, b * N + c * P : b * N + (c + 1) * P].bitcast(FP8X4),
+                    lhsT_scale=wal_sc[:, b * N + c * P : b * N + (c + 1) * P],
+                    rhs=z_codes[b][q][:].bitcast(FP8X4),
+                    rhs_scale=z_scales[b][q][:],
+                    start=b == 0 and c % 2 == 0,
+                    stop=b == R_PASSES - 1 and c % 2 == 1,
+                )
+            return pair
+
+        last_readers = [readings[(ROW_TILES - 1) % TILES_PER_PASS], slot_weights]
+        for q in range(M // QUARTER):
+            landing = last_readers[q % 2]
+            sources = [landing[:, t * QUARTER : (t + 1) * QUARTER] for t in range(TILES_PER_PASS)]
+            for t in range(TILES_PER_PASS):
+                poll(TILES_PER_PASS + t, q * QUARTER, QUARTER, sources[t])
+            alarm_pass(0, q)
+            quantize_z(1, q, sources)
+            pair = alarm_pass(1, q)
+            for g in range(2):
+                staged = result[(2 * q + g) % 4]
+                for c in range(2):
+                    part = slice(c * QUARTER, (c + 1) * QUARTER)
+                    column = bias_col[:, 2 * g + c : 2 * g + c + 1]
+                    if q == M // QUARTER - 1 and g == 1:
+                        nc.vector.tensor_scalar_add(staged[:, part], pair[g][:, part], column)
+                    else:
+                        nc.scalar.activation(staged[:, part], pair[g][:, part], ACT.Identity, bias=column)
+                nc.sync.dma_start(
+                    out=out[2 * g * P : (2 * g + 2) * P, q * QUARTER : (q + 1) * QUARTER].rearrange("(c p) m -> p c m", p=P),
+                    in_=staged[:].rearrange("p (c m) -> p c m", c=2),
+                )

@@ -64,10 +64,21 @@ def tile_list_router_queue_alarms_kernel(
             [placed(f"picked1_{half}", BANK, U32, 8 * T + 4 * BANK * half) for half in range(HALVES)],
         ]
         picked_scales = [placed(f"picked_scales{a}", S, U8, 4 * T2 + S * a) for a in range(K_PASSES)]
-        win_raw = [[sbuf(f"win_raw{lo}_{a}", PACK * P * (hi - lo), F32) for a in range(K_PASSES)] for lo, hi in WIN_CHUNKS]
+        reused = 8 * T + K_PASSES * T
+        win_raw = [
+            [
+                placed(f"win_raw{lo}_{a}", PASS * (hi - lo), F32, reused + 4 * PASS * (K_PASSES * lo + a * (hi - lo)))
+                if hi <= TILES_PER_PASS
+                else sbuf(f"win_raw{lo}_{a}", PASS * (hi - lo), F32)
+                for a in range(K_PASSES)
+            ]
+            for lo, hi in WIN_CHUNKS
+        ]
+        woven_weights = placed("woven_weights", PACK * S, F32, reused)
+        landing = [placed(f"landing{q}", PACK * QUARTER, F32, reused + 4 * PACK * QUARTER * q) for q in range(M // QUARTER)]
         win_bf = tiles("win_bf", 2, K_PASSES * P * PACK, BF16)
         win_codes = [
-            placed("win_codes1", K_PASSES * P, U32, 4 * T + 4 * T2) if u == 1 else sbuf(f"win_codes{u}", K_PASSES * P, U32)
+            placed(f"win_codes{u}", K_PASSES * P, U32, 4 * T * u + 4 * T2 + K_PASSES * S) if u < K_PASSES else sbuf(f"win_codes{u}", K_PASSES * P, U32)
             for u in range(ROW_TILES)
         ]
         win_scales = tiles("win_scales", ROW_TILES, K_PASSES * P, U8)
@@ -81,11 +92,11 @@ def tile_list_router_queue_alarms_kernel(
         pages.extend(placed(f"late_page{a}", T2, F32, 4 * T * a) for a in range(K_PASSES))
         readings = tiles("readings", TILES_PER_PASS, S, F32)
         polled = tiles("polled", TILES_PER_PASS, M, F32)
-        ingress = tiles("ingress", 2, BANK, F32)
-        drained = tiles("drained", 2, BANK, F32)
+        ingress = tiles("ingress", TILES_PER_PASS, BANK, F32)
+        drained = tiles("drained", TILES_PER_PASS, BANK, F32)
         turned = tiles("turned", 4, BANK, F32)
         z_rows = tiles("z_rows", 4, PASS, BF16)
-        z_bf = tiles("z_bf", 2, QUARTER * PACK, BF16)
+        z_bf = tiles("z_bf", 4, QUARTER * PACK, BF16)
         z_codes = [tiles(f"z_codes{b}_", M // QUARTER, QUARTER, U32) for b in range(R_PASSES)]
         z_scales = [tiles(f"z_scales{b}_", M // QUARTER, QUARTER, U8) for b in range(R_PASSES)]
         result = tiles("result", 4, BANK, F32)
@@ -129,12 +140,15 @@ def tile_list_router_queue_alarms_kernel(
             )
 
         def load_base(u):
-            nc.sync.dma_start(out=baseline[u % TILES_PER_PASS][:], in_=base[u * P : (u + 1) * P, :])
+            nc.sync.dma_start(out=baseline[u][:], in_=base[u * P : (u + 1) * P, :])
+
+        def load_woven_base(t):
+            nc.sync.dma_start(out=baseline[t][:], in_=base[PASS:H, :].rearrange("(p t) m -> p t m", t=PACK)[:, t, :])
 
         nc.sync.dma_start(idx[:], offs)
-        load_win(0)
         load_table(0)
         load_scales(table_scales, tab_scales)
+        load_win(0)
         load_weg(0)
         load_table(1)
         load_scales(weg_sc, weg_scales)
@@ -195,7 +209,6 @@ def tile_list_router_queue_alarms_kernel(
                     start=a == 0,
                     stop=a == K_PASSES - 1,
                 )
-            for a in range(K_PASSES):
                 first = 2 * P * (a * (hi - lo) + u - lo)
                 nc.tensor.matmul_mx(
                     out=egress_bank[:],
@@ -210,11 +223,11 @@ def tile_list_router_queue_alarms_kernel(
         def columns(c):
             return slice(c * P, (c + 1) * P)
 
-        def scatter(u, start, count):
+        def scatter(u, start, count, weights):
             nc.vector.tensor_tensor(
                 pages[u % TILES_PER_PASS][:].indirect(entries(idx2, start, count)),
                 readings[u % TILES_PER_PASS][:, start : start + count],
-                slot_weights[:, start : start + count],
+                weights,
                 ALU.mult,
             )
 
@@ -226,100 +239,118 @@ def tile_list_router_queue_alarms_kernel(
                 ALU.subtract,
             )
 
-        quantize_win(0, win_bf[0][:])
         for half in range(HALVES):
             gather_words(0, half)
         for a in range(K_PASSES):
             gather_scales(a)
+        quantize_win(0, win_bf[0][:])
         for half in range(HALVES):
             gather_words(1, half)
         for page in pages[2:]:
             for c in range(T2 // BANK):
                 nc.gpsimd.memset(page[:, c * BANK : (c + 1) * BANK], 0.0)
         quantize_win(1, win_bf[1][:])
-        first_difference = [win_bf[1][:].bitcast(F32), win_bf[0][:].bitcast(F32)]
+
+        def halves(half):
+            return slice(half * BANK, (half + 1) * BANK)
+
+        def reading_on_vector(u, half, pair, staged, difference):
+            project(u, half, pair[0], pair[1])
+            nc.scalar.copy(staged, pair[0][:])
+            nc.vector.scalar_tensor_tensor(difference, pair[1][:], minus_drain[:, u : u + 1], staged, ALU.mult, ALU.add)
+            nc.scalar.activation(readings[u][:, halves(half)], difference, ACT.Abs)
+
+        reading_on_vector(0, 0, banks[0:2], ingress[0][:], win_bf[1][:].bitcast(F32))
+        reading_on_vector(0, 1, banks[4:6], ingress[1][:], win_bf[0][:].bitcast(F32))
         for half in range(HALVES):
-            ingress_bank, egress_bank = banks[4 * half], banks[4 * half + 1]
-            project(0, half, ingress_bank, egress_bank)
-            nc.scalar.copy(ingress[half][:], ingress_bank[:])
-            nc.vector.scalar_tensor_tensor(
-                first_difference[half], egress_bank[:], minus_drain[:, 0:1], ingress[half][:], ALU.mult, ALU.add
+            scatter(0, half * BANK, BANK, slot_weights[:, halves(half)])
+        quantize_win(2, win_bf[1][:])
+        quantize_win(3, win_bf[0][:])
+        for quad in range(4):
+            nc.sync.dma_start(
+                out=woven_weights[32 * quad : 32 * (quad + 1), :], in_=wgs.rearrange("(p t) j -> p (t j)", t=PACK)
             )
-            nc.scalar.activation(readings[0][:, half * BANK : (half + 1) * BANK], first_difference[half], ACT.Abs)
-        for half in range(HALVES):
-            scatter(0, half * BANK, BANK)
-        quantize_win(2, win_bf[0][:])
-        poll(0, 0, M, polled[0][:])
-        load_base(TILES_PER_PASS)
+        for u in range(1, TILES_PER_PASS):
+            reading_on_vector(u, 0, banks[2:4], polled[u - 1][:, halves(0)], turned[2][:])
+            if u == 1:
+                quantize_win(4, turned[2][:].bitcast(BF16))
+            reading_on_vector(u, 1, banks[6:8], polled[u - 1][:, halves(1)], turned[3][:])
+            poll(u - 1, 0, M, polled[u - 1][:])
+            load_woven_base(u - 1)
+            scatter(u, 0, S, slot_weights[:])
+            if u == 1:
+                quantize_win(5, turned[3][:].bitcast(BF16))
+                quantize_win(6, win_bf[1][:])
+                quantize_win(7, win_bf[0][:])
+        poll(TILES_PER_PASS - 1, 0, M, polled[TILES_PER_PASS - 1][:])
+        load_woven_base(TILES_PER_PASS - 1)
 
-        units = [(u, half) for u in range(1, ROW_TILES) for half in range(HALVES)]
+        def stage_products(half, v):
+            pair = banks[0:2] if v % 2 == 0 else banks[4:6]
+            u = TILES_PER_PASS + v
+            project(u, half, pair[0], pair[1])
+            nc.scalar.copy(ingress[v][:], pair[0][:])
+            nc.scalar.activation(drained[v][:], pair[1][:], ACT.Copy, scale=minus_drain[:, u : u + 1])
 
-        def stage_products(n):
-            u, half = units[n]
-            project(u, half, banks[0], banks[1])
-            nc.scalar.copy(ingress[n % 2][:], banks[0][:])
-            nc.scalar.activation(drained[n % 2][:], banks[1][:], ACT.Copy, scale=minus_drain[:, u : u + 1])
+        def stage_difference(c):
+            bank = banks[2 + c % 2]
+            for v in range(TILES_PER_PASS):
+                nc.tensor.matmul(bank[:, columns(v)], ingress[v][:, columns(c)], identity[:], start=True, stop=False, is_transpose=True)
+                nc.tensor.matmul(bank[:, columns(v)], drained[v][:, columns(c)], identity[:], start=False, stop=True, is_transpose=True)
+            nc.scalar.activation(
+                turned[c][:].rearrange("j (t p) -> j t p", t=PACK), bank[:].rearrange("j (p t) -> j t p", t=PACK), ACT.Abs
+            )
 
-        def stage_difference(n):
+        def stage_turn_back(half, t):
+            bank = banks[6 + t % 2]
             for c in range(BANK // P):
-                nc.tensor.matmul(banks[2][:, columns(c)], ingress[n % 2][:, columns(c)], identity[:], start=True, stop=False, is_transpose=True)
-                nc.tensor.matmul(banks[2][:, columns(c)], drained[n % 2][:, columns(c)], identity[:], start=False, stop=True, is_transpose=True)
-            nc.scalar.activation(turned[n % 4][:], banks[2][:], ACT.Abs)
+                nc.tensor.transpose(bank[:, columns(c)], turned[c][:, columns(t)], identity[:])
+            nc.scalar.copy(readings[t][:, halves(half)], bank[:])
+            scatter(t, half * BANK, BANK, woven_weights[:, t * S + half * BANK : t * S + (half + 1) * BANK])
 
-        def stage_turn_back(n):
-            u, half = units[n]
-            for c in range(BANK // P):
-                nc.tensor.transpose(banks[3][:, columns(c)], turned[n % 4][:, columns(c)], identity[:])
-            nc.scalar.copy(readings[u % TILES_PER_PASS][:, half * BANK : (half + 1) * BANK], banks[3][:])
+        def quantize_z(b, q, staged):
+            nc.vector.quantize_mx(out=z_codes[b][q][:].bitcast(FP8X4), scales=z_scales[b][q][:], in_=staged)
 
-        for step in range(-2, len(units)):
-            if step >= 0:
-                stage_turn_back(step)
-            if 0 <= step + 1 < len(units):
-                stage_difference(step + 1)
-            if step + 2 < len(units):
-                stage_products(step + 2)
-            if step >= 0 and step % 2 == 1:
-                u = units[step][0]
-                scatter(u, 0, S)
-                if u < TILES_PER_PASS:
-                    poll(u, 0, M, polled[u][:])
-                    load_base(u + TILES_PER_PASS)
-            if step >= 0 and step % 2 == 0 and step // 2 + 3 < ROW_TILES:
-                quantize_win(step // 2 + 3, turned[step % 4][:].bitcast(BF16))
-
-        def quantize_z(b, q, sources):
-            count = b * (M // QUARTER) + q
-            word_bank = banks[6 + count % 2]
+        def turn_z(q):
+            word_bank = banks[6 + q % 2]
+            rows = [z_rows[(2 * q + c) % 4] for c in range(QUARTER // P)]
             for c in range(QUARTER // P):
-                for t in range(TILES_PER_PASS):
-                    nc.tensor.transpose(banks[2 + c][:, columns(t)], sources[t][:, columns(c)], identity[:])
-                rows = z_rows[(2 * count + c) % 4]
+                for v in range(TILES_PER_PASS):
+                    nc.tensor.transpose(banks[2 + c][:, columns(v)], polled[v][:, columns(2 * q + c)], identity[:])
                 nc.scalar.activation(
-                    rows[:].rearrange("m (w p e) -> m w p e", w=2, e=2),
+                    rows[c][:].rearrange("m (w p e) -> m w p e", w=2, e=2),
                     banks[2 + c][:].rearrange("m (p w e) -> m w p e", w=2, e=2),
                     ACT.Copy,
                     scale=-1.0,
                 )
             for c in range(QUARTER // P):
-                rows = z_rows[(2 * count + c) % 4]
                 for w in range(2):
-                    nc.tensor.transpose(word_bank[:, columns(2 * c + w)], rows[:].bitcast(F32)[:, columns(w)], identity[:])
-            staged = z_bf[count % 2]
+                    nc.tensor.transpose(word_bank[:, columns(2 * c + w)], rows[c][:].bitcast(F32)[:, columns(w)], identity[:])
             nc.scalar.copy(
-                staged[:].bitcast(F32).rearrange("p (c m w) -> p c m w", c=2, w=2),
+                z_bf[q][:].bitcast(F32).rearrange("p (c m w) -> p c m w", c=2, w=2),
                 word_bank[:].rearrange("p (c w m) -> p c m w", c=2, w=2),
             )
-            nc.vector.quantize_mx(out=z_codes[b][q][:].bitcast(FP8X4), scales=z_scales[b][q][:], in_=staged[:])
+            quantize_z(0, q, z_bf[q][:])
 
-        for q in range(M // QUARTER):
-            quantize_z(0, q, [polled[t][:, q * QUARTER : (q + 1) * QUARTER] for t in range(TILES_PER_PASS)])
+        for v in range(TILES_PER_PASS):
+            stage_products(0, v)
+        for c in range(BANK // P):
+            stage_difference(c)
+        for t in range(PACK):
+            stage_turn_back(0, t)
+            stage_products(1, t)
+        for c in range(BANK // P):
+            stage_difference(c)
+        for t in range(PACK):
+            stage_turn_back(1, t)
+            turn_z(t)
+
+        pairs = [banks[6:8], banks[2:4], banks[0:2], banks[4:6]]
 
         def alarm_pass(b, q):
-            pair = (banks[0], banks[1]) if q % 2 == 0 else (banks[4], banks[5])
             for c in range(N_TILES):
                 nc.tensor.matmul_mx(
-                    out=pair[c // 2][:, (c % 2) * QUARTER : (c % 2 + 1) * QUARTER],
+                    out=pairs[q][c // 2][:, (c % 2) * QUARTER : (c % 2 + 1) * QUARTER],
                     lhsT=wal_codes[:, b * N + c * P : b * N + (c + 1) * P].bitcast(FP8X4),
                     lhsT_scale=wal_sc[:, b * N + c * P : b * N + (c + 1) * P],
                     rhs=z_codes[b][q][:].bitcast(FP8X4),
@@ -327,27 +358,37 @@ def tile_list_router_queue_alarms_kernel(
                     start=b == 0 and c % 2 == 0,
                     stop=b == R_PASSES - 1 and c % 2 == 1,
                 )
-            return pair
 
-        last_readers = [readings[(ROW_TILES - 1) % TILES_PER_PASS], slot_weights]
-        for q in range(M // QUARTER):
-            landing = last_readers[q % 2]
-            sources = [landing[:, t * QUARTER : (t + 1) * QUARTER] for t in range(TILES_PER_PASS)]
-            for t in range(TILES_PER_PASS):
-                poll(TILES_PER_PASS + t, q * QUARTER, QUARTER, sources[t])
-            alarm_pass(0, q)
-            quantize_z(1, q, sources)
-            pair = alarm_pass(1, q)
+        def finish(q):
+            alarm_pass(1, q)
             for g in range(2):
                 staged = result[(2 * q + g) % 4]
                 for c in range(2):
                     part = slice(c * QUARTER, (c + 1) * QUARTER)
                     column = bias_col[:, 2 * g + c : 2 * g + c + 1]
-                    if q == M // QUARTER - 1 and g == 1:
-                        nc.vector.tensor_scalar_add(staged[:, part], pair[g][:, part], column)
+                    if q >= 2 and g == 1:
+                        nc.vector.tensor_scalar_add(staged[:, part], pairs[q][g][:, part], column)
                     else:
-                        nc.scalar.activation(staged[:, part], pair[g][:, part], ACT.Identity, bias=column)
+                        nc.scalar.activation(staged[:, part], pairs[q][g][:, part], ACT.Identity, bias=column)
                 nc.sync.dma_start(
                     out=out[2 * g * P : (2 * g + 2) * P, q * QUARTER : (q + 1) * QUARTER].rearrange("(c p) m -> p c m", p=P),
                     in_=staged[:].rearrange("p (c m) -> p c m", c=2),
                 )
+
+        last = M // QUARTER - 1
+        woven = [landing[last][:, halves(0)].bitcast(BF16), landing[last][:, halves(1)].bitcast(BF16), z_bf[0][:], z_bf[1][:]]
+        for q in range(M // QUARTER):
+            alarm_pass(0, q)
+        for q in range(M // QUARTER):
+            for t in range(PACK):
+                poll(t, q * QUARTER, QUARTER, landing[q][:, t * QUARTER : (t + 1) * QUARTER])
+            dst = woven[q].rearrange("p (m t) -> p m t", t=PACK)
+            src = landing[q][:].rearrange("p (t m) -> p m t", t=PACK)
+            if q == last:
+                nc.vector.tensor_scalar_mul(dst, src, -1.0)
+            else:
+                nc.scalar.activation(dst, src, ACT.Copy, scale=-1.0)
+            quantize_z(1, q, woven[q])
+            if q > 0:
+                finish(q - 1)
+        finish(last)

@@ -74,11 +74,12 @@ def tile_list_router_queue_alarms_kernel(
             ]
             for lo, hi in WIN_CHUNKS
         ]
+        late_win_bf = [placed(f"late_win_bf{v}", K_PASSES * PASS, BF16, reused + 2 * K_PASSES * PASS * (PACK + v)) for v in range(TILES_PER_PASS)]
         woven_weights = placed("woven_weights", PACK * S, F32, reused)
         landing = [placed(f"landing{q}", PACK * QUARTER, F32, reused + 4 * PACK * QUARTER * q) for q in range(M // QUARTER)]
         win_bf = tiles("win_bf", 2, K_PASSES * P * PACK, BF16)
         win_codes = [
-            placed(f"win_codes{u}", K_PASSES * P, U32, 4 * T * u + 4 * T2 + K_PASSES * S) if u < K_PASSES else sbuf(f"win_codes{u}", K_PASSES * P, U32)
+            placed(f"win_codes{u}", K_PASSES * P, U32, (4 * T2 + K_PASSES * S, 8 * T - 4 * K_PASSES * P)[u]) if u < K_PASSES else sbuf(f"win_codes{u}", K_PASSES * P, U32)
             for u in range(ROW_TILES)
         ]
         win_scales = tiles("win_scales", ROW_TILES, K_PASSES * P, U8)
@@ -89,40 +90,45 @@ def tile_list_router_queue_alarms_kernel(
         slot_weights = sbuf("slot_weights", S, F32)
         baseline = tiles("baseline", TILES_PER_PASS, M, F32)
         pages = tiles("page", 2, T2, F32)
-        pages.extend(placed(f"late_page{a}", T2, F32, 4 * T * a) for a in range(K_PASSES))
-        readings = tiles("readings", TILES_PER_PASS, S, F32)
+        pages.extend(placed(f"late_page{i}", T2, F32, 4 * T - 4 * K_PASSES * P + 4 * T2 * i) for i in range(2))
+        readings_at = reused + 4 * PACK * S
+        readings = [placed(f"readings{t}", S, F32, readings_at + 4 * S * t) for t in range(PACK)]
         polled = tiles("polled", TILES_PER_PASS, M, F32)
         ingress = tiles("ingress", TILES_PER_PASS, BANK, F32)
         drained = tiles("drained", TILES_PER_PASS, BANK, F32)
         turned = tiles("turned", 4, BANK, F32)
         z_rows = tiles("z_rows", 4, PASS, BF16)
         z_bf = tiles("z_bf", 4, QUARTER * PACK, BF16)
-        z_codes = [tiles(f"z_codes{b}_", M // QUARTER, QUARTER, U32) for b in range(R_PASSES)]
+        z_codes = [
+            [placed(f"z_codes0_{q}", QUARTER, U32, readings_at + 4 * S * q) for q in range(M // QUARTER)],
+            tiles("z_codes1_", M // QUARTER, QUARTER, U32),
+        ]
         z_scales = [tiles(f"z_scales{b}_", M // QUARTER, QUARTER, U8) for b in range(R_PASSES)]
         result = tiles("result", 4, BANK, F32)
         vectors = sbuf("vectors", P, F32)
-        minus_drain = sbuf("minus_drain", ROW_TILES, F32)
+        first_drain = sbuf("first_drain", 1, F32)
+        plus_drain = sbuf("plus_drain", TILES_PER_PASS, F32)
+        minus_drain = sbuf("minus_drain", TILES_PER_PASS, F32)
         bias_col = sbuf("bias_col", N_TILES, F32)
         identity = sbuf("identity", P, F32)
 
         nc.vector.memset(table_scales[:].bitcast(I32), 0)
-        nc.vector.memset(weg_sc[:].bitcast(I32), 0)
         nc.vector.memset(vectors[:], 0.0)
+        nc.vector.memset(weg_sc[:].bitcast(I32), 0)
         nc.vector.memset(wal_sc[:].bitcast(I32), 0)
         for page in pages[:2]:
-            nc.vector.memset(page[:, 0 : T2 - 1], 0.0)
-            nc.vector.memset(page[:, T2 - 1 : T2], 0.0)
+            nc.vector.memset(page[:].bitcast(I32), 0)
         make_identity(nc, identity[:])
 
         def load_scales(plane, scales):
             for quad in range(4):
-                nc.gpsimd.dma_start(
+                nc.sync.dma_start(
                     out=plane[32 * quad : 32 * quad + 4, :].bitcast(I32).rearrange("q (a c) -> q a c", a=2),
                     in_=scales[:, 4 * quad : 4 * quad + 4, :].bitcast(I32).rearrange("a q c -> q a c"),
                 )
 
-        def load_table(a):
-            nc.sync.dma_start(out=table[a][:], in_=tab_words[a].rearrange("p t i -> p (t i)").bitcast(I32))
+        def load_table(a, part):
+            nc.sync.dma_start(out=table[a][:, part], in_=tab_words[a].rearrange("p t i -> p (t i)").bitcast(I32)[:, part])
 
         def load_win(chunk):
             lo, hi = WIN_CHUNKS[chunk]
@@ -146,20 +152,22 @@ def tile_list_router_queue_alarms_kernel(
             nc.sync.dma_start(out=baseline[t][:], in_=base[PASS:H, :].rearrange("(p t) m -> p t m", t=PACK)[:, t, :])
 
         nc.sync.dma_start(idx[:], offs)
-        load_table(0)
-        load_scales(table_scales, tab_scales)
-        load_win(0)
-        load_weg(0)
-        load_table(1)
-        load_scales(weg_sc, weg_scales)
-        nc.gpsimd.dma_start(out=vectors[0:ROW_TILES, :], in_=drain.rearrange("(u p) -> u p", p=P))
-        nc.gpsimd.dma_start(out=vectors[ROW_TILES : ROW_TILES + N_TILES, :], in_=bias.rearrange("(c p) -> c p", p=P))
-        load_win(1)
         nc.sync.dma_start(idx2[:], offs2)
+        nc.sync.dma_start(idx3[:], offs3)
+        load_weg(0)
+        nc.sync.dma_start(out=first_drain[:], in_=drain[0:P].rearrange("(p o) -> p o", o=1))
+        for half in range(2):
+            load_table(0, slice(half * T // 2, (half + 1) * T // 2))
+        load_win(0)
+        load_scales(table_scales, tab_scales)
+        load_table(1, slice(0, T))
+        nc.sync.dma_start(out=vectors[1:ROW_TILES, :], in_=drain[P:H].rearrange("(u p) -> u p", p=P))
+        nc.sync.dma_start(out=vectors[ROW_TILES : ROW_TILES + N_TILES, :], in_=bias.rearrange("(c p) -> c p", p=P))
+        load_scales(weg_sc, weg_scales)
+        load_win(1)
         nc.sync.dma_start(out=slot_weights[:], in_=wgs)
         load_win(2)
         load_weg(1)
-        nc.sync.dma_start(idx3[:], offs3)
         load_base(0)
         load_win(3)
         for u in range(1, TILES_PER_PASS):
@@ -171,7 +179,8 @@ def tile_list_router_queue_alarms_kernel(
         load_scales(wal_sc, wal_scales)
 
         nc.tensor.transpose(banks[7][:, 0:P], vectors[:], identity[:])
-        nc.scalar.activation(minus_drain[:], banks[7][:, 0:ROW_TILES], ACT.Copy, scale=-1.0)
+        nc.scalar.copy(plus_drain[:], banks[7][:, 0:TILES_PER_PASS])
+        nc.scalar.activation(minus_drain[:], banks[7][:, TILES_PER_PASS:ROW_TILES], ACT.Copy, scale=-1.0)
         nc.scalar.copy(bias_col[:], banks[7][:, ROW_TILES : ROW_TILES + N_TILES])
 
         def entries(offsets, start, count):
@@ -254,49 +263,57 @@ def tile_list_router_queue_alarms_kernel(
         def halves(half):
             return slice(half * BANK, (half + 1) * BANK)
 
-        def reading_on_vector(u, half, pair, staged, difference):
+        def products_for_vector(u, half, pair, staged):
             project(u, half, pair[0], pair[1])
             nc.scalar.copy(staged, pair[0][:])
-            nc.vector.scalar_tensor_tensor(difference, pair[1][:], minus_drain[:, u : u + 1], staged, ALU.mult, ALU.add)
+
+        def reading_on_vector(u, half, pair, staged, difference):
+            rate = first_drain[:] if u == 0 else plus_drain[:, u : u + 1]
+            nc.vector.scalar_tensor_tensor(difference, pair[1][:], rate, staged, ALU.mult, ALU.subtract)
             nc.scalar.activation(readings[u][:, halves(half)], difference, ACT.Abs)
 
-        reading_on_vector(0, 0, banks[0:2], ingress[0][:], win_bf[1][:].bitcast(F32))
-        reading_on_vector(0, 1, banks[4:6], ingress[1][:], win_bf[0][:].bitcast(F32))
-        for half in range(HALVES):
-            scatter(0, half * BANK, BANK, slot_weights[:, halves(half)])
-        quantize_win(2, win_bf[1][:])
-        quantize_win(3, win_bf[0][:])
-        for quad in range(4):
-            nc.sync.dma_start(
-                out=woven_weights[32 * quad : 32 * (quad + 1), :], in_=wgs.rearrange("(p t) j -> p (t j)", t=PACK)
-            )
-        for u in range(1, TILES_PER_PASS):
-            reading_on_vector(u, 0, banks[2:4], polled[u - 1][:, halves(0)], turned[2][:])
-            if u == 1:
-                quantize_win(4, turned[2][:].bitcast(BF16))
-            reading_on_vector(u, 1, banks[6:8], polled[u - 1][:, halves(1)], turned[3][:])
-            poll(u - 1, 0, M, polled[u - 1][:])
-            load_woven_base(u - 1)
-            scatter(u, 0, S, slot_weights[:])
-            if u == 1:
-                quantize_win(5, turned[3][:].bitcast(BF16))
-                quantize_win(6, win_bf[1][:])
-                quantize_win(7, win_bf[0][:])
-        poll(TILES_PER_PASS - 1, 0, M, polled[TILES_PER_PASS - 1][:])
-        load_woven_base(TILES_PER_PASS - 1)
+        last_tile = TILES_PER_PASS - 1
+        staged_products = [
+            [(ingress[v][:], drained[v][:]) for v in range(last_tile)]
+            + [(readings[last_tile][:, halves(0)], readings[last_tile][:, halves(1)])],
+            [(ingress[v][:], drained[v][:]) for v in range(TILES_PER_PASS)],
+        ]
 
         def stage_products(half, v):
             pair = banks[0:2] if v % 2 == 0 else banks[4:6]
             u = TILES_PER_PASS + v
             project(u, half, pair[0], pair[1])
-            nc.scalar.copy(ingress[v][:], pair[0][:])
-            nc.scalar.activation(drained[v][:], pair[1][:], ACT.Copy, scale=minus_drain[:, u : u + 1])
+            nc.scalar.copy(staged_products[half][v][0], pair[0][:])
+            nc.scalar.activation(staged_products[half][v][1], pair[1][:], ACT.Copy, scale=minus_drain[:, v : v + 1])
 
-        def stage_difference(c):
+        win_bf_words = [win_bf[1][:].bitcast(F32), win_bf[0][:].bitcast(F32)]
+        for half, pair in enumerate((banks[0:2], banks[4:6])):
+            products_for_vector(0, half, pair, ingress[half][:])
+            reading_on_vector(0, half, pair, ingress[half][:], (turned[0][:], win_bf_words[1])[half])
+        for half in range(HALVES):
+            scatter(0, half * BANK, BANK, slot_weights[:, halves(half)])
+        quantize_win(2, turned[0][:].bitcast(BF16))
+        quantize_win(3, win_bf[0][:])
+
+        pairs_of = {1: (banks[2:4], banks[6:8]), 2: (banks[2:4], banks[6:8]), 3: (banks[0:2], banks[4:6])}
+        differences = {1: [turned[2][:], turned[3][:]], 2: win_bf_words, 3: win_bf_words}
+
+        def begin_tile(u):
+            for half in range(HALVES):
+                products_for_vector(u, half, pairs_of[u][half], polled[u - 1][:, halves(half)])
+
+        def end_tile(u):
+            for half in range(HALVES):
+                reading_on_vector(u, half, pairs_of[u][half], polled[u - 1][:, halves(half)], differences[u][half])
+            poll(u - 1, 0, M, polled[u - 1][:])
+            load_woven_base(u - 1)
+            scatter(u, 0, S, slot_weights[:])
+
+        def stage_difference(half, c):
             bank = banks[2 + c % 2]
             for v in range(TILES_PER_PASS):
-                nc.tensor.matmul(bank[:, columns(v)], ingress[v][:, columns(c)], identity[:], start=True, stop=False, is_transpose=True)
-                nc.tensor.matmul(bank[:, columns(v)], drained[v][:, columns(c)], identity[:], start=False, stop=True, is_transpose=True)
+                nc.tensor.matmul(bank[:, columns(v)], staged_products[half][v][0][:, columns(c)], identity[:], start=True, stop=False, is_transpose=True)
+                nc.tensor.matmul(bank[:, columns(v)], staged_products[half][v][1][:, columns(c)], identity[:], start=False, stop=True, is_transpose=True)
             nc.scalar.activation(
                 turned[c][:].rearrange("j (t p) -> j t p", t=PACK), bank[:].rearrange("j (p t) -> j t p", t=PACK), ACT.Abs
             )
@@ -332,15 +349,29 @@ def tile_list_router_queue_alarms_kernel(
             )
             quantize_z(0, q, z_bf[q][:])
 
+        begin_tile(1)
+        for v in range(TILES_PER_PASS):
+            quantize_win(TILES_PER_PASS + v, late_win_bf[v][:])
+        end_tile(1)
+        for quad in range(4):
+            nc.sync.dma_start(
+                out=woven_weights[32 * quad : 32 * (quad + 1), :], in_=wgs.rearrange("(p t) j -> p (t j)", t=PACK)
+            )
+        begin_tile(2)
         for v in range(TILES_PER_PASS):
             stage_products(0, v)
+        end_tile(2)
+        begin_tile(3)
         for c in range(BANK // P):
-            stage_difference(c)
+            stage_difference(0, c)
+        end_tile(3)
+        poll(last_tile, 0, M, polled[last_tile][:])
+        load_woven_base(last_tile)
         for t in range(PACK):
             stage_turn_back(0, t)
             stage_products(1, t)
         for c in range(BANK // P):
-            stage_difference(c)
+            stage_difference(1, c)
         for t in range(PACK):
             stage_turn_back(1, t)
             turn_z(t)

@@ -58,12 +58,12 @@ def tile_list_router_queue_alarms_kernel(
         idx2 = held.tile([P, S // PER_COLUMN], U16, name="idx2")
         idx3 = held.tile([P, M // PER_COLUMN], U16, name="idx3")
         table = [placed(f"table{a}", T, I32, 4 * T * a) for a in range(K_PASSES)]
-        table_scales = placed("table_scales", K_PASSES * T, U8, 8 * T)
+        table_scales = placed("table_scales", T, U8, 8 * T)
         picked = [
             tiles("picked0_", HALVES, BANK, U32),
             [placed(f"picked1_{half}", BANK, U32, 8 * T + 4 * BANK * half) for half in range(HALVES)],
         ]
-        picked_scales = [placed(f"picked_scales{a}", S, U8, 4 * T2 + S * a) for a in range(K_PASSES)]
+        picked_scales = [placed("picked_scales0", S, U8, 4 * T2), sbuf("picked_scales1", S, U8)]
         reused = 8 * T + K_PASSES * T
         win_raw = [
             [
@@ -79,7 +79,7 @@ def tile_list_router_queue_alarms_kernel(
         landing = [placed(f"landing{q}", PACK * QUARTER, F32, reused + 4 * PACK * QUARTER * q) for q in range(M // QUARTER)]
         win_bf = tiles("win_bf", 2, K_PASSES * P * PACK, BF16)
         win_codes = [
-            placed(f"win_codes{u}", K_PASSES * P, U32, (4 * T2 + K_PASSES * S, 8 * T - 4 * K_PASSES * P)[u]) if u < K_PASSES else sbuf(f"win_codes{u}", K_PASSES * P, U32)
+            placed(f"win_codes{u}", K_PASSES * P, U32, (4 * T2 + K_PASSES * S, 3 * T)[u]) if u < K_PASSES else sbuf(f"win_codes{u}", K_PASSES * P, U32)
             for u in range(ROW_TILES)
         ]
         win_scales = tiles("win_scales", ROW_TILES, K_PASSES * P, U8)
@@ -89,11 +89,12 @@ def tile_list_router_queue_alarms_kernel(
         wal_sc = sbuf("wal_sc", R_PASSES * N, U8)
         slot_weights = sbuf("slot_weights", S, F32)
         baseline = tiles("baseline", TILES_PER_PASS, M, F32)
-        pages = tiles("page", 2, T2, F32)
-        pages.extend(placed(f"late_page{i}", T2, F32, 4 * T - 4 * K_PASSES * P + 4 * T2 * i) for i in range(2))
+        woven_baseline = [placed(f"woven_baseline{t}", M, F32, 4 * T + 4 * M * t) for t in range(PACK)]
+        pages = tiles("page", PACK, T2, F32)
         readings_at = reused + 4 * PACK * S
         readings = [placed(f"readings{t}", S, F32, readings_at + 4 * S * t) for t in range(PACK)]
         polled = tiles("polled", TILES_PER_PASS, M, F32)
+        first_ingress = placed("first_ingress", BANK, F32, 3 * T)
         ingress = tiles("ingress", TILES_PER_PASS, BANK, F32)
         drained = tiles("drained", TILES_PER_PASS, BANK, F32)
         turned = tiles("turned", 4, BANK, F32)
@@ -104,7 +105,7 @@ def tile_list_router_queue_alarms_kernel(
             tiles("z_codes1_", M // QUARTER, QUARTER, U32),
         ]
         z_scales = [tiles(f"z_scales{b}_", M // QUARTER, QUARTER, U8) for b in range(R_PASSES)]
-        result = tiles("result", 4, BANK, F32)
+        result = [placed(f"result{i}", BANK, F32, 4 * BANK * i) for i in range(4)]
         vectors = sbuf("vectors", P, F32)
         first_drain = sbuf("first_drain", 1, F32)
         plus_drain = sbuf("plus_drain", TILES_PER_PASS, F32)
@@ -114,9 +115,10 @@ def tile_list_router_queue_alarms_kernel(
 
         nc.vector.memset(table_scales[:].bitcast(I32), 0)
         nc.vector.memset(vectors[:], 0.0)
+        nc.vector.memset(picked_scales[1][:].bitcast(I32), 0)
         nc.vector.memset(weg_sc[:].bitcast(I32), 0)
         nc.vector.memset(wal_sc[:].bitcast(I32), 0)
-        for page in pages[:2]:
+        for page in pages:
             nc.vector.memset(page[:].bitcast(I32), 0)
         make_identity(nc, identity[:])
 
@@ -149,7 +151,7 @@ def tile_list_router_queue_alarms_kernel(
             nc.sync.dma_start(out=baseline[u][:], in_=base[u * P : (u + 1) * P, :])
 
         def load_woven_base(t):
-            nc.sync.dma_start(out=baseline[t][:], in_=base[PASS:H, :].rearrange("(p t) m -> p t m", t=PACK)[:, t, :])
+            nc.sync.dma_start(out=woven_baseline[t][:], in_=base[PASS:H, :].rearrange("(p t) m -> p t m", t=PACK)[:, t, :])
 
         nc.sync.dma_start(idx[:], offs)
         nc.sync.dma_start(idx2[:], offs2)
@@ -159,7 +161,11 @@ def tile_list_router_queue_alarms_kernel(
         for half in range(2):
             load_table(0, slice(half * T // 2, (half + 1) * T // 2))
         load_win(0)
-        load_scales(table_scales, tab_scales)
+        for quad in range(4):
+            nc.sync.dma_start(
+                out=table_scales[32 * quad : 32 * quad + 8, :].bitcast(I32),
+                in_=tab_scales[:, 4 * quad : 4 * quad + 4, :].bitcast(I32),
+            )
         load_table(1, slice(0, T))
         nc.sync.dma_start(out=vectors[1:ROW_TILES, :], in_=drain[P:H].rearrange("(u p) -> u p", p=P))
         nc.sync.dma_start(out=vectors[ROW_TILES : ROW_TILES + N_TILES, :], in_=bias.rearrange("(c p) -> c p", p=P))
@@ -177,11 +183,6 @@ def tile_list_router_queue_alarms_kernel(
             in_=wal_words.rearrange("b p c i -> p b (c i)").bitcast(I32),
         )
         load_scales(wal_sc, wal_scales)
-
-        nc.tensor.transpose(banks[7][:, 0:P], vectors[:], identity[:])
-        nc.scalar.copy(plus_drain[:], banks[7][:, 0:TILES_PER_PASS])
-        nc.scalar.activation(minus_drain[:], banks[7][:, TILES_PER_PASS:ROW_TILES], ACT.Copy, scale=-1.0)
-        nc.scalar.copy(bias_col[:], banks[7][:, ROW_TILES : ROW_TILES + N_TILES])
 
         def entries(offsets, start, count):
             return offsets[:, start // PER_COLUMN : (start + count) // PER_COLUMN]
@@ -202,9 +203,6 @@ def tile_list_router_queue_alarms_kernel(
         def gather_words(a, half):
             nc.vector.tensor_copy(picked[a][half][:], table[a][:].bitcast(U32).indirect(entries(idx, half * BANK, BANK)))
 
-        def gather_scales(a):
-            nc.vector.tensor_copy(picked_scales[a][:], table_scales[:, a * T : (a + 1) * T].indirect(idx[:]))
-
         def project(u, half, ingress_bank, egress_bank):
             chunk = chunk_of(WEG_CHUNKS, u)
             lo, hi = WEG_CHUNKS[chunk]
@@ -214,7 +212,7 @@ def tile_list_router_queue_alarms_kernel(
                     lhsT=win_codes[u][:, a * P : (a + 1) * P].bitcast(FP8X4),
                     lhsT_scale=win_scales[u][:, a * P : (a + 1) * P],
                     rhs=picked[a][half][:].bitcast(FP8X4),
-                    rhs_scale=picked_scales[a][:, half * BANK : (half + 1) * BANK],
+                    rhs_scale=picked_scales[0][4 * a : P, half * BANK : (half + 1) * BANK],
                     start=a == 0,
                     stop=a == K_PASSES - 1,
                 )
@@ -240,25 +238,21 @@ def tile_list_router_queue_alarms_kernel(
                 ALU.mult,
             )
 
-        def poll(u, start, count, dst):
+        def poll(u, start, count, dst, rows):
             nc.vector.tensor_tensor(
                 dst,
                 pages[u % TILES_PER_PASS][:].indirect(entries(idx3, start, count)),
-                baseline[u % TILES_PER_PASS][:, start : start + count],
+                rows[:, start : start + count],
                 ALU.subtract,
             )
 
         for half in range(HALVES):
             gather_words(0, half)
-        for a in range(K_PASSES):
-            gather_scales(a)
+        nc.vector.tensor_copy(picked_scales[0][:], table_scales[:].indirect(idx[:]))
+        nc.scalar.dma_start(out=picked_scales[1][0:112, :].bitcast(I32), in_=picked_scales[0][4:116, :].bitcast(I32))
         quantize_win(0, win_bf[0][:])
         for half in range(HALVES):
             gather_words(1, half)
-        for page in pages[2:]:
-            for c in range(T2 // BANK):
-                nc.gpsimd.memset(page[:, c * BANK : (c + 1) * BANK], 0.0)
-        quantize_win(1, win_bf[1][:])
 
         def halves(half):
             return slice(half * BANK, (half + 1) * BANK)
@@ -287,9 +281,15 @@ def tile_list_router_queue_alarms_kernel(
             nc.scalar.activation(staged_products[half][v][1], pair[1][:], ACT.Copy, scale=minus_drain[:, v : v + 1])
 
         win_bf_words = [win_bf[1][:].bitcast(F32), win_bf[0][:].bitcast(F32)]
-        for half, pair in enumerate((banks[0:2], banks[4:6])):
-            products_for_vector(0, half, pair, ingress[half][:])
-            reading_on_vector(0, half, pair, ingress[half][:], (turned[0][:], win_bf_words[1])[half])
+        products_for_vector(0, 0, banks[0:2], first_ingress[:])
+        reading_on_vector(0, 0, banks[0:2], first_ingress[:], turned[0][:])
+        quantize_win(1, win_bf[1][:])
+        products_for_vector(0, 1, banks[4:6], ingress[1][:])
+        reading_on_vector(0, 1, banks[4:6], ingress[1][:], win_bf_words[1])
+        nc.tensor.transpose(banks[1][:, 0:P], vectors[:], identity[:])
+        nc.scalar.copy(plus_drain[:], banks[1][:, 0:TILES_PER_PASS])
+        nc.scalar.activation(minus_drain[:], banks[1][:, TILES_PER_PASS:ROW_TILES], ACT.Copy, scale=-1.0)
+        nc.scalar.copy(bias_col[:], banks[1][:, ROW_TILES : ROW_TILES + N_TILES])
         for half in range(HALVES):
             scatter(0, half * BANK, BANK, slot_weights[:, halves(half)])
         quantize_win(2, turned[0][:].bitcast(BF16))
@@ -305,8 +305,7 @@ def tile_list_router_queue_alarms_kernel(
         def end_tile(u):
             for half in range(HALVES):
                 reading_on_vector(u, half, pairs_of[u][half], polled[u - 1][:, halves(half)], differences[u][half])
-            poll(u - 1, 0, M, polled[u - 1][:])
-            load_woven_base(u - 1)
+            poll(u - 1, 0, M, polled[u - 1][:], baseline[u - 1])
             scatter(u, 0, S, slot_weights[:])
 
         def stage_difference(half, c):
@@ -357,6 +356,8 @@ def tile_list_router_queue_alarms_kernel(
             nc.sync.dma_start(
                 out=woven_weights[32 * quad : 32 * (quad + 1), :], in_=wgs.rearrange("(p t) j -> p (t j)", t=PACK)
             )
+        for t in range(PACK):
+            load_woven_base(t)
         begin_tile(2)
         for v in range(TILES_PER_PASS):
             stage_products(0, v)
@@ -365,8 +366,7 @@ def tile_list_router_queue_alarms_kernel(
         for c in range(BANK // P):
             stage_difference(0, c)
         end_tile(3)
-        poll(last_tile, 0, M, polled[last_tile][:])
-        load_woven_base(last_tile)
+        poll(last_tile, 0, M, polled[last_tile][:], baseline[last_tile])
         for t in range(PACK):
             stage_turn_back(0, t)
             stage_products(1, t)
@@ -412,7 +412,7 @@ def tile_list_router_queue_alarms_kernel(
             alarm_pass(0, q)
         for q in range(M // QUARTER):
             for t in range(PACK):
-                poll(t, q * QUARTER, QUARTER, landing[q][:, t * QUARTER : (t + 1) * QUARTER])
+                poll(t, q * QUARTER, QUARTER, landing[q][:, t * QUARTER : (t + 1) * QUARTER], woven_baseline[t])
             dst = woven[q].rearrange("p (m t) -> p m t", t=PACK)
             src = landing[q][:].rearrange("p (t m) -> p m t", t=PACK)
             if q == last:

@@ -21,6 +21,7 @@ P = 128
 PACK = 4
 PASS = P * PACK
 BANK = 512
+QUADS, QUAD = 4, 32
 K_PASSES = K // PASS
 R_PASSES = H // PASS
 ROW_TILES = H // P
@@ -29,8 +30,18 @@ N_TILES = N // P
 HALVES = S // BANK
 PER_COLUMN = 16
 QUARTER = 256
-WIN_CHUNKS = ((0, 1), (1, 2), (2, 4), (4, 8))
+QUARTERS = M // QUARTER
+WIN_CHUNKS = ((0, 1), (1, 2), (2, 4), (4, 6), (6, 8))
 WEG_CHUNKS = ((0, 2), (2, 8))
+POLL_CHUNKS = ((0, 256), (256, 256), (512, 256), (768, 128), (896, 128))
+EMPTIED_BY_VECTOR = ((2, 1), (4, 0))
+MOVED_ROWS = 112
+
+KIB = 1024
+TABLE_AT = (0, 16 * KIB)
+TABLE_SCALES_AT = 32 * KIB
+WIN_RAW_AT = 40 * KIB
+READINGS_AT = 56 * KIB
 
 
 def tile_list_router_queue_alarms_kernel(
@@ -57,29 +68,38 @@ def tile_list_router_queue_alarms_kernel(
         idx = held.tile([P, S // PER_COLUMN], U16, name="idx")
         idx2 = held.tile([P, S // PER_COLUMN], U16, name="idx2")
         idx3 = held.tile([P, M // PER_COLUMN], U16, name="idx3")
-        table = [placed(f"table{a}", T, I32, 4 * T * a) for a in range(K_PASSES)]
-        table_scales = placed("table_scales", T, U8, 8 * T)
+
+        table = [placed(f"table{a}", T, I32, TABLE_AT[a]) for a in range(K_PASSES)]
+        table_scales = placed("table_scales", T, U8, TABLE_SCALES_AT)
         picked = [
             tiles("picked0_", HALVES, BANK, U32),
-            [placed(f"picked1_{half}", BANK, U32, 8 * T + 4 * BANK * half) for half in range(HALVES)],
+            [placed(f"picked1_{half}", BANK, U32, TABLE_SCALES_AT + 4 * BANK * half) for half in range(HALVES)],
         ]
-        picked_scales = [placed("picked_scales0", S, U8, 4 * T2), sbuf("picked_scales1", S, U8)]
-        reused = 8 * T + K_PASSES * T
+        picked_scales = [placed("picked_scales0", S, U8, TABLE_AT[0] + 8 * KIB), sbuf("picked_scales1", S, U8)]
+
         win_raw = [
             [
-                placed(f"win_raw{lo}_{a}", PASS * (hi - lo), F32, reused + 4 * PASS * (K_PASSES * lo + a * (hi - lo)))
+                placed(f"win_raw{lo}_{a}", PASS * (hi - lo), F32, WIN_RAW_AT + 4 * PASS * (K_PASSES * lo + a * (hi - lo)))
                 if hi <= TILES_PER_PASS
                 else sbuf(f"win_raw{lo}_{a}", PASS * (hi - lo), F32)
                 for a in range(K_PASSES)
             ]
             for lo, hi in WIN_CHUNKS
         ]
-        late_win_bf = [placed(f"late_win_bf{v}", K_PASSES * PASS, BF16, reused + 2 * K_PASSES * PASS * (PACK + v)) for v in range(TILES_PER_PASS)]
-        woven_weights = placed("woven_weights", PACK * S, F32, reused)
-        landing = [placed(f"landing{q}", PACK * QUARTER, F32, reused + 4 * PACK * QUARTER * q) for q in range(M // QUARTER)]
-        win_bf = tiles("win_bf", 2, K_PASSES * P * PACK, BF16)
+        late_win_bf = [
+            placed(f"late_win_bf{v}", K_PASSES * PASS, BF16, WIN_RAW_AT + 8 * KIB + 2 * KIB * v)
+            for v in range(TILES_PER_PASS)
+        ]
+        woven_weights = placed("woven_weights", PACK * S, F32, WIN_RAW_AT)
+        landing = [
+            placed(f"landing{first}", PACK * count, F32, WIN_RAW_AT + 4 * PACK * first) for first, count in POLL_CHUNKS
+        ]
+        win_bf = tiles("win_bf", 2, K_PASSES * PASS, BF16)
+        early_codes_at = (TABLE_AT[0] + 10 * KIB, TABLE_AT[0] + 12 * KIB)
         win_codes = [
-            placed(f"win_codes{u}", K_PASSES * P, U32, (4 * T2 + K_PASSES * S, 3 * T)[u]) if u < K_PASSES else sbuf(f"win_codes{u}", K_PASSES * P, U32)
+            placed(f"win_codes{u}", K_PASSES * P, U32, early_codes_at[u])
+            if u < len(early_codes_at)
+            else sbuf(f"win_codes{u}", K_PASSES * P, U32)
             for u in range(ROW_TILES)
         ]
         win_scales = tiles("win_scales", ROW_TILES, K_PASSES * P, U8)
@@ -89,23 +109,25 @@ def tile_list_router_queue_alarms_kernel(
         wal_sc = sbuf("wal_sc", R_PASSES * N, U8)
         slot_weights = sbuf("slot_weights", S, F32)
         baseline = tiles("baseline", TILES_PER_PASS, M, F32)
-        woven_baseline = [placed(f"woven_baseline{t}", M, F32, 4 * T + 4 * M * t) for t in range(PACK)]
+        woven_baseline = [placed(f"woven_baseline{t}", M, F32, TABLE_AT[1] + 4 * M * t) for t in range(PACK)]
         pages = tiles("page", PACK, T2, F32)
-        readings_at = reused + 4 * PACK * S
-        readings = [placed(f"readings{t}", S, F32, readings_at + 4 * S * t) for t in range(PACK)]
+        readings = [placed(f"readings{t}", S, F32, READINGS_AT + 4 * S * t) for t in range(PACK)]
         polled = tiles("polled", TILES_PER_PASS, M, F32)
-        first_ingress = placed("first_ingress", BANK, F32, 3 * T)
+        first_ingress = placed("first_ingress", BANK, F32, early_codes_at[1])
         ingress = tiles("ingress", TILES_PER_PASS, BANK, F32)
         drained = tiles("drained", TILES_PER_PASS, BANK, F32)
-        turned = tiles("turned", 4, BANK, F32)
+        turned = tiles("turned", BANK // P, BANK, F32)
         z_rows = tiles("z_rows", 4, PASS, BF16)
-        z_bf = tiles("z_bf", 4, QUARTER * PACK, BF16)
+        z_bf = tiles("z_bf", QUARTERS, QUARTER * PACK, BF16)
         z_codes = [
-            [placed(f"z_codes0_{q}", QUARTER, U32, readings_at + 4 * S * q) for q in range(M // QUARTER)],
-            tiles("z_codes1_", M // QUARTER, QUARTER, U32),
+            [placed(f"z_codes0_{q}", QUARTER, U32, READINGS_AT + 4 * S * q) for q in range(QUARTERS)],
+            [sbuf(f"z_codes1_{first}", count, U32) for first, count in POLL_CHUNKS],
         ]
-        z_scales = [tiles(f"z_scales{b}_", M // QUARTER, QUARTER, U8) for b in range(R_PASSES)]
-        result = [placed(f"result{i}", BANK, F32, 4 * BANK * i) for i in range(4)]
+        z_scales = [
+            tiles("z_scales0_", QUARTERS, QUARTER, U8),
+            [sbuf(f"z_scales1_{first}", count, U8) for first, count in POLL_CHUNKS],
+        ]
+        results = [placed(f"result{i}", BANK, F32, TABLE_AT[0] + 4 * BANK * i) for i in range(4)]
         vectors = sbuf("vectors", P, F32)
         first_drain = sbuf("first_drain", 1, F32)
         plus_drain = sbuf("plus_drain", TILES_PER_PASS, F32)
@@ -122,10 +144,10 @@ def tile_list_router_queue_alarms_kernel(
             nc.vector.memset(page[:].bitcast(I32), 0)
         make_identity(nc, identity[:])
 
-        def load_scales(plane, scales):
-            for quad in range(4):
+        def load_scales(scale_tile, scales):
+            for quad in range(QUADS):
                 nc.sync.dma_start(
-                    out=plane[32 * quad : 32 * quad + 4, :].bitcast(I32).rearrange("q (a c) -> q a c", a=2),
+                    out=scale_tile[QUAD * quad : QUAD * quad + 4, :].bitcast(I32).rearrange("q (a c) -> q a c", a=2),
                     in_=scales[:, 4 * quad : 4 * quad + 4, :].bitcast(I32).rearrange("a q c -> q a c"),
                 )
 
@@ -150,20 +172,17 @@ def tile_list_router_queue_alarms_kernel(
         def load_base(u):
             nc.sync.dma_start(out=baseline[u][:], in_=base[u * P : (u + 1) * P, :])
 
-        def load_woven_base(t):
-            nc.sync.dma_start(out=woven_baseline[t][:], in_=base[PASS:H, :].rearrange("(p t) m -> p t m", t=PACK)[:, t, :])
-
         nc.sync.dma_start(idx[:], offs)
         nc.sync.dma_start(idx2[:], offs2)
         nc.sync.dma_start(idx3[:], offs3)
         load_weg(0)
         nc.sync.dma_start(out=first_drain[:], in_=drain[0:P].rearrange("(p o) -> p o", o=1))
-        for half in range(2):
-            load_table(0, slice(half * T // 2, (half + 1) * T // 2))
+        for part in (slice(0, T // 2), slice(T // 2, T)):
+            load_table(0, part)
         load_win(0)
-        for quad in range(4):
+        for quad in range(QUADS):
             nc.sync.dma_start(
-                out=table_scales[32 * quad : 32 * quad + 8, :].bitcast(I32),
+                out=table_scales[QUAD * quad : QUAD * quad + 4 * K_PASSES, :].bitcast(I32),
                 in_=tab_scales[:, 4 * quad : 4 * quad + 4, :].bitcast(I32),
             )
         load_table(1, slice(0, T))
@@ -174,8 +193,9 @@ def tile_list_router_queue_alarms_kernel(
         nc.sync.dma_start(out=slot_weights[:], in_=wgs)
         load_win(2)
         load_weg(1)
-        load_base(0)
         load_win(3)
+        load_base(0)
+        load_win(4)
         for u in range(1, TILES_PER_PASS):
             load_base(u)
         nc.sync.dma_start(
@@ -184,11 +204,17 @@ def tile_list_router_queue_alarms_kernel(
         )
         load_scales(wal_sc, wal_scales)
 
-        def entries(offsets, start, count):
-            return offsets[:, start // PER_COLUMN : (start + count) // PER_COLUMN]
+        def entries(offsets, first, count):
+            return offsets[:, first // PER_COLUMN : (first + count) // PER_COLUMN]
 
         def chunk_of(chunks, u):
             return [c for c, (lo, hi) in enumerate(chunks) if lo <= u < hi][0]
+
+        def columns(c):
+            return slice(c * P, (c + 1) * P)
+
+        def halves(half):
+            return slice(half * BANK, (half + 1) * BANK)
 
         def quantize_win(u, staged):
             chunk = chunk_of(WIN_CHUNKS, u)
@@ -203,89 +229,68 @@ def tile_list_router_queue_alarms_kernel(
         def gather_words(a, half):
             nc.vector.tensor_copy(picked[a][half][:], table[a][:].bitcast(U32).indirect(entries(idx, half * BANK, BANK)))
 
-        def project(u, half, ingress_bank, egress_bank):
+        def project(u, half, pair):
             chunk = chunk_of(WEG_CHUNKS, u)
             lo, hi = WEG_CHUNKS[chunk]
             for a in range(K_PASSES):
                 nc.tensor.matmul_mx(
-                    out=ingress_bank[:],
-                    lhsT=win_codes[u][:, a * P : (a + 1) * P].bitcast(FP8X4),
-                    lhsT_scale=win_scales[u][:, a * P : (a + 1) * P],
+                    out=pair[0][:],
+                    lhsT=win_codes[u][:, columns(a)].bitcast(FP8X4),
+                    lhsT_scale=win_scales[u][:, columns(a)],
                     rhs=picked[a][half][:].bitcast(FP8X4),
-                    rhs_scale=picked_scales[0][4 * a : P, half * BANK : (half + 1) * BANK],
+                    rhs_scale=picked_scales[0][4 * a : P, halves(half)],
                     start=a == 0,
                     stop=a == K_PASSES - 1,
                 )
                 first = 2 * P * (a * (hi - lo) + u - lo)
                 nc.tensor.matmul_mx(
-                    out=egress_bank[:],
+                    out=pair[1][:],
                     lhsT=weg_codes[chunk][:, first : first + 2 * P].bitcast(FP4X4),
                     lhsT_scale=weg_sc[:, a * H + u * P : a * H + (u + 1) * P],
                     rhs=picked[a][half][:].bitcast(FP8X4),
-                    rhs_scale=picked_scales[a][:, half * BANK : (half + 1) * BANK],
+                    rhs_scale=picked_scales[a][:, halves(half)],
                     start=a == 0,
                     stop=a == K_PASSES - 1,
                 )
 
-        def columns(c):
-            return slice(c * P, (c + 1) * P)
-
-        def scatter(u, start, count, weights):
+        def scatter(t, first, count, weights):
             nc.vector.tensor_tensor(
-                pages[u % TILES_PER_PASS][:].indirect(entries(idx2, start, count)),
-                readings[u % TILES_PER_PASS][:, start : start + count],
-                weights,
-                ALU.mult,
+                pages[t][:].indirect(entries(idx2, first, count)), readings[t][:, first : first + count], weights, ALU.mult
             )
 
-        def poll(u, start, count, dst, rows):
+        def poll(t, first, count, dst, base_rows):
             nc.vector.tensor_tensor(
-                dst,
-                pages[u % TILES_PER_PASS][:].indirect(entries(idx3, start, count)),
-                rows[:, start : start + count],
-                ALU.subtract,
+                dst, pages[t][:].indirect(entries(idx3, first, count)), base_rows[:, first : first + count], ALU.subtract
             )
+
+        def quantize_z(b, i, staged):
+            nc.vector.quantize_mx(out=z_codes[b][i][:].bitcast(FP8X4), scales=z_scales[b][i][:], in_=staged)
 
         for half in range(HALVES):
             gather_words(0, half)
         nc.vector.tensor_copy(picked_scales[0][:], table_scales[:].indirect(idx[:]))
-        nc.scalar.dma_start(out=picked_scales[1][0:112, :].bitcast(I32), in_=picked_scales[0][4:116, :].bitcast(I32))
+        nc.scalar.dma_start(
+            out=picked_scales[1][0:MOVED_ROWS, :].bitcast(I32), in_=picked_scales[0][4 : 4 + MOVED_ROWS, :].bitcast(I32)
+        )
         quantize_win(0, win_bf[0][:])
         for half in range(HALVES):
             gather_words(1, half)
 
-        def halves(half):
-            return slice(half * BANK, (half + 1) * BANK)
-
-        def products_for_vector(u, half, pair, staged):
-            project(u, half, pair[0], pair[1])
+        def plain_products(u, half, pair, staged):
+            project(u, half, pair)
             nc.scalar.copy(staged, pair[0][:])
 
-        def reading_on_vector(u, half, pair, staged, difference):
+        def plain_reading(u, half, pair, staged, difference):
             rate = first_drain[:] if u == 0 else plus_drain[:, u : u + 1]
             nc.vector.scalar_tensor_tensor(difference, pair[1][:], rate, staged, ALU.mult, ALU.subtract)
             nc.scalar.activation(readings[u][:, halves(half)], difference, ACT.Abs)
 
-        last_tile = TILES_PER_PASS - 1
-        staged_products = [
-            [(ingress[v][:], drained[v][:]) for v in range(last_tile)]
-            + [(readings[last_tile][:, halves(0)], readings[last_tile][:, halves(1)])],
-            [(ingress[v][:], drained[v][:]) for v in range(TILES_PER_PASS)],
-        ]
-
-        def stage_products(half, v):
-            pair = banks[0:2] if v % 2 == 0 else banks[4:6]
-            u = TILES_PER_PASS + v
-            project(u, half, pair[0], pair[1])
-            nc.scalar.copy(staged_products[half][v][0], pair[0][:])
-            nc.scalar.activation(staged_products[half][v][1], pair[1][:], ACT.Copy, scale=minus_drain[:, v : v + 1])
-
-        win_bf_words = [win_bf[1][:].bitcast(F32), win_bf[0][:].bitcast(F32)]
-        products_for_vector(0, 0, banks[0:2], first_ingress[:])
-        reading_on_vector(0, 0, banks[0:2], first_ingress[:], turned[0][:])
+        win_bf_as_f32 = [win_bf[1][:].bitcast(F32), win_bf[0][:].bitcast(F32)]
+        plain_products(0, 0, banks[0:2], first_ingress[:])
+        plain_reading(0, 0, banks[0:2], first_ingress[:], turned[0][:])
         quantize_win(1, win_bf[1][:])
-        products_for_vector(0, 1, banks[4:6], ingress[1][:])
-        reading_on_vector(0, 1, banks[4:6], ingress[1][:], win_bf_words[1])
+        plain_products(0, 1, banks[4:6], ingress[1][:])
+        plain_reading(0, 1, banks[4:6], ingress[1][:], win_bf_as_f32[1])
         nc.tensor.transpose(banks[1][:, 0:P], vectors[:], identity[:])
         nc.scalar.copy(plus_drain[:], banks[1][:, 0:TILES_PER_PASS])
         nc.scalar.activation(minus_drain[:], banks[1][:, TILES_PER_PASS:ROW_TILES], ACT.Copy, scale=-1.0)
@@ -296,40 +301,46 @@ def tile_list_router_queue_alarms_kernel(
         quantize_win(3, win_bf[0][:])
 
         pairs_of = {1: (banks[2:4], banks[6:8]), 2: (banks[2:4], banks[6:8]), 3: (banks[0:2], banks[4:6])}
-        differences = {1: [turned[2][:], turned[3][:]], 2: win_bf_words, 3: win_bf_words}
+        differences = {1: [turned[2][:], turned[3][:]], 2: win_bf_as_f32, 3: win_bf_as_f32}
 
         def begin_tile(u):
             for half in range(HALVES):
-                products_for_vector(u, half, pairs_of[u][half], polled[u - 1][:, halves(half)])
+                plain_products(u, half, pairs_of[u][half], polled[u - 1][:, halves(half)])
 
         def end_tile(u):
             for half in range(HALVES):
-                reading_on_vector(u, half, pairs_of[u][half], polled[u - 1][:, halves(half)], differences[u][half])
+                plain_reading(u, half, pairs_of[u][half], polled[u - 1][:, halves(half)], differences[u][half])
             poll(u - 1, 0, M, polled[u - 1][:], baseline[u - 1])
             scatter(u, 0, S, slot_weights[:])
 
-        def stage_difference(half, c):
+        def woven_products(half, v):
+            pair = banks[0:2] if v % 2 == 0 else banks[4:6]
+            project(TILES_PER_PASS + v, half, pair)
+            nc.scalar.copy(ingress[v][:], pair[0][:])
+            nc.scalar.activation(drained[v][:], pair[1][:], ACT.Copy, scale=minus_drain[:, v : v + 1])
+
+        def woven_difference(c):
             bank = banks[2 + c % 2]
             for v in range(TILES_PER_PASS):
-                nc.tensor.matmul(bank[:, columns(v)], staged_products[half][v][0][:, columns(c)], identity[:], start=True, stop=False, is_transpose=True)
-                nc.tensor.matmul(bank[:, columns(v)], staged_products[half][v][1][:, columns(c)], identity[:], start=False, stop=True, is_transpose=True)
+                for term, staged in enumerate((ingress[v], drained[v])):
+                    nc.tensor.matmul(
+                        bank[:, columns(v)], staged[:, columns(c)], identity[:],
+                        start=term == 0, stop=term == 1, is_transpose=True,
+                    )
             nc.scalar.activation(
                 turned[c][:].rearrange("j (t p) -> j t p", t=PACK), bank[:].rearrange("j (p t) -> j t p", t=PACK), ACT.Abs
             )
 
-        def stage_turn_back(half, t):
+        def woven_reading(half, t):
             bank = banks[6 + t % 2]
             for c in range(BANK // P):
                 nc.tensor.transpose(bank[:, columns(c)], turned[c][:, columns(t)], identity[:])
             nc.scalar.copy(readings[t][:, halves(half)], bank[:])
             scatter(t, half * BANK, BANK, woven_weights[:, t * S + half * BANK : t * S + (half + 1) * BANK])
 
-        def quantize_z(b, q, staged):
-            nc.vector.quantize_mx(out=z_codes[b][q][:].bitcast(FP8X4), scales=z_scales[b][q][:], in_=staged)
-
-        def turn_z(q):
+        def turn_plain_z(q):
             word_bank = banks[6 + q % 2]
-            rows = [z_rows[(2 * q + c) % 4] for c in range(QUARTER // P)]
+            rows = [z_rows[(2 * q + c) % len(z_rows)] for c in range(QUARTER // P)]
             for c in range(QUARTER // P):
                 for v in range(TILES_PER_PASS):
                     nc.tensor.transpose(banks[2 + c][:, columns(v)], polled[v][:, columns(2 * q + c)], identity[:])
@@ -348,78 +359,86 @@ def tile_list_router_queue_alarms_kernel(
             )
             quantize_z(0, q, z_bf[q][:])
 
+        before, after = range(0, TILES_PER_PASS // 2), range(TILES_PER_PASS // 2, TILES_PER_PASS)
         begin_tile(1)
-        for v in range(TILES_PER_PASS):
+        for v in before:
             quantize_win(TILES_PER_PASS + v, late_win_bf[v][:])
         end_tile(1)
-        for quad in range(4):
+        for v in after:
+            quantize_win(TILES_PER_PASS + v, late_win_bf[v][:])
+        for quad in range(QUADS):
             nc.sync.dma_start(
-                out=woven_weights[32 * quad : 32 * (quad + 1), :], in_=wgs.rearrange("(p t) j -> p (t j)", t=PACK)
+                out=woven_weights[QUAD * quad : QUAD * (quad + 1), :], in_=wgs.rearrange("(p t) j -> p (t j)", t=PACK)
             )
         for t in range(PACK):
-            load_woven_base(t)
+            nc.sync.dma_start(out=woven_baseline[t][:], in_=base[PASS:H, :].rearrange("(p t) m -> p t m", t=PACK)[:, t, :])
         begin_tile(2)
-        for v in range(TILES_PER_PASS):
-            stage_products(0, v)
+        for v in before:
+            woven_products(0, v)
         end_tile(2)
+        for v in after:
+            woven_products(0, v)
         begin_tile(3)
         for c in range(BANK // P):
-            stage_difference(0, c)
+            woven_difference(c)
         end_tile(3)
-        poll(last_tile, 0, M, polled[last_tile][:], baseline[last_tile])
+        poll(3, 0, M, polled[3][:], baseline[3])
         for t in range(PACK):
-            stage_turn_back(0, t)
-            stage_products(1, t)
+            woven_reading(0, t)
+            woven_products(1, t)
         for c in range(BANK // P):
-            stage_difference(1, c)
+            woven_difference(c)
         for t in range(PACK):
-            stage_turn_back(1, t)
-            turn_z(t)
+            woven_reading(1, t)
+            turn_plain_z(t)
 
-        pairs = [banks[6:8], banks[2:4], banks[0:2], banks[4:6]]
+        sums = [banks[6:8], banks[2:4], banks[0:2], banks[4:5], banks[5:6]]
 
-        def alarm_pass(b, q):
+        def alarm_pass(b, i):
+            first, count = POLL_CHUNKS[i]
+            per_bank = BANK // count
+            source, at = (first // QUARTER, first % QUARTER) if b == 0 else (i, 0)
             for c in range(N_TILES):
                 nc.tensor.matmul_mx(
-                    out=pairs[q][c // 2][:, (c % 2) * QUARTER : (c % 2 + 1) * QUARTER],
+                    out=sums[i][c // per_bank][:, (c % per_bank) * count : (c % per_bank + 1) * count],
                     lhsT=wal_codes[:, b * N + c * P : b * N + (c + 1) * P].bitcast(FP8X4),
                     lhsT_scale=wal_sc[:, b * N + c * P : b * N + (c + 1) * P],
-                    rhs=z_codes[b][q][:].bitcast(FP8X4),
-                    rhs_scale=z_scales[b][q][:],
-                    start=b == 0 and c % 2 == 0,
-                    stop=b == R_PASSES - 1 and c % 2 == 1,
+                    rhs=z_codes[b][source][:, at : at + count].bitcast(FP8X4),
+                    rhs_scale=z_scales[b][source][:, at : at + count],
+                    start=b == 0 and c % per_bank == 0,
+                    stop=b == R_PASSES - 1 and c % per_bank == per_bank - 1,
                 )
 
-        def finish(q):
-            alarm_pass(1, q)
-            for g in range(2):
-                staged = result[(2 * q + g) % 4]
-                for c in range(2):
-                    part = slice(c * QUARTER, (c + 1) * QUARTER)
-                    column = bias_col[:, 2 * g + c : 2 * g + c + 1]
-                    if q >= 2 and g == 1:
-                        nc.vector.tensor_scalar_add(staged[:, part], pairs[q][g][:, part], column)
+        def finish(i):
+            first, count = POLL_CHUNKS[i]
+            per_bank = BANK // count
+            alarm_pass(1, i)
+            for g, bank in enumerate(sums[i]):
+                result = results[(first // P + g) % len(results)]
+                for c in range(per_bank):
+                    part = slice(c * count, (c + 1) * count)
+                    column = bias_col[:, per_bank * g + c : per_bank * g + c + 1]
+                    if (i, g) in EMPTIED_BY_VECTOR:
+                        nc.vector.tensor_scalar_add(result[:, part], bank[:, part], column)
                     else:
-                        nc.scalar.activation(staged[:, part], pairs[q][g][:, part], ACT.Identity, bias=column)
+                        nc.scalar.activation(result[:, part], bank[:, part], ACT.Identity, bias=column)
+                scores = slice(per_bank * g * P, per_bank * (g + 1) * P)
                 nc.sync.dma_start(
-                    out=out[2 * g * P : (2 * g + 2) * P, q * QUARTER : (q + 1) * QUARTER].rearrange("(c p) m -> p c m", p=P),
-                    in_=staged[:].rearrange("p (c m) -> p c m", c=2),
+                    out=out[scores, first : first + count].rearrange("(c p) m -> p c m", p=P),
+                    in_=result[:].rearrange("p (c m) -> p c m", c=per_bank),
                 )
 
-        last = M // QUARTER - 1
-        woven = [landing[last][:, halves(0)].bitcast(BF16), landing[last][:, halves(1)].bitcast(BF16), z_bf[0][:], z_bf[1][:]]
-        for q in range(M // QUARTER):
-            alarm_pass(0, q)
-        for q in range(M // QUARTER):
+        woven_bf = [landing[3][:].bitcast(BF16), landing[4][:].bitcast(BF16), z_bf[0][:], z_bf[1][:, 0:PASS], z_bf[2][:, 0:PASS]]
+        for i in range(len(POLL_CHUNKS)):
+            alarm_pass(0, i)
+        for i, (first, count) in enumerate(POLL_CHUNKS):
             for t in range(PACK):
-                poll(t, q * QUARTER, QUARTER, landing[q][:, t * QUARTER : (t + 1) * QUARTER], woven_baseline[t])
-            dst = woven[q].rearrange("p (m t) -> p m t", t=PACK)
-            src = landing[q][:].rearrange("p (t m) -> p m t", t=PACK)
-            if q == last:
+                poll(t, first, count, landing[i][:, t * count : (t + 1) * count], woven_baseline[t])
+            dst = woven_bf[i].rearrange("p (m t) -> p m t", t=PACK)
+            src = landing[i][:].rearrange("p (t m) -> p m t", t=PACK)
+            if count < QUARTER:
                 nc.vector.tensor_scalar_mul(dst, src, -1.0)
             else:
                 nc.scalar.activation(dst, src, ACT.Copy, scale=-1.0)
-            quantize_z(1, q, woven[q])
-            if q > 0:
-                finish(q - 1)
-        finish(last)
+            quantize_z(1, i, woven_bf[i])
+            finish(i)

@@ -35,7 +35,8 @@ WIN_CHUNKS = ((0, 1), (1, 2), (2, 4), (4, 6), (6, 8))
 WEG_CHUNKS = ((0, 2), (2, 8))
 POLL_CHUNKS = ((0, 256), (256, 256), (512, 256), (768, 128), (896, 128))
 EMPTIED_BY_VECTOR = ((2, 1), (4, 0))
-MOVED_ROWS = 112
+PASS_SHIFT = 16
+MOVED_ROWS = P - PASS_SHIFT
 
 KIB = 1024
 TABLE_AT = (0, 16 * KIB)
@@ -75,7 +76,7 @@ def tile_list_router_queue_alarms_kernel(
             tiles("picked0_", HALVES, BANK, U32),
             [placed(f"picked1_{half}", BANK, U32, TABLE_SCALES_AT + 4 * BANK * half) for half in range(HALVES)],
         ]
-        picked_scales = [placed("picked_scales0", S, U8, TABLE_AT[0] + 8 * KIB), sbuf("picked_scales1", S, U8)]
+        picked_scales = tiles("picked_scales", K_PASSES, S, U8)
 
         win_raw = [
             [
@@ -95,13 +96,7 @@ def tile_list_router_queue_alarms_kernel(
             placed(f"landing{first}", PACK * count, F32, WIN_RAW_AT + 4 * PACK * first) for first, count in POLL_CHUNKS
         ]
         win_bf = tiles("win_bf", 2, K_PASSES * PASS, BF16)
-        early_codes_at = (TABLE_AT[0] + 10 * KIB, TABLE_AT[0] + 12 * KIB)
-        win_codes = [
-            placed(f"win_codes{u}", K_PASSES * P, U32, early_codes_at[u])
-            if u < len(early_codes_at)
-            else sbuf(f"win_codes{u}", K_PASSES * P, U32)
-            for u in range(ROW_TILES)
-        ]
+        win_codes = [placed(f"win_codes{u}", K_PASSES * P, U32, TABLE_AT[0] + 8 * KIB + KIB * u) if u > 0 else sbuf("win_codes0", K_PASSES * P, U32) for u in range(ROW_TILES)]
         win_scales = tiles("win_scales", ROW_TILES, K_PASSES * P, U8)
         weg_codes = [sbuf(f"weg_codes{lo}", K_PASSES * 2 * P * (hi - lo), U8) for lo, hi in WEG_CHUNKS]
         weg_sc = sbuf("weg_sc", K_PASSES * H, U8)
@@ -113,7 +108,6 @@ def tile_list_router_queue_alarms_kernel(
         pages = tiles("page", PACK, T2, F32)
         readings = [placed(f"readings{t}", S, F32, READINGS_AT + 4 * S * t) for t in range(PACK)]
         polled = tiles("polled", TILES_PER_PASS, M, F32)
-        first_ingress = placed("first_ingress", BANK, F32, early_codes_at[1])
         ingress = tiles("ingress", TILES_PER_PASS, BANK, F32)
         drained = tiles("drained", TILES_PER_PASS, BANK, F32)
         turned = tiles("turned", BANK // P, BANK, F32)
@@ -130,18 +124,16 @@ def tile_list_router_queue_alarms_kernel(
         results = [placed(f"result{i}", BANK, F32, TABLE_AT[0] + 4 * BANK * i) for i in range(4)]
         vectors = sbuf("vectors", P, F32)
         first_drain = sbuf("first_drain", 1, F32)
-        plus_drain = sbuf("plus_drain", TILES_PER_PASS, F32)
-        minus_drain = sbuf("minus_drain", TILES_PER_PASS, F32)
+        plus_drain = sbuf("plus_drain", 2, F32)
+        minus_drain = sbuf("minus_drain", ROW_TILES, F32)
         bias_col = sbuf("bias_col", N_TILES, F32)
         identity = sbuf("identity", P, F32)
 
         nc.vector.memset(table_scales[:].bitcast(I32), 0)
-        nc.vector.memset(vectors[:], 0.0)
-        nc.vector.memset(picked_scales[1][:].bitcast(I32), 0)
         nc.vector.memset(weg_sc[:].bitcast(I32), 0)
+        nc.vector.memset(picked_scales[1][:].bitcast(I32), 0)
+        nc.vector.memset(vectors[:], 0.0)
         nc.vector.memset(wal_sc[:].bitcast(I32), 0)
-        for page in pages:
-            nc.vector.memset(page[:].bitcast(I32), 0)
         make_identity(nc, identity[:])
 
         def load_scales(scale_tile, scales):
@@ -177,24 +169,27 @@ def tile_list_router_queue_alarms_kernel(
         nc.sync.dma_start(idx3[:], offs3)
         load_weg(0)
         nc.sync.dma_start(out=first_drain[:], in_=drain[0:P].rearrange("(p o) -> p o", o=1))
-        for part in (slice(0, T // 2), slice(T // 2, T)):
+        table_parts = (slice(0, T // 2), slice(T // 2, T))
+        for part in table_parts:
             load_table(0, part)
         load_win(0)
-        for quad in range(QUADS):
-            nc.sync.dma_start(
-                out=table_scales[QUAD * quad : QUAD * quad + 4 * K_PASSES, :].bitcast(I32),
-                in_=tab_scales[:, 4 * quad : 4 * quad + 4, :].bitcast(I32),
+        for r in range(4):
+            nc.scalar.dma_start(
+                out=table_scales[r:P:PASS_SHIFT, :].bitcast(I32),
+                in_=tab_scales.bitcast(I32).rearrange("a (q r) c -> r q a c", r=4)[r],
             )
-        load_table(1, slice(0, T))
-        nc.sync.dma_start(out=vectors[1:ROW_TILES, :], in_=drain[P:H].rearrange("(u p) -> u p", p=P))
-        nc.sync.dma_start(out=vectors[ROW_TILES : ROW_TILES + N_TILES, :], in_=bias.rearrange("(c p) -> c p", p=P))
+        for part in table_parts:
+            load_table(1, part)
         load_scales(weg_sc, weg_scales)
+        nc.sync.dma_start(out=slot_weights[:, 0:BANK], in_=wgs[:, 0:BANK])
         load_win(1)
-        nc.sync.dma_start(out=slot_weights[:], in_=wgs)
+        nc.sync.dma_start(out=vectors[0:ROW_TILES, :], in_=drain.rearrange("(u p) -> u p", p=P))
+        nc.sync.dma_start(out=vectors[ROW_TILES : ROW_TILES + N_TILES, :], in_=bias.rearrange("(c p) -> c p", p=P))
+        nc.sync.dma_start(out=slot_weights[:, BANK:S], in_=wgs[:, BANK:S])
         load_win(2)
+        load_base(0)
         load_weg(1)
         load_win(3)
-        load_base(0)
         load_win(4)
         for u in range(1, TILES_PER_PASS):
             load_base(u)
@@ -221,37 +216,40 @@ def tile_list_router_queue_alarms_kernel(
             first = (u - WIN_CHUNKS[chunk][0]) * P
             for a in range(K_PASSES):
                 nc.scalar.copy(
-                    staged[:, a * PASS : (a + 1) * PASS].rearrange("p (r i) -> p r i", i=PACK),
-                    win_raw[chunk][a][:].rearrange("p (i r) -> p r i", i=PACK)[:, first : first + P, :],
+                    staged[:, a * PASS : (a + 1) * PASS].rearrange("p (c e i) -> p c i e", i=PACK, e=4),
+                    win_raw[chunk][a][:].rearrange("p (i c e) -> p c i e", i=PACK, e=4)[:, first // 4 : (first + P) // 4, :, :],
                 )
             nc.vector.quantize_mx(out=win_codes[u][:].bitcast(FP8X4), scales=win_scales[u][:], in_=staged)
 
         def gather_words(a, half):
             nc.vector.tensor_copy(picked[a][half][:], table[a][:].bitcast(U32).indirect(entries(idx, half * BANK, BANK)))
 
-        def project(u, half, pair):
+        def project(u, half, pair, at=0, count=BANK):
             chunk = chunk_of(WEG_CHUNKS, u)
             lo, hi = WEG_CHUNKS[chunk]
             for a in range(K_PASSES):
                 nc.tensor.matmul_mx(
-                    out=pair[0][:],
+                    out=pair[0][:, 0:count],
                     lhsT=win_codes[u][:, columns(a)].bitcast(FP8X4),
                     lhsT_scale=win_scales[u][:, columns(a)],
-                    rhs=picked[a][half][:].bitcast(FP8X4),
-                    rhs_scale=picked_scales[0][4 * a : P, halves(half)],
+                    rhs=picked[a][half][:, at : at + count].bitcast(FP8X4),
+                    rhs_scale=picked_scales[a][:, half * BANK + at : half * BANK + at + count],
                     start=a == 0,
                     stop=a == K_PASSES - 1,
                 )
                 first = 2 * P * (a * (hi - lo) + u - lo)
-                nc.tensor.matmul_mx(
-                    out=pair[1][:],
-                    lhsT=weg_codes[chunk][:, first : first + 2 * P].bitcast(FP4X4),
-                    lhsT_scale=weg_sc[:, a * H + u * P : a * H + (u + 1) * P],
-                    rhs=picked[a][half][:].bitcast(FP8X4),
-                    rhs_scale=picked_scales[a][:, halves(half)],
-                    start=a == 0,
-                    stop=a == K_PASSES - 1,
-                )
+                width = BANK if count == BANK else P
+                for lo_port in range(0, count, width):
+                    port = at + lo_port
+                    nc.tensor.matmul_mx(
+                        out=pair[1][:, lo_port : lo_port + width],
+                        lhsT=weg_codes[chunk][:, first : first + 2 * P].bitcast(FP4X4),
+                        lhsT_scale=weg_sc[:, a * H + u * P : a * H + (u + 1) * P],
+                        rhs=picked[a][half][:, port : port + width].bitcast(FP8X4),
+                        rhs_scale=picked_scales[a][:, half * BANK + port : half * BANK + port + width],
+                        start=a == 0 and lo_port == 0,
+                        stop=a == K_PASSES - 1 and lo_port + width == count,
+                    )
 
         def scatter(t, first, count, weights):
             nc.vector.tensor_tensor(
@@ -266,61 +264,78 @@ def tile_list_router_queue_alarms_kernel(
         def quantize_z(b, i, staged):
             nc.vector.quantize_mx(out=z_codes[b][i][:].bitcast(FP8X4), scales=z_scales[b][i][:], in_=staged)
 
-        for half in range(HALVES):
-            gather_words(0, half)
         nc.vector.tensor_copy(picked_scales[0][:], table_scales[:].indirect(idx[:]))
         nc.scalar.dma_start(
-            out=picked_scales[1][0:MOVED_ROWS, :].bitcast(I32), in_=picked_scales[0][4 : 4 + MOVED_ROWS, :].bitcast(I32)
+            out=picked_scales[1][0:MOVED_ROWS, :].bitcast(I32), in_=picked_scales[0][PASS_SHIFT:P, :].bitcast(I32)
         )
+        for half in range(HALVES):
+            gather_words(0, half)
         quantize_win(0, win_bf[0][:])
         for half in range(HALVES):
             gather_words(1, half)
 
-        def plain_products(u, half, pair, staged):
-            project(u, half, pair)
-            nc.scalar.copy(staged, pair[0][:])
+        def plain_products(u, half, pair, staged, at=0, count=BANK):
+            project(u, half, pair, at, count)
+            nc.scalar.copy(staged, pair[0][:, 0:count])
 
-        def plain_reading(u, half, pair, staged, difference):
+        def plain_reading(u, half, pair, staged, difference, at=0, count=BANK):
             rate = first_drain[:] if u == 0 else plus_drain[:, u : u + 1]
-            nc.vector.scalar_tensor_tensor(difference, pair[1][:], rate, staged, ALU.mult, ALU.subtract)
-            nc.scalar.activation(readings[u][:, halves(half)], difference, ACT.Abs)
+            nc.vector.scalar_tensor_tensor(difference, pair[1][:, 0:count], rate, staged, ALU.mult, ALU.subtract)
+            nc.scalar.activation(readings[u][:, half * BANK + at : half * BANK + at + count], difference, ACT.Abs)
 
-        win_bf_as_f32 = [win_bf[1][:].bitcast(F32), win_bf[0][:].bitcast(F32)]
-        plain_products(0, 0, banks[0:2], first_ingress[:])
-        plain_reading(0, 0, banks[0:2], first_ingress[:], turned[0][:])
+        for q in range(2):
+            part = slice(q * QUARTER, (q + 1) * QUARTER)
+            plain_products(0, 0, banks[2 * q : 2 * q + 2], ingress[2][:, part], q * QUARTER, QUARTER)
+        for q in range(2):
+            part = slice(q * QUARTER, (q + 1) * QUARTER)
+            plain_reading(0, 0, banks[2 * q : 2 * q + 2], ingress[2][:, part], drained[2][:, part], q * QUARTER, QUARTER)
+        for page in pages:
+            nc.vector.memset(page[:].bitcast(I32), 0)
+        plain_products(0, 1, banks[4:6], ingress[3][:])
+        scatter(0, 0, QUARTER, slot_weights[:, 0:QUARTER])
+        plain_reading(0, 1, banks[4:6], ingress[3][:], drained[3][:])
         quantize_win(1, win_bf[1][:])
-        plain_products(0, 1, banks[4:6], ingress[1][:])
-        plain_reading(0, 1, banks[4:6], ingress[1][:], win_bf_as_f32[1])
+        scatter(0, QUARTER, QUARTER, slot_weights[:, QUARTER:BANK])
+        scatter(0, BANK, BANK, slot_weights[:, halves(1)])
         nc.tensor.transpose(banks[1][:, 0:P], vectors[:], identity[:])
-        nc.scalar.copy(plus_drain[:], banks[1][:, 0:TILES_PER_PASS])
-        nc.scalar.activation(minus_drain[:], banks[1][:, TILES_PER_PASS:ROW_TILES], ACT.Copy, scale=-1.0)
+        nc.scalar.copy(plus_drain[:], banks[1][:, 0:2])
+        nc.scalar.activation(minus_drain[:], banks[1][:, 0:ROW_TILES], ACT.Copy, scale=-1.0)
         nc.scalar.copy(bias_col[:], banks[1][:, ROW_TILES : ROW_TILES + N_TILES])
-        for half in range(HALVES):
-            scatter(0, half * BANK, BANK, slot_weights[:, halves(half)])
-        quantize_win(2, turned[0][:].bitcast(BF16))
-        quantize_win(3, win_bf[0][:])
 
-        pairs_of = {1: (banks[2:4], banks[6:8]), 2: (banks[2:4], banks[6:8]), 3: (banks[0:2], banks[4:6])}
-        differences = {1: [turned[2][:], turned[3][:]], 2: win_bf_as_f32, 3: win_bf_as_f32}
+        def staged_products(u, half, pair, slot):
+            project(u, half, pair)
+            nc.scalar.copy(ingress[slot][:], pair[0][:])
+            nc.scalar.activation(drained[slot][:], pair[1][:], ACT.Copy, scale=minus_drain[:, u : u + 1])
 
-        def begin_tile(u):
+        def turned_products(u):
             for half in range(HALVES):
-                plain_products(u, half, pairs_of[u][half], polled[u - 1][:, halves(half)])
+                staged_products(u, half, banks[2 * half : 2 * half + 2], 2 * (u % 2) + half)
 
-        def end_tile(u):
+        def turned_difference(u):
             for half in range(HALVES):
-                plain_reading(u, half, pairs_of[u][half], polled[u - 1][:, halves(half)], differences[u][half])
-            poll(u - 1, 0, M, polled[u - 1][:], baseline[u - 1])
+                slot, bank = 2 * (u % 2) + half, banks[4 + half]
+                for c in range(BANK // P):
+                    for term, staged in enumerate((ingress[slot], drained[slot])):
+                        nc.tensor.matmul(
+                            bank[:, columns(c)], staged[:, columns(c)], identity[:],
+                            start=term == 0, stop=term == 1, is_transpose=True,
+                        )
+                nc.scalar.activation(turned[slot][:], bank[:], ACT.Abs)
+
+        def turned_reading(u):
+            for half in range(HALVES):
+                slot, bank = 2 * (u % 2) + half, banks[6 + half]
+                for c in range(BANK // P):
+                    nc.tensor.transpose(bank[:, columns(c)], turned[slot][:, columns(c)], identity[:])
+                nc.scalar.copy(readings[u][:, halves(half)], bank[:])
             scatter(u, 0, S, slot_weights[:])
+            poll(u, 0, M, polled[u][:], baseline[u])
 
         def woven_products(half, v):
-            pair = banks[0:2] if v % 2 == 0 else banks[4:6]
-            project(TILES_PER_PASS + v, half, pair)
-            nc.scalar.copy(ingress[v][:], pair[0][:])
-            nc.scalar.activation(drained[v][:], pair[1][:], ACT.Copy, scale=minus_drain[:, v : v + 1])
+            staged_products(TILES_PER_PASS + v, half, banks[2 * (v % 2) : 2 * (v % 2) + 2], v)
 
         def woven_difference(c):
-            bank = banks[2 + c % 2]
+            bank = banks[4 + c % 2]
             for v in range(TILES_PER_PASS):
                 for term, staged in enumerate((ingress[v], drained[v])):
                     nc.tensor.matmul(
@@ -343,10 +358,10 @@ def tile_list_router_queue_alarms_kernel(
             rows = [z_rows[(2 * q + c) % len(z_rows)] for c in range(QUARTER // P)]
             for c in range(QUARTER // P):
                 for v in range(TILES_PER_PASS):
-                    nc.tensor.transpose(banks[2 + c][:, columns(v)], polled[v][:, columns(2 * q + c)], identity[:])
+                    nc.tensor.transpose(banks[4 + c][:, columns(v)], polled[v][:, columns(2 * q + c)], identity[:])
                 nc.scalar.activation(
                     rows[c][:].rearrange("m (w p e) -> m w p e", w=2, e=2),
-                    banks[2 + c][:].rearrange("m (p w e) -> m w p e", w=2, e=2),
+                    banks[4 + c][:].rearrange("m (p w e) -> m w p e", w=2, e=2),
                     ACT.Copy,
                     scale=-1.0,
                 )
@@ -359,30 +374,38 @@ def tile_list_router_queue_alarms_kernel(
             )
             quantize_z(0, q, z_bf[q][:])
 
-        before, after = range(0, TILES_PER_PASS // 2), range(TILES_PER_PASS // 2, TILES_PER_PASS)
-        begin_tile(1)
-        for v in before:
+        quantize_win(2, win_bf[0][:])
+        tile1_pairs = (banks[6:8], banks[2:4])
+        for half in range(HALVES):
+            plain_products(1, half, tile1_pairs[half], polled[0][:, halves(half)])
+        quantize_win(3, win_bf[1][:])
+        for half in range(HALVES):
+            plain_reading(1, half, tile1_pairs[half], polled[0][:, halves(half)], turned[2 + half][:])
+        poll(0, 0, M, polled[0][:], baseline[0])
+        scatter(1, 0, S, slot_weights[:])
+        poll(1, 0, M, polled[1][:], baseline[1])
+        turned_products(2)
+        for v in (0, 1):
             quantize_win(TILES_PER_PASS + v, late_win_bf[v][:])
-        end_tile(1)
-        for v in after:
+        turned_difference(2)
+        for v in (2, 3):
             quantize_win(TILES_PER_PASS + v, late_win_bf[v][:])
+        turned_reading(2)
         for quad in range(QUADS):
             nc.sync.dma_start(
                 out=woven_weights[QUAD * quad : QUAD * (quad + 1), :], in_=wgs.rearrange("(p t) j -> p (t j)", t=PACK)
             )
         for t in range(PACK):
             nc.sync.dma_start(out=woven_baseline[t][:], in_=base[PASS:H, :].rearrange("(p t) m -> p t m", t=PACK)[:, t, :])
-        begin_tile(2)
-        for v in before:
+        turned_products(3)
+        turned_difference(3)
+        for v in (0, 1):
             woven_products(0, v)
-        end_tile(2)
-        for v in after:
+        turned_reading(3)
+        for v in (2, 3):
             woven_products(0, v)
-        begin_tile(3)
         for c in range(BANK // P):
             woven_difference(c)
-        end_tile(3)
-        poll(3, 0, M, polled[3][:], baseline[3])
         for t in range(PACK):
             woven_reading(0, t)
             woven_products(1, t)
@@ -392,7 +415,7 @@ def tile_list_router_queue_alarms_kernel(
             woven_reading(1, t)
             turn_plain_z(t)
 
-        sums = [banks[6:8], banks[2:4], banks[0:2], banks[4:5], banks[5:6]]
+        sums = [banks[6:8], banks[4:6], banks[0:2], banks[2:3], banks[3:4]]
 
         def alarm_pass(b, i):
             first, count = POLL_CHUNKS[i]
@@ -434,8 +457,8 @@ def tile_list_router_queue_alarms_kernel(
         for i, (first, count) in enumerate(POLL_CHUNKS):
             for t in range(PACK):
                 poll(t, first, count, landing[i][:, t * count : (t + 1) * count], woven_baseline[t])
-            dst = woven_bf[i].rearrange("p (m t) -> p m t", t=PACK)
-            src = landing[i][:].rearrange("p (t m) -> p m t", t=PACK)
+            dst = woven_bf[i].rearrange("p (c e t) -> p c t e", t=PACK, e=4)
+            src = landing[i][:].rearrange("p (t c e) -> p c t e", t=PACK, e=4)
             if count < QUARTER:
                 nc.vector.tensor_scalar_mul(dst, src, -1.0)
             else:

@@ -34,7 +34,7 @@ QUARTERS = M // QUARTER
 WIN_CHUNKS = ((0, 1), (1, 2), (2, 4), (4, 6), (6, 8))
 WEG_CHUNKS = ((0, 2), (2, 8))
 POLL_CHUNKS = ((0, 256), (256, 256), (512, 256), (768, 128), (896, 128))
-EMPTIED_BY_VECTOR = ((2, 1), (4, 0))
+EMPTIED_BY_VECTOR = ((2, 1), (4, 1))
 PASS_SHIFT = 16
 MOVED_ROWS = P - PASS_SHIFT
 
@@ -99,7 +99,7 @@ def tile_list_router_queue_alarms_kernel(
         win_codes = [placed(f"win_codes{u}", K_PASSES * P, U32, TABLE_AT[0] + 8 * KIB + KIB * u) if u > 0 else sbuf("win_codes0", K_PASSES * P, U32) for u in range(ROW_TILES)]
         win_scales = tiles("win_scales", ROW_TILES, K_PASSES * P, U8)
         weg_codes = [sbuf(f"weg_codes{lo}", K_PASSES * 2 * P * (hi - lo), U8) for lo, hi in WEG_CHUNKS]
-        weg_sc = sbuf("weg_sc", K_PASSES * H, U8)
+        weg_sc = [sbuf(f"weg_sc{lo}", K_PASSES * P * (hi - lo), U8) for lo, hi in WEG_CHUNKS]
         wal_codes = sbuf("wal_codes", R_PASSES * N, I32)
         wal_sc = sbuf("wal_sc", R_PASSES * N, U8)
         slot_weights = sbuf("slot_weights", S, F32)
@@ -121,17 +121,18 @@ def tile_list_router_queue_alarms_kernel(
             tiles("z_scales0_", QUARTERS, QUARTER, U8),
             [sbuf(f"z_scales1_{first}", count, U8) for first, count in POLL_CHUNKS],
         ]
-        results = [placed(f"result{i}", BANK, F32, TABLE_AT[0] + 4 * BANK * i) for i in range(4)]
+        results = [placed(f"result{i}", BANK, F32, TABLE_AT[0] + 4 * BANK * i) for i in range(8)]
         vectors = sbuf("vectors", P, F32)
         first_drain = sbuf("first_drain", 1, F32)
-        plus_drain = sbuf("plus_drain", 2, F32)
+        minus_first_drain = sbuf("minus_first_drain", 1, F32)
         minus_drain = sbuf("minus_drain", ROW_TILES, F32)
         bias_col = sbuf("bias_col", N_TILES, F32)
         identity = sbuf("identity", P, F32)
 
         nc.vector.memset(table_scales[:].bitcast(I32), 0)
-        nc.vector.memset(weg_sc[:].bitcast(I32), 0)
+        nc.vector.memset(weg_sc[0][:].bitcast(I32), 0)
         nc.vector.memset(picked_scales[1][:].bitcast(I32), 0)
+        nc.vector.memset(weg_sc[1][:].bitcast(I32), 0)
         nc.vector.memset(vectors[:], 0.0)
         nc.vector.memset(wal_sc[:].bitcast(I32), 0)
         make_identity(nc, identity[:])
@@ -146,9 +147,9 @@ def tile_list_router_queue_alarms_kernel(
         def load_table(a, part):
             nc.sync.dma_start(out=table[a][:, part], in_=tab_words[a].rearrange("p t i -> p (t i)").bitcast(I32)[:, part])
 
-        def load_win(chunk):
+        def load_win(chunk, *passes):
             lo, hi = WIN_CHUNKS[chunk]
-            for a in range(K_PASSES):
+            for a in passes or range(K_PASSES):
                 nc.sync.dma_start(
                     out=win_raw[chunk][a][:].rearrange("p (i r) -> p i r", i=PACK),
                     in_=win[a * PASS : (a + 1) * PASS, lo * P : hi * P].rearrange("(p i) r -> p i r", i=PACK),
@@ -160,6 +161,10 @@ def tile_list_router_queue_alarms_kernel(
                 out=weg_codes[chunk][:].bitcast(I32).rearrange("p (a c) -> p a c", a=K_PASSES),
                 in_=weg_words[:, :, 2 * lo * P : 2 * hi * P].bitcast(I32).rearrange("a p c -> p a c"),
             )
+
+        def load_weg_scales(chunk):
+            lo, hi = WEG_CHUNKS[chunk]
+            load_scales(weg_sc[chunk], weg_scales[:, :, lo * P : hi * P])
 
         def load_base(u):
             nc.sync.dma_start(out=baseline[u][:], in_=base[u * P : (u + 1) * P, :])
@@ -178,17 +183,19 @@ def tile_list_router_queue_alarms_kernel(
                 out=table_scales[r:P:PASS_SHIFT, :].bitcast(I32),
                 in_=tab_scales.bitcast(I32).rearrange("a (q r) c -> r q a c", r=4)[r],
             )
-        for part in table_parts:
-            load_table(1, part)
-        load_scales(weg_sc, weg_scales)
-        nc.sync.dma_start(out=slot_weights[:, 0:BANK], in_=wgs[:, 0:BANK])
+        load_table(1, table_parts[0])
+        load_weg_scales(0)
+        load_table(1, table_parts[1])
+        nc.sync.dma_start(out=slot_weights[:, 0:QUARTER], in_=wgs[:, 0:QUARTER])
         load_win(1)
         nc.sync.dma_start(out=vectors[0:ROW_TILES, :], in_=drain.rearrange("(u p) -> u p", p=P))
         nc.sync.dma_start(out=vectors[ROW_TILES : ROW_TILES + N_TILES, :], in_=bias.rearrange("(c p) -> c p", p=P))
-        nc.sync.dma_start(out=slot_weights[:, BANK:S], in_=wgs[:, BANK:S])
-        load_win(2)
+        load_win(2, 0)
+        nc.sync.dma_start(out=slot_weights[:, QUARTER:S], in_=wgs[:, QUARTER:S])
+        load_win(2, 1)
         load_base(0)
         load_weg(1)
+        load_weg_scales(1)
         load_win(3)
         load_win(4)
         for u in range(1, TILES_PER_PASS):
@@ -244,7 +251,7 @@ def tile_list_router_queue_alarms_kernel(
                     nc.tensor.matmul_mx(
                         out=pair[1][:, lo_port : lo_port + width],
                         lhsT=weg_codes[chunk][:, first : first + 2 * P].bitcast(FP4X4),
-                        lhsT_scale=weg_sc[:, a * H + u * P : a * H + (u + 1) * P],
+                        lhsT_scale=weg_sc[chunk][:, first // 2 : first // 2 + P],
                         rhs=picked[a][half][:, port : port + width].bitcast(FP8X4),
                         rhs_scale=picked_scales[a][:, half * BANK + port : half * BANK + port + width],
                         start=a == 0 and lo_port == 0,
@@ -264,6 +271,7 @@ def tile_list_router_queue_alarms_kernel(
         def quantize_z(b, i, staged):
             nc.vector.quantize_mx(out=z_codes[b][i][:].bitcast(FP8X4), scales=z_scales[b][i][:], in_=staged)
 
+        nc.scalar.activation(minus_first_drain[:], first_drain[:], ACT.Copy, scale=-1.0)
         nc.vector.tensor_copy(picked_scales[0][:], table_scales[:].indirect(idx[:]))
         nc.scalar.dma_start(
             out=picked_scales[1][0:MOVED_ROWS, :].bitcast(I32), in_=picked_scales[0][PASS_SHIFT:P, :].bitcast(I32)
@@ -279,8 +287,7 @@ def tile_list_router_queue_alarms_kernel(
             nc.scalar.copy(staged, pair[0][:, 0:count])
 
         def plain_reading(u, half, pair, staged, difference, at=0, count=BANK):
-            rate = first_drain[:] if u == 0 else plus_drain[:, u : u + 1]
-            nc.vector.scalar_tensor_tensor(difference, pair[1][:, 0:count], rate, staged, ALU.mult, ALU.subtract)
+            nc.vector.scalar_tensor_tensor(difference, pair[1][:, 0:count], minus_first_drain[:], staged, ALU.mult, ALU.add)
             nc.scalar.activation(readings[u][:, half * BANK + at : half * BANK + at + count], difference, ACT.Abs)
 
         for q in range(2):
@@ -293,14 +300,13 @@ def tile_list_router_queue_alarms_kernel(
             nc.vector.memset(page[:].bitcast(I32), 0)
         plain_products(0, 1, banks[4:6], ingress[3][:])
         scatter(0, 0, QUARTER, slot_weights[:, 0:QUARTER])
-        plain_reading(0, 1, banks[4:6], ingress[3][:], drained[3][:])
         quantize_win(1, win_bf[1][:])
+        plain_reading(0, 1, banks[4:6], ingress[3][:], drained[3][:])
         scatter(0, QUARTER, QUARTER, slot_weights[:, QUARTER:BANK])
         scatter(0, BANK, BANK, slot_weights[:, halves(1)])
-        nc.tensor.transpose(banks[1][:, 0:P], vectors[:], identity[:])
-        nc.scalar.copy(plus_drain[:], banks[1][:, 0:2])
-        nc.scalar.activation(minus_drain[:], banks[1][:, 0:ROW_TILES], ACT.Copy, scale=-1.0)
-        nc.scalar.copy(bias_col[:], banks[1][:, ROW_TILES : ROW_TILES + N_TILES])
+        nc.tensor.transpose(banks[7][:, 0:P], vectors[:], identity[:])
+        nc.scalar.activation(minus_drain[:], banks[7][:, 0:ROW_TILES], ACT.Copy, scale=-1.0)
+        nc.scalar.copy(bias_col[:], banks[7][:, ROW_TILES : ROW_TILES + N_TILES])
 
         def staged_products(u, half, pair, slot):
             project(u, half, pair)
@@ -328,7 +334,10 @@ def tile_list_router_queue_alarms_kernel(
                 for c in range(BANK // P):
                     nc.tensor.transpose(bank[:, columns(c)], turned[slot][:, columns(c)], identity[:])
                 nc.scalar.copy(readings[u][:, halves(half)], bank[:])
-            scatter(u, 0, S, slot_weights[:])
+                if u == 1:
+                    scatter(u, half * BANK, BANK, slot_weights[:, halves(half)])
+            if u > 1:
+                scatter(u, 0, S, slot_weights[:])
             poll(u, 0, M, polled[u][:], baseline[u])
 
         def woven_products(half, v):
@@ -375,22 +384,18 @@ def tile_list_router_queue_alarms_kernel(
             quantize_z(0, q, z_bf[q][:])
 
         quantize_win(2, win_bf[0][:])
-        tile1_pairs = (banks[6:8], banks[2:4])
-        for half in range(HALVES):
-            plain_products(1, half, tile1_pairs[half], polled[0][:, halves(half)])
-        quantize_win(3, win_bf[1][:])
-        for half in range(HALVES):
-            plain_reading(1, half, tile1_pairs[half], polled[0][:, halves(half)], turned[2 + half][:])
+        turned_products(1)
         poll(0, 0, M, polled[0][:], baseline[0])
-        scatter(1, 0, S, slot_weights[:])
-        poll(1, 0, M, polled[1][:], baseline[1])
-        turned_products(2)
+        turned_difference(1)
+        turned_reading(1)
+        quantize_win(3, win_bf[1][:])
         for v in (0, 1):
             quantize_win(TILES_PER_PASS + v, late_win_bf[v][:])
+        turned_products(2)
         turned_difference(2)
+        turned_reading(2)
         for v in (2, 3):
             quantize_win(TILES_PER_PASS + v, late_win_bf[v][:])
-        turned_reading(2)
         for quad in range(QUADS):
             nc.sync.dma_start(
                 out=woven_weights[QUAD * quad : QUAD * (quad + 1), :], in_=wgs.rearrange("(p t) j -> p (t j)", t=PACK)
@@ -415,13 +420,13 @@ def tile_list_router_queue_alarms_kernel(
             woven_reading(1, t)
             turn_plain_z(t)
 
-        sums = [banks[6:8], banks[4:6], banks[0:2], banks[2:3], banks[3:4]]
+        sums = [banks[6:8], banks[4:6], banks[0:2], banks[2:3], [banks[3], banks[6]]]
 
-        def alarm_pass(b, i):
+        def alarm_pass(b, i, score_tiles=range(N_TILES)):
             first, count = POLL_CHUNKS[i]
-            per_bank = BANK // count
+            per_bank = N_TILES // len(sums[i])
             source, at = (first // QUARTER, first % QUARTER) if b == 0 else (i, 0)
-            for c in range(N_TILES):
+            for c in score_tiles:
                 nc.tensor.matmul_mx(
                     out=sums[i][c // per_bank][:, (c % per_bank) * count : (c % per_bank + 1) * count],
                     lhsT=wal_codes[:, b * N + c * P : b * N + (c + 1) * P].bitcast(FP8X4),
@@ -434,26 +439,34 @@ def tile_list_router_queue_alarms_kernel(
 
         def finish(i):
             first, count = POLL_CHUNKS[i]
-            per_bank = BANK // count
+            per_bank = N_TILES // len(sums[i])
             alarm_pass(1, i)
             for g, bank in enumerate(sums[i]):
-                result = results[(first // P + g) % len(results)]
-                for c in range(per_bank):
-                    part = slice(c * count, (c + 1) * count)
-                    column = bias_col[:, per_bank * g + c : per_bank * g + c + 1]
-                    if (i, g) in EMPTIED_BY_VECTOR:
-                        nc.vector.tensor_scalar_add(result[:, part], bank[:, part], column)
-                    else:
+                result = results[(2 * i + g) % len(results)]
+                used = slice(0, per_bank * count)
+                if (i, g) in EMPTIED_BY_VECTOR:
+                    nc.vector.tensor_tensor(
+                        result[:, used].rearrange("p (c m) -> p c m", c=per_bank),
+                        bank[:, used].rearrange("p (c m) -> p c m", c=per_bank),
+                        bias_col[:, per_bank * g : per_bank * (g + 1)].unsqueeze(2).to_broadcast([P, per_bank, count]),
+                        ALU.add,
+                    )
+                else:
+                    for c in range(per_bank):
+                        part = slice(c * count, (c + 1) * count)
+                        column = bias_col[:, per_bank * g + c : per_bank * g + c + 1]
                         nc.scalar.activation(result[:, part], bank[:, part], ACT.Identity, bias=column)
                 scores = slice(per_bank * g * P, per_bank * (g + 1) * P)
                 nc.sync.dma_start(
                     out=out[scores, first : first + count].rearrange("(c p) m -> p c m", p=P),
-                    in_=result[:].rearrange("p (c m) -> p c m", c=per_bank),
+                    in_=result[:, used].rearrange("p (c m) -> p c m", c=per_bank),
                 )
 
         woven_bf = [landing[3][:].bitcast(BF16), landing[4][:].bitcast(BF16), z_bf[0][:], z_bf[1][:, 0:PASS], z_bf[2][:, 0:PASS]]
-        for i in range(len(POLL_CHUNKS)):
+        last = len(POLL_CHUNKS) - 1
+        for i in range(last):
             alarm_pass(0, i)
+        alarm_pass(0, last, range(0, 2))
         for i, (first, count) in enumerate(POLL_CHUNKS):
             for t in range(PACK):
                 poll(t, first, count, landing[i][:, t * count : (t + 1) * count], woven_baseline[t])
@@ -465,3 +478,5 @@ def tile_list_router_queue_alarms_kernel(
                 nc.scalar.activation(dst, src, ACT.Copy, scale=-1.0)
             quantize_z(1, i, woven_bf[i])
             finish(i)
+            if i == 0:
+                alarm_pass(0, last, range(2, 4))

@@ -73,8 +73,8 @@ def tile_list_router_queue_alarms_kernel(
         table = [placed(f"table{a}", T, I32, TABLE_AT[a]) for a in range(K_PASSES)]
         table_scales = placed("table_scales", T, U8, TABLE_SCALES_AT)
         picked = [
-            tiles("picked0_", HALVES, BANK, U32),
-            [placed(f"picked1_{half}", BANK, U32, TABLE_SCALES_AT + 4 * BANK * half) for half in range(HALVES)],
+            [sbuf("picked0_0", BANK, U32), placed("picked0_1", BANK, U32, TABLE_SCALES_AT)],
+            [placed("picked1_0", BANK, U32, TABLE_SCALES_AT + 4 * BANK), sbuf("picked1_1", BANK, U32)],
         ]
         picked_scales = tiles("picked_scales", K_PASSES, S, U8)
 
@@ -91,6 +91,7 @@ def tile_list_router_queue_alarms_kernel(
             placed(f"late_win_bf{v}", K_PASSES * PASS, BF16, WIN_RAW_AT + 8 * KIB + 2 * KIB * v)
             for v in range(TILES_PER_PASS)
         ]
+        second_quarter = placed("second_quarter", QUARTER, F32, WIN_RAW_AT + 6 * KIB)
         woven_weights = placed("woven_weights", PACK * S, F32, WIN_RAW_AT)
         landing = [
             placed(f"landing{first}", PACK * count, F32, WIN_RAW_AT + 4 * PACK * first) for first, count in POLL_CHUNKS
@@ -147,9 +148,9 @@ def tile_list_router_queue_alarms_kernel(
         def load_table(a, part):
             nc.sync.dma_start(out=table[a][:, part], in_=tab_words[a].rearrange("p t i -> p (t i)").bitcast(I32)[:, part])
 
-        def load_win(chunk, *passes):
+        def load_win(chunk):
             lo, hi = WIN_CHUNKS[chunk]
-            for a in passes or range(K_PASSES):
+            for a in range(K_PASSES):
                 nc.sync.dma_start(
                     out=win_raw[chunk][a][:].rearrange("p (i r) -> p i r", i=PACK),
                     in_=win[a * PASS : (a + 1) * PASS, lo * P : hi * P].rearrange("(p i) r -> p i r", i=PACK),
@@ -174,25 +175,23 @@ def tile_list_router_queue_alarms_kernel(
         nc.sync.dma_start(idx3[:], offs3)
         load_weg(0)
         nc.sync.dma_start(out=first_drain[:], in_=drain[0:P].rearrange("(p o) -> p o", o=1))
-        table_parts = (slice(0, T // 2), slice(T // 2, T))
-        for part in table_parts:
-            load_table(0, part)
-        load_win(0)
+        for part in range(4):
+            load_table(0, slice(part * T // 4, (part + 1) * T // 4))
         for r in range(4):
-            nc.scalar.dma_start(
+            nc.sync.dma_start(
                 out=table_scales[r:P:PASS_SHIFT, :].bitcast(I32),
                 in_=tab_scales.bitcast(I32).rearrange("a (q r) c -> r q a c", r=4)[r],
             )
-        load_table(1, table_parts[0])
+        load_win(0)
+        load_table(1, slice(0, T // 2))
         load_weg_scales(0)
-        load_table(1, table_parts[1])
+        load_table(1, slice(T // 2, T))
         nc.sync.dma_start(out=slot_weights[:, 0:QUARTER], in_=wgs[:, 0:QUARTER])
         load_win(1)
         nc.sync.dma_start(out=vectors[0:ROW_TILES, :], in_=drain.rearrange("(u p) -> u p", p=P))
         nc.sync.dma_start(out=vectors[ROW_TILES : ROW_TILES + N_TILES, :], in_=bias.rearrange("(c p) -> c p", p=P))
-        load_win(2, 0)
+        load_win(2)
         nc.sync.dma_start(out=slot_weights[:, QUARTER:S], in_=wgs[:, QUARTER:S])
-        load_win(2, 1)
         load_base(0)
         load_weg(1)
         load_weg_scales(1)
@@ -258,10 +257,9 @@ def tile_list_router_queue_alarms_kernel(
                         stop=a == K_PASSES - 1 and lo_port + width == count,
                     )
 
-        def scatter(t, first, count, weights):
-            nc.vector.tensor_tensor(
-                pages[t][:].indirect(entries(idx2, first, count)), readings[t][:, first : first + count], weights, ALU.mult
-            )
+        def scatter(t, first, count, weights, values=None):
+            values = readings[t][:, first : first + count] if values is None else values
+            nc.vector.tensor_tensor(pages[t][:].indirect(entries(idx2, first, count)), values, weights, ALU.mult)
 
         def poll(t, first, count, dst, base_rows):
             nc.vector.tensor_tensor(
@@ -272,12 +270,12 @@ def tile_list_router_queue_alarms_kernel(
             nc.vector.quantize_mx(out=z_codes[b][i][:].bitcast(FP8X4), scales=z_scales[b][i][:], in_=staged)
 
         nc.scalar.activation(minus_first_drain[:], first_drain[:], ACT.Copy, scale=-1.0)
+        gather_words(0, 0)
         nc.vector.tensor_copy(picked_scales[0][:], table_scales[:].indirect(idx[:]))
         nc.scalar.dma_start(
             out=picked_scales[1][0:MOVED_ROWS, :].bitcast(I32), in_=picked_scales[0][PASS_SHIFT:P, :].bitcast(I32)
         )
-        for half in range(HALVES):
-            gather_words(0, half)
+        gather_words(0, 1)
         quantize_win(0, win_bf[0][:])
         for half in range(HALVES):
             gather_words(1, half)
@@ -286,23 +284,26 @@ def tile_list_router_queue_alarms_kernel(
             project(u, half, pair, at, count)
             nc.scalar.copy(staged, pair[0][:, 0:count])
 
-        def plain_reading(u, half, pair, staged, difference, at=0, count=BANK):
+        def first_difference(pair, staged, difference, count):
             nc.vector.scalar_tensor_tensor(difference, pair[1][:, 0:count], minus_first_drain[:], staged, ALU.mult, ALU.add)
-            nc.scalar.activation(readings[u][:, half * BANK + at : half * BANK + at + count], difference, ACT.Abs)
 
         for q in range(2):
             part = slice(q * QUARTER, (q + 1) * QUARTER)
             plain_products(0, 0, banks[2 * q : 2 * q + 2], ingress[2][:, part], q * QUARTER, QUARTER)
         for q in range(2):
             part = slice(q * QUARTER, (q + 1) * QUARTER)
-            plain_reading(0, 0, banks[2 * q : 2 * q + 2], ingress[2][:, part], drained[2][:, part], q * QUARTER, QUARTER)
+            first_difference(banks[2 * q : 2 * q + 2], ingress[2][:, part], drained[2][:, part], QUARTER)
+        nc.scalar.activation(readings[0][:, 0:QUARTER], drained[2][:, 0:QUARTER], ACT.Abs)
         for page in pages:
             nc.vector.memset(page[:].bitcast(I32), 0)
         plain_products(0, 1, banks[4:6], ingress[3][:])
         scatter(0, 0, QUARTER, slot_weights[:, 0:QUARTER])
         quantize_win(1, win_bf[1][:])
-        plain_reading(0, 1, banks[4:6], ingress[3][:], drained[3][:])
-        scatter(0, QUARTER, QUARTER, slot_weights[:, QUARTER:BANK])
+        nc.scalar.activation(second_quarter[:], drained[2][:, QUARTER:BANK], ACT.Abs)
+        first_difference(banks[4:6], ingress[3][:], win_bf[1][:].bitcast(F32), BANK)
+        scatter(0, QUARTER, QUARTER, slot_weights[:, QUARTER:BANK], second_quarter[:])
+        quantize_win(2, win_bf[0][:])
+        nc.scalar.activation(readings[0][:, halves(1)], win_bf[1][:].bitcast(F32), ACT.Abs)
         scatter(0, BANK, BANK, slot_weights[:, halves(1)])
         nc.tensor.transpose(banks[7][:, 0:P], vectors[:], identity[:])
         nc.scalar.activation(minus_drain[:], banks[7][:, 0:ROW_TILES], ACT.Copy, scale=-1.0)
@@ -383,7 +384,6 @@ def tile_list_router_queue_alarms_kernel(
             )
             quantize_z(0, q, z_bf[q][:])
 
-        quantize_win(2, win_bf[0][:])
         turned_products(1)
         poll(0, 0, M, polled[0][:], baseline[0])
         turned_difference(1)

@@ -89,7 +89,7 @@ def tile_list_router_queue_alarms_kernel(
         ]
         late_win_bf = [
             placed(f"late_win_bf{v}", K_PASSES * PASS, BF16, WIN_RAW_AT + 8 * KIB + 2 * KIB * v)
-            for v in range(TILES_PER_PASS)
+            for v in range(2)
         ]
         second_quarter = placed("second_quarter", QUARTER, F32, WIN_RAW_AT + 6 * KIB)
         woven_weights = placed("woven_weights", PACK * S, F32, WIN_RAW_AT)
@@ -136,7 +136,11 @@ def tile_list_router_queue_alarms_kernel(
         nc.vector.memset(weg_sc[1][:].bitcast(I32), 0)
         nc.vector.memset(vectors[:], 0.0)
         nc.vector.memset(wal_sc[:].bitcast(I32), 0)
+        for page in pages[:2]:
+            nc.vector.memset(page[:].bitcast(I32), 0)
         make_identity(nc, identity[:])
+        for page in pages[2:]:
+            nc.gpsimd.memset(page[:].bitcast(I32), 0)
 
         def load_scales(scale_tile, scales):
             for quad in range(QUADS):
@@ -293,17 +297,15 @@ def tile_list_router_queue_alarms_kernel(
         for q in range(2):
             part = slice(q * QUARTER, (q + 1) * QUARTER)
             first_difference(banks[2 * q : 2 * q + 2], ingress[2][:, part], drained[2][:, part], QUARTER)
-        nc.scalar.activation(readings[0][:, 0:QUARTER], drained[2][:, 0:QUARTER], ACT.Abs)
-        for page in pages:
-            nc.vector.memset(page[:].bitcast(I32), 0)
+        nc.scalar.activation(drained[3][:, 0:QUARTER], drained[2][:, 0:QUARTER], ACT.Abs)
         plain_products(0, 1, banks[4:6], ingress[3][:])
-        scatter(0, 0, QUARTER, slot_weights[:, 0:QUARTER])
+        scatter(0, 0, QUARTER, slot_weights[:, 0:QUARTER], drained[3][:, 0:QUARTER])
         quantize_win(1, win_bf[1][:])
         nc.scalar.activation(second_quarter[:], drained[2][:, QUARTER:BANK], ACT.Abs)
-        first_difference(banks[4:6], ingress[3][:], win_bf[1][:].bitcast(F32), BANK)
+        first_difference(banks[4:6], ingress[3][:], drained[3][:], BANK)
         scatter(0, QUARTER, QUARTER, slot_weights[:, QUARTER:BANK], second_quarter[:])
         quantize_win(2, win_bf[0][:])
-        nc.scalar.activation(readings[0][:, halves(1)], win_bf[1][:].bitcast(F32), ACT.Abs)
+        nc.scalar.activation(readings[0][:, halves(1)], drained[3][:], ACT.Abs)
         scatter(0, BANK, BANK, slot_weights[:, halves(1)])
         nc.tensor.transpose(banks[7][:, 0:P], vectors[:], identity[:])
         nc.scalar.activation(minus_drain[:], banks[7][:, 0:ROW_TILES], ACT.Copy, scale=-1.0)
@@ -390,12 +392,12 @@ def tile_list_router_queue_alarms_kernel(
         turned_reading(1)
         quantize_win(3, win_bf[1][:])
         for v in (0, 1):
-            quantize_win(TILES_PER_PASS + v, late_win_bf[v][:])
+            quantize_win(TILES_PER_PASS + v, turned[2 + v][:].bitcast(BF16))
         turned_products(2)
         turned_difference(2)
         turned_reading(2)
         for v in (2, 3):
-            quantize_win(TILES_PER_PASS + v, late_win_bf[v][:])
+            quantize_win(TILES_PER_PASS + v, late_win_bf[v - 2][:])
         for quad in range(QUADS):
             nc.sync.dma_start(
                 out=woven_weights[QUAD * quad : QUAD * (quad + 1), :], in_=wgs.rearrange("(p t) j -> p (t j)", t=PACK)

@@ -34,7 +34,7 @@ QUARTERS = M // QUARTER
 WIN_CHUNKS = ((0, 1), (1, 2), (2, 4), (4, 6), (6, 8))
 WEG_CHUNKS = ((0, 2), (2, 8))
 POLL_CHUNKS = ((0, 256), (256, 256), (512, 256), (768, 128), (896, 128))
-EMPTIED_BY_VECTOR = ((2, 1), (4, 1))
+EMPTIED_BY_VECTOR = ((3, 0), (4, 1))
 PASS_SHIFT = 16
 MOVED_ROWS = P - PASS_SHIFT
 
@@ -87,16 +87,12 @@ def tile_list_router_queue_alarms_kernel(
             ]
             for lo, hi in WIN_CHUNKS
         ]
-        late_win_bf = [
-            placed(f"late_win_bf{v}", K_PASSES * PASS, BF16, WIN_RAW_AT + 8 * KIB + 2 * KIB * v)
-            for v in range(2)
-        ]
         second_quarter = placed("second_quarter", QUARTER, F32, WIN_RAW_AT + 6 * KIB)
         woven_weights = placed("woven_weights", PACK * S, F32, WIN_RAW_AT)
         landing = [
             placed(f"landing{first}", PACK * count, F32, WIN_RAW_AT + 4 * PACK * first) for first, count in POLL_CHUNKS
         ]
-        win_bf = tiles("win_bf", 2, K_PASSES * PASS, BF16)
+        win_bf = sbuf("win_bf", K_PASSES * PASS, BF16)
         win_codes = [placed(f"win_codes{u}", K_PASSES * P, U32, TABLE_AT[0] + 8 * KIB + KIB * u) if u > 0 else sbuf("win_codes0", K_PASSES * P, U32) for u in range(ROW_TILES)]
         win_scales = tiles("win_scales", ROW_TILES, K_PASSES * P, U8)
         weg_codes = [sbuf(f"weg_codes{lo}", K_PASSES * 2 * P * (hi - lo), U8) for lo, hi in WEG_CHUNKS]
@@ -136,11 +132,9 @@ def tile_list_router_queue_alarms_kernel(
         nc.vector.memset(weg_sc[1][:].bitcast(I32), 0)
         nc.vector.memset(vectors[:], 0.0)
         nc.vector.memset(wal_sc[:].bitcast(I32), 0)
-        for page in pages[:2]:
+        for page in pages:
             nc.vector.memset(page[:].bitcast(I32), 0)
         make_identity(nc, identity[:])
-        for page in pages[2:]:
-            nc.gpsimd.memset(page[:].bitcast(I32), 0)
 
         def load_scales(scale_tile, scales):
             for quad in range(QUADS):
@@ -194,8 +188,8 @@ def tile_list_router_queue_alarms_kernel(
         load_win(1)
         nc.sync.dma_start(out=vectors[0:ROW_TILES, :], in_=drain.rearrange("(u p) -> u p", p=P))
         nc.sync.dma_start(out=vectors[ROW_TILES : ROW_TILES + N_TILES, :], in_=bias.rearrange("(c p) -> c p", p=P))
-        load_win(2)
         nc.sync.dma_start(out=slot_weights[:, QUARTER:S], in_=wgs[:, QUARTER:S])
+        load_win(2)
         load_base(0)
         load_weg(1)
         load_weg_scales(1)
@@ -280,7 +274,7 @@ def tile_list_router_queue_alarms_kernel(
             out=picked_scales[1][0:MOVED_ROWS, :].bitcast(I32), in_=picked_scales[0][PASS_SHIFT:P, :].bitcast(I32)
         )
         gather_words(0, 1)
-        quantize_win(0, win_bf[0][:])
+        quantize_win(0, win_bf[:])
         for half in range(HALVES):
             gather_words(1, half)
 
@@ -288,43 +282,44 @@ def tile_list_router_queue_alarms_kernel(
             project(u, half, pair, at, count)
             nc.scalar.copy(staged, pair[0][:, 0:count])
 
-        def first_difference(pair, staged, difference, count):
-            nc.vector.scalar_tensor_tensor(difference, pair[1][:, 0:count], minus_first_drain[:], staged, ALU.mult, ALU.add)
+        def vector_difference(pair, staged, difference, count, minus_rate):
+            nc.vector.scalar_tensor_tensor(difference, pair[1][:, 0:count], minus_rate, staged, ALU.mult, ALU.add)
 
         for q in range(2):
             part = slice(q * QUARTER, (q + 1) * QUARTER)
             plain_products(0, 0, banks[2 * q : 2 * q + 2], ingress[2][:, part], q * QUARTER, QUARTER)
-        for q in range(2):
-            part = slice(q * QUARTER, (q + 1) * QUARTER)
-            first_difference(banks[2 * q : 2 * q + 2], ingress[2][:, part], drained[2][:, part], QUARTER)
-        nc.scalar.activation(drained[3][:, 0:QUARTER], drained[2][:, 0:QUARTER], ACT.Abs)
+        vector_difference(banks[0:2], ingress[2][:, 0:QUARTER], ingress[3][:, 0:QUARTER], QUARTER, minus_first_drain[:])
+        vector_difference(banks[2:4], ingress[2][:, QUARTER:BANK], drained[2][:, 0:QUARTER], QUARTER, minus_first_drain[:])
+        nc.scalar.activation(drained[3][:, 0:QUARTER], ingress[3][:, 0:QUARTER], ACT.Abs)
         plain_products(0, 1, banks[4:6], ingress[3][:])
         scatter(0, 0, QUARTER, slot_weights[:, 0:QUARTER], drained[3][:, 0:QUARTER])
-        quantize_win(1, win_bf[1][:])
-        nc.scalar.activation(second_quarter[:], drained[2][:, QUARTER:BANK], ACT.Abs)
-        first_difference(banks[4:6], ingress[3][:], drained[3][:], BANK)
+        quantize_win(1, ingress[2][:].bitcast(BF16))
+        nc.scalar.activation(second_quarter[:], drained[2][:, 0:QUARTER], ACT.Abs)
+        vector_difference(banks[4:6], ingress[3][:], drained[3][:], BANK, minus_first_drain[:])
         scatter(0, QUARTER, QUARTER, slot_weights[:, QUARTER:BANK], second_quarter[:])
-        quantize_win(2, win_bf[0][:])
+        nc.tensor.transpose(banks[1][:, 0:P], vectors[:], identity[:])
+        nc.scalar.activation(minus_drain[:], banks[1][:, 0:ROW_TILES], ACT.Copy, scale=-1.0)
+        nc.scalar.copy(bias_col[:], banks[1][:, ROW_TILES : ROW_TILES + N_TILES])
+        quantize_win(2, drained[2][:].bitcast(BF16))
         nc.scalar.activation(readings[0][:, halves(1)], drained[3][:], ACT.Abs)
         scatter(0, BANK, BANK, slot_weights[:, halves(1)])
-        nc.tensor.transpose(banks[7][:, 0:P], vectors[:], identity[:])
-        nc.scalar.activation(minus_drain[:], banks[7][:, 0:ROW_TILES], ACT.Copy, scale=-1.0)
-        nc.scalar.copy(bias_col[:], banks[7][:, ROW_TILES : ROW_TILES + N_TILES])
 
-        def staged_products(u, half, pair, slot):
+        def staged_products(u, half, pair, slot, staged):
             project(u, half, pair)
-            nc.scalar.copy(ingress[slot][:], pair[0][:])
+            nc.scalar.copy(staged, pair[0][:])
             nc.scalar.activation(drained[slot][:], pair[1][:], ACT.Copy, scale=minus_drain[:, u : u + 1])
+
+        turned_ingress = {2: [z_bf[half][:].bitcast(F32) for half in range(HALVES)], 3: [ingress[2][:], ingress[3][:]]}
 
         def turned_products(u):
             for half in range(HALVES):
-                staged_products(u, half, banks[2 * half : 2 * half + 2], 2 * (u % 2) + half)
+                staged_products(u, half, banks[2 * half : 2 * half + 2], 2 * (u % 2) + half, turned_ingress[u][half])
 
         def turned_difference(u):
             for half in range(HALVES):
                 slot, bank = 2 * (u % 2) + half, banks[4 + half]
                 for c in range(BANK // P):
-                    for term, staged in enumerate((ingress[slot], drained[slot])):
+                    for term, staged in enumerate((turned_ingress[u][half], drained[slot][:])):
                         nc.tensor.matmul(
                             bank[:, columns(c)], staged[:, columns(c)], identity[:],
                             start=term == 0, stop=term == 1, is_transpose=True,
@@ -337,14 +332,11 @@ def tile_list_router_queue_alarms_kernel(
                 for c in range(BANK // P):
                     nc.tensor.transpose(bank[:, columns(c)], turned[slot][:, columns(c)], identity[:])
                 nc.scalar.copy(readings[u][:, halves(half)], bank[:])
-                if u == 1:
-                    scatter(u, half * BANK, BANK, slot_weights[:, halves(half)])
-            if u > 1:
-                scatter(u, 0, S, slot_weights[:])
+            scatter(u, 0, S, slot_weights[:])
             poll(u, 0, M, polled[u][:], baseline[u])
 
         def woven_products(half, v):
-            staged_products(TILES_PER_PASS + v, half, banks[2 * (v % 2) : 2 * (v % 2) + 2], v)
+            staged_products(TILES_PER_PASS + v, half, banks[2 * (v % 2) : 2 * (v % 2) + 2], v, ingress[v][:])
 
         def woven_difference(c):
             bank = banks[4 + c % 2]
@@ -386,18 +378,23 @@ def tile_list_router_queue_alarms_kernel(
             )
             quantize_z(0, q, z_bf[q][:])
 
-        turned_products(1)
+        tile1_pairs = (banks[6:8], banks[4:6])
+        for half in range(HALVES):
+            plain_products(1, half, tile1_pairs[half], polled[0][:, halves(half)])
+        quantize_win(3, drained[3][:].bitcast(BF16))
+        for half in range(HALVES):
+            vector_difference(tile1_pairs[half], polled[0][:, halves(half)], polled[1][:, halves(half)], BANK, minus_drain[:, 1:2])
+            nc.scalar.activation(readings[1][:, halves(half)], polled[1][:, halves(half)], ACT.Abs)
         poll(0, 0, M, polled[0][:], baseline[0])
-        turned_difference(1)
-        turned_reading(1)
-        quantize_win(3, win_bf[1][:])
-        for v in (0, 1):
-            quantize_win(TILES_PER_PASS + v, turned[2 + v][:].bitcast(BF16))
+        scatter(1, 0, S, slot_weights[:])
         turned_products(2)
+        for v in (0, 1):
+            quantize_win(TILES_PER_PASS + v, polled[1][:, halves(v)].bitcast(BF16))
+        poll(1, 0, M, polled[1][:], baseline[1])
         turned_difference(2)
-        turned_reading(2)
         for v in (2, 3):
-            quantize_win(TILES_PER_PASS + v, late_win_bf[v - 2][:])
+            quantize_win(TILES_PER_PASS + v, z_bf[v - 2][:])
+        turned_reading(2)
         for quad in range(QUADS):
             nc.sync.dma_start(
                 out=woven_weights[QUAD * quad : QUAD * (quad + 1), :], in_=wgs.rearrange("(p t) j -> p (t j)", t=PACK)
@@ -479,6 +476,9 @@ def tile_list_router_queue_alarms_kernel(
             else:
                 nc.scalar.activation(dst, src, ACT.Copy, scale=-1.0)
             quantize_z(1, i, woven_bf[i])
-            finish(i)
+            if i < last - 1:
+                finish(i)
             if i == 0:
                 alarm_pass(0, last, range(2, 4))
+        finish(last - 1)
+        finish(last)

@@ -304,44 +304,50 @@ def tile_list_router_queue_alarms_kernel(
         nc.scalar.activation(readings[0][:, halves(1)], drained[3][:], ACT.Abs)
         scatter(0, BANK, BANK, slot_weights[:, halves(1)])
 
-        def staged_products(u, half, pair, slot, staged):
+        def staged_products(u, half, pair, staged, staged_drain):
             project(u, half, pair)
             nc.scalar.copy(staged, pair[0][:])
-            nc.scalar.activation(drained[slot][:], pair[1][:], ACT.Copy, scale=minus_drain[:, u : u + 1])
+            nc.scalar.activation(staged_drain, pair[1][:], ACT.Copy, scale=minus_drain[:, u : u + 1])
 
-        turned_ingress = {2: [z_bf[half][:].bitcast(F32) for half in range(HALVES)], 3: [ingress[2][:], ingress[3][:]]}
+        turned_ingress = {1: [ingress[0][:], ingress[1][:]], 2: [z_bf[half][:].bitcast(F32) for half in range(HALVES)], 3: [ingress[0][:], ingress[1][:]]}
+        turned_drained = {1: drained[0:2], 2: drained[2:4], 3: drained[0:2]}
+        turned_abs = {1: [polled[1][:, halves(half)] for half in range(HALVES)], 2: [turned[2][:], turned[3][:]], 3: [turned[0][:], turned[1][:]]}
 
-        def turned_products(u):
-            for half in range(HALVES):
-                staged_products(u, half, banks[2 * half : 2 * half + 2], 2 * (u % 2) + half, turned_ingress[u][half])
+        def turned_products(u, which=range(HALVES)):
+            for half in which:
+                pair = banks[0:2] if u == 1 else banks[2 * half : 2 * half + 2]
+                staged_products(u, half, pair, turned_ingress[u][half], turned_drained[u][half][:])
 
-        def turned_difference(u):
-            for half in range(HALVES):
-                slot, bank = 2 * (u % 2) + half, banks[4 + half]
+        def turned_difference(u, which=range(HALVES)):
+            for half in which:
+                bank = banks[4 + half]
                 for c in range(BANK // P):
-                    for term, staged in enumerate((turned_ingress[u][half], drained[slot][:])):
+                    for term, staged in enumerate((turned_ingress[u][half], turned_drained[u][half][:])):
                         nc.tensor.matmul(
                             bank[:, columns(c)], staged[:, columns(c)], identity[:],
                             start=term == 0, stop=term == 1, is_transpose=True,
                         )
-                nc.scalar.activation(turned[slot][:], bank[:], ACT.Abs)
+                nc.scalar.activation(turned_abs[u][half], bank[:], ACT.Abs)
 
-        def turned_reading(u):
-            for half in range(HALVES):
-                slot, bank = 2 * (u % 2) + half, banks[6 + half]
+        def turned_reading(u, which=range(HALVES)):
+            for half in which:
+                bank = banks[(2 if u == 1 else 6) + half]
                 for c in range(BANK // P):
-                    nc.tensor.transpose(bank[:, columns(c)], turned[slot][:, columns(c)], identity[:])
+                    nc.tensor.transpose(bank[:, columns(c)], turned_abs[u][half][:, columns(c)], identity[:])
                 nc.scalar.copy(readings[u][:, halves(half)], bank[:])
-            scatter(u, 0, S, slot_weights[:])
-            poll(u, 0, M, polled[u][:], baseline[u])
+                if u == 1:
+                    scatter(u, half * BANK, BANK, slot_weights[:, halves(half)])
+            if u > 1:
+                scatter(u, 0, S, slot_weights[:])
+                poll(u, 0, M, polled[u][:], baseline[u])
 
         def woven_products(half, v):
-            staged_products(TILES_PER_PASS + v, half, banks[2 * (v % 2) : 2 * (v % 2) + 2], v, ingress[v][:])
+            staged_products(TILES_PER_PASS + v, half, banks[2 * (v % 2) : 2 * (v % 2) + 2], ingress[(v + 2) % 4][:], drained[(v + 2) % 4][:])
 
         def woven_difference(c):
             bank = banks[4 + c % 2]
             for v in range(TILES_PER_PASS):
-                for term, staged in enumerate((ingress[v], drained[v])):
+                for term, staged in enumerate((ingress[(v + 2) % 4], drained[(v + 2) % 4])):
                     nc.tensor.matmul(
                         bank[:, columns(v)], staged[:, columns(c)], identity[:],
                         start=term == 0, stop=term == 1, is_transpose=True,
@@ -378,15 +384,14 @@ def tile_list_router_queue_alarms_kernel(
             )
             quantize_z(0, q, z_bf[q][:])
 
-        tile1_pairs = (banks[6:8], banks[4:6])
-        for half in range(HALVES):
-            plain_products(1, half, tile1_pairs[half], polled[0][:, halves(half)])
+        turned_products(1, [0])
+        turned_difference(1, [0])
+        turned_products(1, [1])
         quantize_win(3, drained[3][:].bitcast(BF16))
-        for half in range(HALVES):
-            vector_difference(tile1_pairs[half], polled[0][:, halves(half)], polled[1][:, halves(half)], BANK, minus_drain[:, 1:2])
-            nc.scalar.activation(readings[1][:, halves(half)], polled[1][:, halves(half)], ACT.Abs)
         poll(0, 0, M, polled[0][:], baseline[0])
-        scatter(1, 0, S, slot_weights[:])
+        turned_reading(1, [0])
+        turned_difference(1, [1])
+        turned_reading(1, [1])
         turned_products(2)
         for v in (0, 1):
             quantize_win(TILES_PER_PASS + v, polled[1][:, halves(v)].bitcast(BF16))

@@ -31,6 +31,9 @@ HALVES = S // BANK
 PER_COLUMN = 16
 QUARTER = 256
 QUARTERS = M // QUARTER
+LINE = 4
+SLOTS = 4
+FIRST_PASS_PARTS = 4
 WIN_CHUNKS = ((0, 1), (1, 2), (2, 4), (4, 6), (6, 8))
 WEG_CHUNKS = ((0, 2), (2, 8))
 POLL_CHUNKS = ((0, 256), (256, 256), (512, 256), (768, 128), (896, 128))
@@ -40,6 +43,7 @@ MOVED_ROWS = P - PASS_SHIFT
 
 KIB = 1024
 TABLE_AT = (0, 16 * KIB)
+WIN_CODES_AT = 8 * KIB
 TABLE_SCALES_AT = 32 * KIB
 WIN_RAW_AT = 40 * KIB
 READINGS_AT = 56 * KIB
@@ -78,22 +82,27 @@ def tile_list_router_queue_alarms_kernel(
         ]
         picked_scales = tiles("picked_scales", K_PASSES, S, U8)
 
+        def win_raw_at(lo, hi, a):
+            return WIN_RAW_AT + 4 * PASS * (K_PASSES * lo + a * (hi - lo))
+
         win_raw = [
             [
-                placed(f"win_raw{lo}_{a}", PASS * (hi - lo), F32, WIN_RAW_AT + 4 * PASS * (K_PASSES * lo + a * (hi - lo)))
+                placed(f"win_raw{lo}_{a}", PASS * (hi - lo), F32, win_raw_at(lo, hi, a))
                 if hi <= TILES_PER_PASS
                 else sbuf(f"win_raw{lo}_{a}", PASS * (hi - lo), F32)
                 for a in range(K_PASSES)
             ]
             for lo, hi in WIN_CHUNKS
         ]
-        second_quarter = placed("second_quarter", QUARTER, F32, WIN_RAW_AT + 6 * KIB)
+        second_quarter = placed("second_quarter", QUARTER, F32, win_raw_at(*WIN_CHUNKS[1], K_PASSES - 1))
         woven_weights = placed("woven_weights", PACK * S, F32, WIN_RAW_AT)
         landing = [
             placed(f"landing{first}", PACK * count, F32, WIN_RAW_AT + 4 * PACK * first) for first, count in POLL_CHUNKS
         ]
         win_bf = sbuf("win_bf", K_PASSES * PASS, BF16)
-        win_codes = [placed(f"win_codes{u}", K_PASSES * P, U32, TABLE_AT[0] + 8 * KIB + KIB * u) if u > 0 else sbuf("win_codes0", K_PASSES * P, U32) for u in range(ROW_TILES)]
+        win_codes = [sbuf("win_codes0", K_PASSES * P, U32)] + [
+            placed(f"win_codes{u}", K_PASSES * P, U32, WIN_CODES_AT + KIB * u) for u in range(1, ROW_TILES)
+        ]
         win_scales = tiles("win_scales", ROW_TILES, K_PASSES * P, U8)
         weg_codes = [sbuf(f"weg_codes{lo}", K_PASSES * 2 * P * (hi - lo), U8) for lo, hi in WEG_CHUNKS]
         weg_sc = [sbuf(f"weg_sc{lo}", K_PASSES * P * (hi - lo), U8) for lo, hi in WEG_CHUNKS]
@@ -104,21 +113,23 @@ def tile_list_router_queue_alarms_kernel(
         woven_baseline = [placed(f"woven_baseline{t}", M, F32, TABLE_AT[1] + 4 * M * t) for t in range(PACK)]
         pages = tiles("page", PACK, T2, F32)
         readings = [placed(f"readings{t}", S, F32, READINGS_AT + 4 * S * t) for t in range(PACK)]
+        spare_reading = sbuf("spare_reading", BANK, F32)
         polled = tiles("polled", TILES_PER_PASS, M, F32)
-        ingress = tiles("ingress", TILES_PER_PASS, BANK, F32)
-        drained = tiles("drained", TILES_PER_PASS, BANK, F32)
+        ingress = tiles("ingress", SLOTS, BANK, F32)
+        drained = tiles("drained", SLOTS, BANK, F32)
         turned = tiles("turned", BANK // P, BANK, F32)
         z_rows = tiles("z_rows", 4, PASS, BF16)
         z_bf = tiles("z_bf", QUARTERS, QUARTER * PACK, BF16)
         z_codes = [
-            [placed(f"z_codes0_{q}", QUARTER, U32, READINGS_AT + 4 * S * q) for q in range(QUARTERS)],
+            [sbuf("z_codes0_0", QUARTER, U32)]
+            + [placed(f"z_codes0_{q}", QUARTER, U32, READINGS_AT + 4 * S * (q - 1)) for q in range(1, QUARTERS)],
             [sbuf(f"z_codes1_{first}", count, U32) for first, count in POLL_CHUNKS],
         ]
         z_scales = [
             tiles("z_scales0_", QUARTERS, QUARTER, U8),
             [sbuf(f"z_scales1_{first}", count, U8) for first, count in POLL_CHUNKS],
         ]
-        results = [placed(f"result{i}", BANK, F32, TABLE_AT[0] + 4 * BANK * i) for i in range(8)]
+        results = [placed(f"result{i}", BANK, F32, TABLE_AT[0] + 4 * BANK * i) for i in range(len(banks))]
         vectors = sbuf("vectors", P, F32)
         first_drain = sbuf("first_drain", 1, F32)
         minus_first_drain = sbuf("minus_first_drain", 1, F32)
@@ -173,8 +184,8 @@ def tile_list_router_queue_alarms_kernel(
         nc.sync.dma_start(idx3[:], offs3)
         load_weg(0)
         nc.sync.dma_start(out=first_drain[:], in_=drain[0:P].rearrange("(p o) -> p o", o=1))
-        for part in range(4):
-            load_table(0, slice(part * T // 4, (part + 1) * T // 4))
+        for part in range(FIRST_PASS_PARTS):
+            load_table(0, slice(part * T // FIRST_PASS_PARTS, (part + 1) * T // FIRST_PASS_PARTS))
         for r in range(4):
             nc.sync.dma_start(
                 out=table_scales[r:P:PASS_SHIFT, :].bitcast(I32),
@@ -218,10 +229,11 @@ def tile_list_router_queue_alarms_kernel(
         def quantize_win(u, staged):
             chunk = chunk_of(WIN_CHUNKS, u)
             first = (u - WIN_CHUNKS[chunk][0]) * P
+            lines = slice(first // LINE, (first + P) // LINE)
             for a in range(K_PASSES):
                 nc.scalar.copy(
-                    staged[:, a * PASS : (a + 1) * PASS].rearrange("p (c e i) -> p c i e", i=PACK, e=4),
-                    win_raw[chunk][a][:].rearrange("p (i c e) -> p c i e", i=PACK, e=4)[:, first // 4 : (first + P) // 4, :, :],
+                    staged[:, a * PASS : (a + 1) * PASS].rearrange("p (c e i) -> p c i e", i=PACK, e=LINE),
+                    win_raw[chunk][a][:].rearrange("p (i c e) -> p c i e", i=PACK, e=LINE)[:, lines, :, :],
                 )
             nc.vector.quantize_mx(out=win_codes[u][:].bitcast(FP8X4), scales=win_scales[u][:], in_=staged)
 
@@ -255,8 +267,7 @@ def tile_list_router_queue_alarms_kernel(
                         stop=a == K_PASSES - 1 and lo_port + width == count,
                     )
 
-        def scatter(t, first, count, weights, values=None):
-            values = readings[t][:, first : first + count] if values is None else values
+        def scatter(t, first, count, values, weights):
             nc.vector.tensor_tensor(pages[t][:].indirect(entries(idx2, first, count)), values, weights, ALU.mult)
 
         def poll(t, first, count, dst, base_rows):
@@ -278,100 +289,116 @@ def tile_list_router_queue_alarms_kernel(
         for half in range(HALVES):
             gather_words(1, half)
 
-        def plain_products(u, half, pair, staged, at=0, count=BANK):
-            project(u, half, pair, at, count)
+        def first_products(half, pair, staged, at, count):
+            project(0, half, pair, at, count)
             nc.scalar.copy(staged, pair[0][:, 0:count])
 
-        def vector_difference(pair, staged, difference, count, minus_rate):
-            nc.vector.scalar_tensor_tensor(difference, pair[1][:, 0:count], minus_rate, staged, ALU.mult, ALU.add)
+        def first_difference(pair, staged, difference, count):
+            nc.vector.scalar_tensor_tensor(difference, pair[1][:, 0:count], minus_first_drain[:], staged, ALU.mult, ALU.add)
 
-        for q in range(2):
-            part = slice(q * QUARTER, (q + 1) * QUARTER)
-            plain_products(0, 0, banks[2 * q : 2 * q + 2], ingress[2][:, part], q * QUARTER, QUARTER)
-        vector_difference(banks[0:2], ingress[2][:, 0:QUARTER], ingress[3][:, 0:QUARTER], QUARTER, minus_first_drain[:])
-        vector_difference(banks[2:4], ingress[2][:, QUARTER:BANK], drained[2][:, 0:QUARTER], QUARTER, minus_first_drain[:])
-        nc.scalar.activation(drained[3][:, 0:QUARTER], ingress[3][:, 0:QUARTER], ACT.Abs)
-        plain_products(0, 1, banks[4:6], ingress[3][:])
-        scatter(0, 0, QUARTER, slot_weights[:, 0:QUARTER], drained[3][:, 0:QUARTER])
+        low, high = slice(0, QUARTER), slice(QUARTER, BANK)
+        first_products(0, banks[0:2], ingress[2][:, low], 0, QUARTER)
+        first_products(0, banks[2:4], ingress[2][:, high], QUARTER, QUARTER)
+        first_difference(banks[0:2], ingress[2][:, low], ingress[3][:, low], QUARTER)
+        first_difference(banks[2:4], ingress[2][:, high], drained[2][:, low], QUARTER)
+        nc.scalar.activation(drained[3][:, low], ingress[3][:, low], ACT.Abs)
+        first_products(1, banks[4:6], ingress[3][:], 0, BANK)
+        scatter(0, 0, QUARTER, drained[3][:, low], slot_weights[:, low])
         quantize_win(1, ingress[2][:].bitcast(BF16))
-        nc.scalar.activation(second_quarter[:], drained[2][:, 0:QUARTER], ACT.Abs)
-        vector_difference(banks[4:6], ingress[3][:], drained[3][:], BANK, minus_first_drain[:])
-        scatter(0, QUARTER, QUARTER, slot_weights[:, QUARTER:BANK], second_quarter[:])
+        nc.scalar.activation(second_quarter[:], drained[2][:, low], ACT.Abs)
+        first_difference(banks[4:6], ingress[3][:], drained[3][:], BANK)
+        scatter(0, QUARTER, QUARTER, second_quarter[:], slot_weights[:, high])
         nc.tensor.transpose(banks[1][:, 0:P], vectors[:], identity[:])
         nc.scalar.activation(minus_drain[:], banks[1][:, 0:ROW_TILES], ACT.Copy, scale=-1.0)
         nc.scalar.copy(bias_col[:], banks[1][:, ROW_TILES : ROW_TILES + N_TILES])
         quantize_win(2, drained[2][:].bitcast(BF16))
         nc.scalar.activation(readings[0][:, halves(1)], drained[3][:], ACT.Abs)
-        scatter(0, BANK, BANK, slot_weights[:, halves(1)])
+        scatter(0, BANK, BANK, readings[0][:, halves(1)], slot_weights[:, halves(1)])
 
-        def staged_products(u, half, pair, staged, staged_drain):
+        def staged_products(u, half, pair, staged_ingress, staged_drained):
             project(u, half, pair)
-            nc.scalar.copy(staged, pair[0][:])
-            nc.scalar.activation(staged_drain, pair[1][:], ACT.Copy, scale=minus_drain[:, u : u + 1])
+            nc.scalar.copy(staged_ingress, pair[0][:])
+            nc.scalar.activation(staged_drained, pair[1][:], ACT.Copy, scale=minus_drain[:, u : u + 1])
 
-        turned_ingress = {1: [ingress[0][:], ingress[1][:]], 2: [z_bf[half][:].bitcast(F32) for half in range(HALVES)], 3: [ingress[0][:], ingress[1][:]]}
-        turned_drained = {1: drained[0:2], 2: drained[2:4], 3: drained[0:2]}
-        turned_abs = {1: [polled[1][:, halves(half)] for half in range(HALVES)], 2: [turned[2][:], turned[3][:]], 3: [turned[0][:], turned[1][:]]}
+        def add_turned(dst, staged_ingress, staged_drained):
+            for term, staged in enumerate((staged_ingress, staged_drained)):
+                nc.tensor.matmul(dst, staged, identity[:], start=term == 0, stop=term == 1, is_transpose=True)
 
-        def turned_products(u, which=range(HALVES)):
-            for half in which:
-                pair = banks[0:2] if u == 1 else banks[2 * half : 2 * half + 2]
-                staged_products(u, half, pair, turned_ingress[u][half], turned_drained[u][half][:])
+        plain_ingress = {
+            1: [ingress[0][:], ingress[1][:]],
+            2: [z_bf[half][:].bitcast(F32) for half in range(HALVES)],
+            3: [ingress[0][:], ingress[1][:]],
+        }
+        plain_drained = {1: drained[0:2], 2: drained[2:4], 3: drained[0:2]}
+        plain_turned = {
+            1: [polled[1][:, halves(half)] for half in range(HALVES)],
+            2: [turned[2][:], turned[3][:]],
+            3: [turned[0][:], turned[1][:]],
+        }
+        product_banks = {1: (banks[0:2], banks[0:2]), 2: (banks[0:2], banks[2:4]), 3: (banks[0:2], banks[2:4])}
+        difference_banks = banks[4:6]
+        return_banks = {1: banks[2:4], 2: banks[6:8], 3: banks[6:8]}
 
-        def turned_difference(u, which=range(HALVES)):
-            for half in which:
-                bank = banks[4 + half]
-                for c in range(BANK // P):
-                    for term, staged in enumerate((turned_ingress[u][half], turned_drained[u][half][:])):
-                        nc.tensor.matmul(
-                            bank[:, columns(c)], staged[:, columns(c)], identity[:],
-                            start=term == 0, stop=term == 1, is_transpose=True,
-                        )
-                nc.scalar.activation(turned_abs[u][half], bank[:], ACT.Abs)
+        def plain_products(u, half):
+            staged_products(u, half, product_banks[u][half], plain_ingress[u][half], plain_drained[u][half][:])
 
-        def turned_reading(u, which=range(HALVES)):
-            for half in which:
-                bank = banks[(2 if u == 1 else 6) + half]
-                for c in range(BANK // P):
-                    nc.tensor.transpose(bank[:, columns(c)], turned_abs[u][half][:, columns(c)], identity[:])
-                nc.scalar.copy(readings[u][:, halves(half)], bank[:])
-                if u == 1:
-                    scatter(u, half * BANK, BANK, slot_weights[:, halves(half)])
-            if u > 1:
-                scatter(u, 0, S, slot_weights[:])
-                poll(u, 0, M, polled[u][:], baseline[u])
+        def plain_difference(u, half):
+            bank = difference_banks[half]
+            for c in range(BANK // P):
+                add_turned(bank[:, columns(c)], plain_ingress[u][half][:, columns(c)], plain_drained[u][half][:, columns(c)])
+            nc.scalar.activation(plain_turned[u][half], bank[:], ACT.Abs)
+
+        def plain_reading(u, half):
+            bank = return_banks[u][half]
+            for c in range(BANK // P):
+                nc.tensor.transpose(bank[:, columns(c)], plain_turned[u][half][:, columns(c)], identity[:])
+            nc.scalar.copy(readings[u][:, halves(half)], bank[:])
+
+        def both_halves(step, u):
+            for half in range(HALVES):
+                step(u, half)
+
+        def poll_plain(u):
+            poll(u, 0, M, polled[u][:], baseline[u])
+
+        def finish_plain(u):
+            both_halves(plain_reading, u)
+            scatter(u, 0, S, readings[u][:], slot_weights[:])
+            poll_plain(u)
+
+        def woven_slot(v):
+            return (v + 2) % SLOTS
 
         def woven_products(half, v):
-            staged_products(TILES_PER_PASS + v, half, banks[2 * (v % 2) : 2 * (v % 2) + 2], ingress[(v + 2) % 4][:], drained[(v + 2) % 4][:])
+            pair = banks[2 * (v % 2) : 2 * (v % 2) + 2]
+            staged_products(TILES_PER_PASS + v, half, pair, ingress[woven_slot(v)][:], drained[woven_slot(v)][:])
 
         def woven_difference(c):
-            bank = banks[4 + c % 2]
+            bank = difference_banks[c % 2]
             for v in range(TILES_PER_PASS):
-                for term, staged in enumerate((ingress[(v + 2) % 4], drained[(v + 2) % 4])):
-                    nc.tensor.matmul(
-                        bank[:, columns(v)], staged[:, columns(c)], identity[:],
-                        start=term == 0, stop=term == 1, is_transpose=True,
-                    )
+                add_turned(bank[:, columns(v)], ingress[woven_slot(v)][:, columns(c)], drained[woven_slot(v)][:, columns(c)])
             nc.scalar.activation(
                 turned[c][:].rearrange("j (t p) -> j t p", t=PACK), bank[:].rearrange("j (p t) -> j t p", t=PACK), ACT.Abs
             )
 
-        def woven_reading(half, t):
+        def woven_reading(half, t, at=0, count=BANK):
             bank = banks[6 + t % 2]
-            for c in range(BANK // P):
+            for c in range(at // P, (at + count) // P):
                 nc.tensor.transpose(bank[:, columns(c)], turned[c][:, columns(t)], identity[:])
-            nc.scalar.copy(readings[t][:, halves(half)], bank[:])
-            scatter(t, half * BANK, BANK, woven_weights[:, t * S + half * BANK : t * S + (half + 1) * BANK])
+            first = half * BANK + at
+            values = spare_reading[:] if (half, t) == (0, PACK - 1) else readings[t][:, first : first + count]
+            nc.scalar.copy(values, bank[:, at : at + count])
+            scatter(t, first, count, values, woven_weights[:, t * S + first : t * S + first + count])
 
         def turn_plain_z(q):
             word_bank = banks[6 + q % 2]
             rows = [z_rows[(2 * q + c) % len(z_rows)] for c in range(QUARTER // P)]
             for c in range(QUARTER // P):
                 for v in range(TILES_PER_PASS):
-                    nc.tensor.transpose(banks[4 + c][:, columns(v)], polled[v][:, columns(2 * q + c)], identity[:])
+                    nc.tensor.transpose(difference_banks[c][:, columns(v)], polled[v][:, columns(2 * q + c)], identity[:])
                 nc.scalar.activation(
                     rows[c][:].rearrange("m (w p e) -> m w p e", w=2, e=2),
-                    banks[4 + c][:].rearrange("m (p w e) -> m w p e", w=2, e=2),
+                    difference_banks[c][:].rearrange("m (p w e) -> m w p e", w=2, e=2),
                     ACT.Copy,
                     scale=-1.0,
                 )
@@ -384,39 +411,45 @@ def tile_list_router_queue_alarms_kernel(
             )
             quantize_z(0, q, z_bf[q][:])
 
-        turned_products(1, [0])
-        turned_difference(1, [0])
-        turned_products(1, [1])
+        plain_products(1, 0)
+        plain_difference(1, 0)
+        plain_products(1, 1)
         quantize_win(3, drained[3][:].bitcast(BF16))
-        poll(0, 0, M, polled[0][:], baseline[0])
-        turned_reading(1, [0])
-        turned_difference(1, [1])
-        turned_reading(1, [1])
-        turned_products(2)
+        poll_plain(0)
+        plain_reading(1, 0)
+        scatter(1, 0, BANK, readings[1][:, halves(0)], slot_weights[:, halves(0)])
+        plain_difference(1, 1)
+        plain_reading(1, 1)
+        scatter(1, BANK, BANK, readings[1][:, halves(1)], slot_weights[:, halves(1)])
+        both_halves(plain_products, 2)
         for v in (0, 1):
             quantize_win(TILES_PER_PASS + v, polled[1][:, halves(v)].bitcast(BF16))
-        poll(1, 0, M, polled[1][:], baseline[1])
-        turned_difference(2)
+        poll_plain(1)
+        both_halves(plain_difference, 2)
         for v in (2, 3):
             quantize_win(TILES_PER_PASS + v, z_bf[v - 2][:])
-        turned_reading(2)
+        finish_plain(2)
         for quad in range(QUADS):
             nc.sync.dma_start(
                 out=woven_weights[QUAD * quad : QUAD * (quad + 1), :], in_=wgs.rearrange("(p t) j -> p (t j)", t=PACK)
             )
         for t in range(PACK):
             nc.sync.dma_start(out=woven_baseline[t][:], in_=base[PASS:H, :].rearrange("(p t) m -> p t m", t=PACK)[:, t, :])
-        turned_products(3)
-        turned_difference(3)
+        both_halves(plain_products, 3)
+        both_halves(plain_difference, 3)
         for v in (0, 1):
             woven_products(0, v)
-        turned_reading(3)
+        finish_plain(3)
         for v in (2, 3):
             woven_products(0, v)
-        for c in range(BANK // P):
-            woven_difference(c)
+        for q in range(2):
+            for c in (2 * q, 2 * q + 1):
+                woven_difference(c)
+            for t in (0, 1):
+                woven_reading(0, t, q * QUARTER, QUARTER)
         for t in range(PACK):
-            woven_reading(0, t)
+            if t > 1:
+                woven_reading(0, t)
             woven_products(1, t)
         for c in range(BANK // P):
             woven_difference(c)
@@ -470,12 +503,12 @@ def tile_list_router_queue_alarms_kernel(
         last = len(POLL_CHUNKS) - 1
         for i in range(last):
             alarm_pass(0, i)
-        alarm_pass(0, last, range(0, 2))
+        alarm_pass(0, last, range(N_TILES // 2))
         for i, (first, count) in enumerate(POLL_CHUNKS):
             for t in range(PACK):
                 poll(t, first, count, landing[i][:, t * count : (t + 1) * count], woven_baseline[t])
-            dst = woven_bf[i].rearrange("p (c e t) -> p c t e", t=PACK, e=4)
-            src = landing[i][:].rearrange("p (t c e) -> p c t e", t=PACK, e=4)
+            dst = woven_bf[i].rearrange("p (c e t) -> p c t e", t=PACK, e=LINE)
+            src = landing[i][:].rearrange("p (t c e) -> p c t e", t=PACK, e=LINE)
             if count < QUARTER:
                 nc.vector.tensor_scalar_mul(dst, src, -1.0)
             else:
@@ -484,6 +517,6 @@ def tile_list_router_queue_alarms_kernel(
             if i < last - 1:
                 finish(i)
             if i == 0:
-                alarm_pass(0, last, range(2, 4))
+                alarm_pass(0, last, range(N_TILES // 2, N_TILES))
         finish(last - 1)
         finish(last)

@@ -38,15 +38,18 @@ WIN_CHUNKS = ((0, 1), (1, 2), (2, 4), (4, 6), (6, 8))
 WEG_CHUNKS = ((0, 2), (2, 8))
 POLL_CHUNKS = ((0, 256), (256, 256), (512, 256), (768, 128), (896, 128))
 EMPTIED_BY_VECTOR = ((3, 0), (4, 1))
+EARLY_PAGES = 2
 PASS_SHIFT = 16
 MOVED_ROWS = P - PASS_SHIFT
 
 KIB = 1024
 TABLE_AT = (0, 16 * KIB)
 WIN_CODES_AT = 8 * KIB
-TABLE_SCALES_AT = 32 * KIB
-WIN_RAW_AT = 40 * KIB
-READINGS_AT = 56 * KIB
+LATE_PAGES_AT = (32 * KIB, 42 * KIB)
+WIN_BF_AT = 40 * KIB
+TABLE_SCALES_AT = 39 * KIB
+WIN_RAW_AT = 50 * KIB
+READINGS_AT = 66 * KIB
 
 
 def tile_list_router_queue_alarms_kernel(
@@ -76,10 +79,7 @@ def tile_list_router_queue_alarms_kernel(
 
         table = [placed(f"table{a}", T, I32, TABLE_AT[a]) for a in range(K_PASSES)]
         table_scales = placed("table_scales", T, U8, TABLE_SCALES_AT)
-        picked = [
-            [sbuf("picked0_0", BANK, U32), placed("picked0_1", BANK, U32, TABLE_SCALES_AT)],
-            [placed("picked1_0", BANK, U32, TABLE_SCALES_AT + 4 * BANK), sbuf("picked1_1", BANK, U32)],
-        ]
+        picked = [tiles(f"picked{a}_", HALVES, BANK, U32) for a in range(K_PASSES)]
         picked_scales = tiles("picked_scales", K_PASSES, S, U8)
 
         def win_raw_at(lo, hi, a):
@@ -95,11 +95,12 @@ def tile_list_router_queue_alarms_kernel(
             for lo, hi in WIN_CHUNKS
         ]
         second_quarter = placed("second_quarter", QUARTER, F32, win_raw_at(*WIN_CHUNKS[1], K_PASSES - 1))
+        first_staged = placed("first_staged", BANK, F32, win_raw_at(*WIN_CHUNKS[0], K_PASSES - 1))
         woven_weights = placed("woven_weights", PACK * S, F32, WIN_RAW_AT)
         landing = [
             placed(f"landing{first}", PACK * count, F32, WIN_RAW_AT + 4 * PACK * first) for first, count in POLL_CHUNKS
         ]
-        win_bf = sbuf("win_bf", K_PASSES * PASS, BF16)
+        win_bf = placed("win_bf", K_PASSES * PASS, BF16, WIN_BF_AT)
         win_codes = [sbuf("win_codes0", K_PASSES * P, U32)] + [
             placed(f"win_codes{u}", K_PASSES * P, U32, WIN_CODES_AT + KIB * u) for u in range(1, ROW_TILES)
         ]
@@ -111,7 +112,9 @@ def tile_list_router_queue_alarms_kernel(
         slot_weights = sbuf("slot_weights", S, F32)
         baseline = tiles("baseline", TILES_PER_PASS, M, F32)
         woven_baseline = [placed(f"woven_baseline{t}", M, F32, TABLE_AT[1] + 4 * M * t) for t in range(PACK)]
-        pages = tiles("page", PACK, T2, F32)
+        pages = tiles("page", EARLY_PAGES, T2, F32) + [
+            placed(f"page{t}", T2, F32, LATE_PAGES_AT[t - EARLY_PAGES]) for t in range(EARLY_PAGES, PACK)
+        ]
         readings = [placed(f"readings{t}", S, F32, READINGS_AT + 4 * S * t) for t in range(PACK)]
         spare_reading = sbuf("spare_reading", BANK, F32)
         polled = tiles("polled", TILES_PER_PASS, M, F32)
@@ -143,7 +146,7 @@ def tile_list_router_queue_alarms_kernel(
         nc.vector.memset(weg_sc[1][:].bitcast(I32), 0)
         nc.vector.memset(vectors[:], 0.0)
         nc.vector.memset(wal_sc[:].bitcast(I32), 0)
-        for page in pages:
+        for page in pages[:EARLY_PAGES]:
             nc.vector.memset(page[:].bitcast(I32), 0)
         make_identity(nc, identity[:])
 
@@ -180,27 +183,26 @@ def tile_list_router_queue_alarms_kernel(
             nc.sync.dma_start(out=baseline[u][:], in_=base[u * P : (u + 1) * P, :])
 
         nc.sync.dma_start(idx[:], offs)
-        nc.sync.dma_start(idx2[:], offs2)
-        nc.sync.dma_start(idx3[:], offs3)
-        load_weg(0)
+        load_table(0, slice(0, T // 2))
         nc.sync.dma_start(out=first_drain[:], in_=drain[0:P].rearrange("(p o) -> p o", o=1))
-        for part in range(FIRST_PASS_PARTS):
-            load_table(0, slice(part * T // FIRST_PASS_PARTS, (part + 1) * T // FIRST_PASS_PARTS))
+        nc.sync.dma_start(idx2[:], offs2)
         for r in range(4):
             nc.sync.dma_start(
                 out=table_scales[r:P:PASS_SHIFT, :].bitcast(I32),
                 in_=tab_scales.bitcast(I32).rearrange("a (q r) c -> r q a c", r=4)[r],
             )
-        load_win(0)
-        load_table(1, slice(0, T // 2))
+        load_table(0, slice(T // 2, T))
+        load_table(1, slice(0, T))
         load_weg_scales(0)
-        load_table(1, slice(T // 2, T))
+        load_weg(0)
+        load_win(0)
         nc.sync.dma_start(out=slot_weights[:, 0:QUARTER], in_=wgs[:, 0:QUARTER])
         load_win(1)
         nc.sync.dma_start(out=vectors[0:ROW_TILES, :], in_=drain.rearrange("(u p) -> u p", p=P))
         nc.sync.dma_start(out=vectors[ROW_TILES : ROW_TILES + N_TILES, :], in_=bias.rearrange("(c p) -> c p", p=P))
         nc.sync.dma_start(out=slot_weights[:, QUARTER:S], in_=wgs[:, QUARTER:S])
         load_win(2)
+        nc.sync.dma_start(idx3[:], offs3)
         load_base(0)
         load_weg(1)
         load_weg_scales(1)
@@ -226,46 +228,55 @@ def tile_list_router_queue_alarms_kernel(
         def halves(half):
             return slice(half * BANK, (half + 1) * BANK)
 
-        def quantize_win(u, staged):
+        def cast_win(u, a, staged):
             chunk = chunk_of(WIN_CHUNKS, u)
             first = (u - WIN_CHUNKS[chunk][0]) * P
             lines = slice(first // LINE, (first + P) // LINE)
+            nc.scalar.copy(
+                staged[:, a * PASS : (a + 1) * PASS].rearrange("p (c e i) -> p c i e", i=PACK, e=LINE),
+                win_raw[chunk][a][:].rearrange("p (i c e) -> p c i e", i=PACK, e=LINE)[:, lines, :, :],
+            )
+
+        def quantize_win(u, staged):
             for a in range(K_PASSES):
-                nc.scalar.copy(
-                    staged[:, a * PASS : (a + 1) * PASS].rearrange("p (c e i) -> p c i e", i=PACK, e=LINE),
-                    win_raw[chunk][a][:].rearrange("p (i c e) -> p c i e", i=PACK, e=LINE)[:, lines, :, :],
-                )
+                cast_win(u, a, staged)
             nc.vector.quantize_mx(out=win_codes[u][:].bitcast(FP8X4), scales=win_scales[u][:], in_=staged)
 
         def gather_words(a, half):
             nc.vector.tensor_copy(picked[a][half][:], table[a][:].bitcast(U32).indirect(entries(idx, half * BANK, BANK)))
 
-        def project(u, half, pair, at=0, count=BANK):
+        def ingress_pass(u, a, half, bank, at, count):
+            nc.tensor.matmul_mx(
+                out=bank[:, 0:count],
+                lhsT=win_codes[u][:, columns(a)].bitcast(FP8X4),
+                lhsT_scale=win_scales[u][:, columns(a)],
+                rhs=picked[a][half][:, at : at + count].bitcast(FP8X4),
+                rhs_scale=picked_scales[a][:, half * BANK + at : half * BANK + at + count],
+                start=a == 0,
+                stop=a == K_PASSES - 1,
+            )
+
+        def egress_pass(u, a, half, bank, at, count):
             chunk = chunk_of(WEG_CHUNKS, u)
             lo, hi = WEG_CHUNKS[chunk]
-            for a in range(K_PASSES):
+            first = 2 * P * (a * (hi - lo) + u - lo)
+            width = BANK if count == BANK else P
+            for lo_port in range(0, count, width):
+                port = at + lo_port
                 nc.tensor.matmul_mx(
-                    out=pair[0][:, 0:count],
-                    lhsT=win_codes[u][:, columns(a)].bitcast(FP8X4),
-                    lhsT_scale=win_scales[u][:, columns(a)],
-                    rhs=picked[a][half][:, at : at + count].bitcast(FP8X4),
-                    rhs_scale=picked_scales[a][:, half * BANK + at : half * BANK + at + count],
-                    start=a == 0,
-                    stop=a == K_PASSES - 1,
+                    out=bank[:, lo_port : lo_port + width],
+                    lhsT=weg_codes[chunk][:, first : first + 2 * P].bitcast(FP4X4),
+                    lhsT_scale=weg_sc[chunk][:, first // 2 : first // 2 + P],
+                    rhs=picked[a][half][:, port : port + width].bitcast(FP8X4),
+                    rhs_scale=picked_scales[a][:, half * BANK + port : half * BANK + port + width],
+                    start=a == 0 and lo_port == 0,
+                    stop=a == K_PASSES - 1 and lo_port + width == count,
                 )
-                first = 2 * P * (a * (hi - lo) + u - lo)
-                width = BANK if count == BANK else P
-                for lo_port in range(0, count, width):
-                    port = at + lo_port
-                    nc.tensor.matmul_mx(
-                        out=pair[1][:, lo_port : lo_port + width],
-                        lhsT=weg_codes[chunk][:, first : first + 2 * P].bitcast(FP4X4),
-                        lhsT_scale=weg_sc[chunk][:, first // 2 : first // 2 + P],
-                        rhs=picked[a][half][:, port : port + width].bitcast(FP8X4),
-                        rhs_scale=picked_scales[a][:, half * BANK + port : half * BANK + port + width],
-                        start=a == 0 and lo_port == 0,
-                        stop=a == K_PASSES - 1 and lo_port + width == count,
-                    )
+
+        def project(u, half, pair):
+            for a in range(K_PASSES):
+                ingress_pass(u, a, half, pair[0], 0, BANK)
+                egress_pass(u, a, half, pair[1], 0, BANK)
 
         def scatter(t, first, count, values, weights):
             nc.vector.tensor_tensor(pages[t][:].indirect(entries(idx2, first, count)), values, weights, ALU.mult)
@@ -279,34 +290,46 @@ def tile_list_router_queue_alarms_kernel(
             nc.vector.quantize_mx(out=z_codes[b][i][:].bitcast(FP8X4), scales=z_scales[b][i][:], in_=staged)
 
         nc.scalar.activation(minus_first_drain[:], first_drain[:], ACT.Copy, scale=-1.0)
-        gather_words(0, 0)
         nc.vector.tensor_copy(picked_scales[0][:], table_scales[:].indirect(idx[:]))
         nc.scalar.dma_start(
             out=picked_scales[1][0:MOVED_ROWS, :].bitcast(I32), in_=picked_scales[0][PASS_SHIFT:P, :].bitcast(I32)
         )
-        gather_words(0, 1)
-        quantize_win(0, win_bf[:])
+        for half in range(HALVES):
+            gather_words(0, half)
+        for page in pages[EARLY_PAGES:]:
+            nc.vector.memset(page[:].bitcast(I32), 0)
         for half in range(HALVES):
             gather_words(1, half)
+        for a in range(K_PASSES):
+            cast_win(0, a, win_bf[:])
+            nc.vector.quantize_mx(
+                out=win_codes[0][:, columns(a)].bitcast(FP8X4),
+                scales=win_scales[0][:, columns(a)],
+                in_=win_bf[:, a * PASS : (a + 1) * PASS],
+            )
 
         def first_products(half, pair, staged, at, count):
-            project(0, half, pair, at, count)
-            nc.scalar.copy(staged, pair[0][:, 0:count])
+            for a in range(K_PASSES):
+                egress_pass(0, a, half, pair[1], at, count)
+            nc.scalar.activation(staged, pair[1][:, 0:count], ACT.Copy, scale=minus_first_drain[:])
+            for a in range(K_PASSES):
+                ingress_pass(0, a, half, pair[0], at, count)
 
         def first_difference(pair, staged, difference, count):
-            nc.vector.scalar_tensor_tensor(difference, pair[1][:, 0:count], minus_first_drain[:], staged, ALU.mult, ALU.add)
+            nc.vector.tensor_tensor(difference, pair[0][:, 0:count], staged, ALU.add)
 
         low, high = slice(0, QUARTER), slice(QUARTER, BANK)
-        first_products(0, banks[0:2], ingress[2][:, low], 0, QUARTER)
-        first_products(0, banks[2:4], ingress[2][:, high], QUARTER, QUARTER)
-        first_difference(banks[0:2], ingress[2][:, low], ingress[3][:, low], QUARTER)
-        first_difference(banks[2:4], ingress[2][:, high], drained[2][:, low], QUARTER)
+        first_products(0, banks[0:2], first_staged[:, low], 0, QUARTER)
+        first_products(0, banks[2:4], first_staged[:, high], QUARTER, QUARTER)
+        first_difference(banks[0:2], first_staged[:, low], ingress[3][:, low], QUARTER)
+        first_difference(banks[2:4], first_staged[:, high], drained[2][:, low], QUARTER)
         nc.scalar.activation(drained[3][:, low], ingress[3][:, low], ACT.Abs)
-        first_products(1, banks[4:6], ingress[3][:], 0, BANK)
+        second_pair = (banks[2], banks[0])
+        first_products(1, second_pair, ingress[3][:], 0, BANK)
         scatter(0, 0, QUARTER, drained[3][:, low], slot_weights[:, low])
-        quantize_win(1, ingress[2][:].bitcast(BF16))
+        quantize_win(1, first_staged[:].bitcast(BF16))
         nc.scalar.activation(second_quarter[:], drained[2][:, low], ACT.Abs)
-        first_difference(banks[4:6], ingress[3][:], drained[3][:], BANK)
+        first_difference(second_pair, ingress[3][:], drained[3][:], BANK)
         scatter(0, QUARTER, QUARTER, second_quarter[:], slot_weights[:, high])
         nc.tensor.transpose(banks[1][:, 0:P], vectors[:], identity[:])
         nc.scalar.activation(minus_drain[:], banks[1][:, 0:ROW_TILES], ACT.Copy, scale=-1.0)
@@ -335,7 +358,7 @@ def tile_list_router_queue_alarms_kernel(
             2: [turned[2][:], turned[3][:]],
             3: [turned[0][:], turned[1][:]],
         }
-        product_banks = {1: (banks[0:2], banks[0:2]), 2: (banks[0:2], banks[2:4]), 3: (banks[0:2], banks[2:4])}
+        product_banks = {1: (banks[6:8], banks[6:8]), 2: (banks[0:2], banks[2:4]), 3: (banks[0:2], banks[2:4])}
         difference_banks = banks[4:6]
         return_banks = {1: banks[2:4], 2: banks[6:8], 3: banks[6:8]}
 

@@ -37,19 +37,18 @@ FIRST_PASS_PARTS = 4
 WIN_CHUNKS = ((0, 1), (1, 2), (2, 4), (4, 6), (6, 8))
 WEG_CHUNKS = ((0, 2), (2, 8))
 POLL_CHUNKS = ((0, 256), (256, 256), (512, 256), (768, 128), (896, 128))
-EMPTIED_BY_VECTOR = ((3, 0), (4, 1))
-EARLY_PAGES = 2
+EMPTIED_BY_VECTOR = ((4, 1),)
 PASS_SHIFT = 16
 MOVED_ROWS = P - PASS_SHIFT
 
 KIB = 1024
 TABLE_AT = (0, 16 * KIB)
 WIN_CODES_AT = 8 * KIB
-LATE_PAGES_AT = (32 * KIB, 42 * KIB)
-WIN_BF_AT = 40 * KIB
-TABLE_SCALES_AT = 39 * KIB
-WIN_RAW_AT = 50 * KIB
-READINGS_AT = 66 * KIB
+TABLE_SCALES_AT = 32 * KIB
+WIN_BF_AT = TABLE_SCALES_AT
+WIN_RAW_AT = 40 * KIB
+LATE_Z_CODES_AT = (0, 4 * KIB, 5 * KIB)
+READINGS_AT = 56 * KIB
 
 
 def tile_list_router_queue_alarms_kernel(
@@ -112,9 +111,7 @@ def tile_list_router_queue_alarms_kernel(
         slot_weights = sbuf("slot_weights", S, F32)
         baseline = tiles("baseline", TILES_PER_PASS, M, F32)
         woven_baseline = [placed(f"woven_baseline{t}", M, F32, TABLE_AT[1] + 4 * M * t) for t in range(PACK)]
-        pages = tiles("page", EARLY_PAGES, T2, F32) + [
-            placed(f"page{t}", T2, F32, LATE_PAGES_AT[t - EARLY_PAGES]) for t in range(EARLY_PAGES, PACK)
-        ]
+        pages = tiles("page", PACK, T2, F32)
         readings = [placed(f"readings{t}", S, F32, READINGS_AT + 4 * S * t) for t in range(PACK)]
         spare_reading = sbuf("spare_reading", BANK, F32)
         polled = tiles("polled", TILES_PER_PASS, M, F32)
@@ -125,14 +122,16 @@ def tile_list_router_queue_alarms_kernel(
         z_bf = tiles("z_bf", QUARTERS, QUARTER * PACK, BF16)
         z_codes = [
             [sbuf("z_codes0_0", QUARTER, U32)]
-            + [placed(f"z_codes0_{q}", QUARTER, U32, READINGS_AT + 4 * S * (q - 1)) for q in range(1, QUARTERS)],
+            + [placed(f"z_codes0_{q}", QUARTER, U32, WIN_RAW_AT + LATE_Z_CODES_AT[q - 1]) for q in range(1, QUARTERS)],
             [sbuf(f"z_codes1_{first}", count, U32) for first, count in POLL_CHUNKS],
         ]
         z_scales = [
             tiles("z_scales0_", QUARTERS, QUARTER, U8),
             [sbuf(f"z_scales1_{first}", count, U8) for first, count in POLL_CHUNKS],
         ]
-        results = [placed(f"result{i}", BANK, F32, TABLE_AT[0] + 4 * BANK * i) for i in range(len(banks))]
+        results_at = [TABLE_AT[0] + 4 * BANK * i for i in range(len(banks))]
+        results_at[2:4] = [WIN_RAW_AT + 4 * PACK * POLL_CHUNKS[2][0] + 4 * BANK * g for g in range(2)]
+        results = [placed(f"result{i}", BANK, F32, at) for i, at in enumerate(results_at)]
         vectors = sbuf("vectors", P, F32)
         first_drain = sbuf("first_drain", 1, F32)
         minus_first_drain = sbuf("minus_first_drain", 1, F32)
@@ -140,15 +139,17 @@ def tile_list_router_queue_alarms_kernel(
         bias_col = sbuf("bias_col", N_TILES, F32)
         identity = sbuf("identity", P, F32)
 
-        nc.vector.memset(table_scales[:].bitcast(I32), 0)
-        nc.vector.memset(weg_sc[0][:].bitcast(I32), 0)
-        nc.vector.memset(picked_scales[1][:].bitcast(I32), 0)
-        nc.vector.memset(weg_sc[1][:].bitcast(I32), 0)
-        nc.vector.memset(vectors[:], 0.0)
-        nc.vector.memset(wal_sc[:].bitcast(I32), 0)
-        for page in pages[:EARLY_PAGES]:
-            nc.vector.memset(page[:].bitcast(I32), 0)
+        nc.gpsimd.memset(table_scales[:].bitcast(I32), 0)
+        nc.gpsimd.memset(weg_sc[0][:].bitcast(I32), 0)
+        nc.gpsimd.memset(picked_scales[1][:].bitcast(I32), 0)
+        nc.gpsimd.memset(weg_sc[1][:].bitcast(I32), 0)
+        nc.gpsimd.memset(vectors[:], 0.0)
+        nc.gpsimd.memset(wal_sc[:].bitcast(I32), 0)
         make_identity(nc, identity[:])
+        nc.gpsimd.memset(pages[PACK - 1][:].bitcast(I32), 0)
+        for page in pages[: PACK - 1]:
+            nc.vector.memset(page[:, 0 : T2 // 2 - 1].bitcast(I32), 0)
+            nc.vector.memset(page[:, T2 // 2 - 1 : T2].bitcast(I32), 0)
 
         def load_scales(scale_tile, scales):
             for quad in range(QUADS):
@@ -296,8 +297,6 @@ def tile_list_router_queue_alarms_kernel(
         )
         for half in range(HALVES):
             gather_words(0, half)
-        for page in pages[EARLY_PAGES:]:
-            nc.vector.memset(page[:].bitcast(I32), 0)
         for half in range(HALVES):
             gather_words(1, half)
         for a in range(K_PASSES):
@@ -384,11 +383,6 @@ def tile_list_router_queue_alarms_kernel(
         def poll_plain(u):
             poll(u, 0, M, polled[u][:], baseline[u])
 
-        def finish_plain(u):
-            both_halves(plain_reading, u)
-            scatter(u, 0, S, readings[u][:], slot_weights[:])
-            poll_plain(u)
-
         def woven_slot(v):
             return (v + 2) % SLOTS
 
@@ -404,12 +398,14 @@ def tile_list_router_queue_alarms_kernel(
                 turned[c][:].rearrange("j (t p) -> j t p", t=PACK), bank[:].rearrange("j (p t) -> j t p", t=PACK), ACT.Abs
             )
 
+        elsewhere = {(0, 0): polled[3][:, 0:QUARTER], (0, PACK - 1): spare_reading[:]}
+
         def woven_reading(half, t, at=0, count=BANK):
             bank = banks[6 + t % 2]
             for c in range(at // P, (at + count) // P):
                 nc.tensor.transpose(bank[:, columns(c)], turned[c][:, columns(t)], identity[:])
             first = half * BANK + at
-            values = spare_reading[:] if (half, t) == (0, PACK - 1) else readings[t][:, first : first + count]
+            values = elsewhere.get((first, t), readings[t][:, first : first + count])
             nc.scalar.copy(values, bank[:, at : at + count])
             scatter(t, first, count, values, woven_weights[:, t * S + first : t * S + first + count])
 
@@ -432,7 +428,6 @@ def tile_list_router_queue_alarms_kernel(
                 z_bf[q][:].bitcast(F32).rearrange("p (c m w) -> p c m w", c=2, w=2),
                 word_bank[:].rearrange("p (c w m) -> p c m w", c=2, w=2),
             )
-            quantize_z(0, q, z_bf[q][:])
 
         plain_products(1, 0)
         plain_difference(1, 0)
@@ -449,9 +444,11 @@ def tile_list_router_queue_alarms_kernel(
             quantize_win(TILES_PER_PASS + v, polled[1][:, halves(v)].bitcast(BF16))
         poll_plain(1)
         both_halves(plain_difference, 2)
+        both_halves(plain_reading, 2)
+        scatter(2, 0, S, readings[2][:], slot_weights[:])
         for v in (2, 3):
-            quantize_win(TILES_PER_PASS + v, z_bf[v - 2][:])
-        finish_plain(2)
+            quantize_win(TILES_PER_PASS + v, polled[2][:, halves(v - 2)].bitcast(BF16))
+        poll_plain(2)
         for quad in range(QUADS):
             nc.sync.dma_start(
                 out=woven_weights[QUAD * quad : QUAD * (quad + 1), :], in_=wgs.rearrange("(p t) j -> p (t j)", t=PACK)
@@ -462,7 +459,8 @@ def tile_list_router_queue_alarms_kernel(
         both_halves(plain_difference, 3)
         for v in (0, 1):
             woven_products(0, v)
-        finish_plain(3)
+        both_halves(plain_reading, 3)
+        scatter(3, 0, S, readings[3][:], slot_weights[:])
         for v in (2, 3):
             woven_products(0, v)
         for q in range(2):
@@ -470,6 +468,8 @@ def tile_list_router_queue_alarms_kernel(
                 woven_difference(c)
             for t in (0, 1):
                 woven_reading(0, t, q * QUARTER, QUARTER)
+                if (q, t) == (0, 0):
+                    poll_plain(3)
         for t in range(PACK):
             if t > 1:
                 woven_reading(0, t)
@@ -522,11 +522,10 @@ def tile_list_router_queue_alarms_kernel(
                     in_=result[:, used].rearrange("p (c m) -> p c m", c=per_bank),
                 )
 
-        woven_bf = [landing[3][:].bitcast(BF16), landing[4][:].bitcast(BF16), z_bf[0][:], z_bf[1][:, 0:PASS], z_bf[2][:, 0:PASS]]
+        woven_bf = [landing[i + 2][:].bitcast(BF16)[:, 0 : PACK * QUARTER] for i in range(3)] + [z_bf[1][:, 0:PASS], z_bf[2][:, 0:PASS]]
         last = len(POLL_CHUNKS) - 1
-        for i in range(last):
-            alarm_pass(0, i)
-        alarm_pass(0, last, range(N_TILES // 2))
+        quantize_z(0, 0, z_bf[0][:])
+        alarm_pass(0, 0)
         for i, (first, count) in enumerate(POLL_CHUNKS):
             for t in range(PACK):
                 poll(t, first, count, landing[i][:, t * count : (t + 1) * count], woven_baseline[t])
@@ -539,7 +538,10 @@ def tile_list_router_queue_alarms_kernel(
             quantize_z(1, i, woven_bf[i])
             if i < last - 1:
                 finish(i)
-            if i == 0:
-                alarm_pass(0, last, range(N_TILES // 2, N_TILES))
+            for q in {0: (1,), 1: (2, 3)}.get(i, ()):
+                quantize_z(0, q, z_bf[q][:])
+                for j in range(len(POLL_CHUNKS)):
+                    if POLL_CHUNKS[j][0] // QUARTER == q:
+                        alarm_pass(0, j)
         finish(last - 1)
         finish(last)

from contextlib import ExitStack

import concourse.mybir as mybir
from concourse.masks import make_identity

K, T, S, H, T2, M, N = 1024, 4096, 1024, 1024, 2048, 1024, 512
FLOPS = 2 * (2 * K * H * S + H * N * M)

F32 = mybir.dt.float32
BF16 = mybir.dt.bfloat16
I32 = mybir.dt.int32
U32 = mybir.dt.uint32
U16 = mybir.dt.uint16
U8 = mybir.dt.uint8
FP8X4 = mybir.dt.float8_e4m3fn_x4
FP4X4 = mybir.dt.float4_e2m1fn_x4
ALU = mybir.AluOpType
ACT = mybir.ActivationFunctionType

P = 128
PACK = 4
PASS = P * PACK
BANK = 512
QUADS, QUAD = 4, 32
K_PASSES = K // PASS
R_PASSES = H // PASS
ROW_TILES = H // P
TILES_PER_PASS = PASS // P
N_TILES = N // P
HALVES = S // BANK
PER_COLUMN = 16
QUARTER = 256
QUARTERS = M // QUARTER
LINE = 4
SLOTS = 4
FIRST_PASS_PARTS = 4
WIN_CHUNKS = ((0, 1), (1, 2), (2, 4), (4, 6), (6, 8))
WEG_CHUNKS = ((0, 2), (2, 8))
POLL_CHUNKS = ((0, 256), (256, 256), (512, 256), (768, 128), (896, 128))
EMPTIED_BY_VECTOR = ((4, 1),)
PASS_SHIFT = 16
MOVED_ROWS = P - PASS_SHIFT

KIB = 1024
TABLE_AT = (0, 16 * KIB)
WIN_CODES_AT = 8 * KIB
TABLE_SCALES_AT = 32 * KIB
WIN_BF_AT = TABLE_SCALES_AT
WIN_RAW_AT = 40 * KIB
LATE_Z_CODES_AT = (0, 4 * KIB, 5 * KIB)
READINGS_AT = 56 * KIB


def tile_list_router_queue_alarms_kernel(
    tc, tab_words, tab_scales, offs, win, weg_words, weg_scales, drain, wgs, offs2, offs3, base,
    wal_words, wal_scales, bias, out,
):
    nc = tc.nc
    with ExitStack() as ctx:
        held = ctx.enter_context(tc.tile_pool(name="held", bufs=1))
        shared = ctx.enter_context(tc.tile_pool(name="shared", bufs=1))
        psum = ctx.enter_context(tc.psum_pool(name="psum", bufs=1))

        def sbuf(name, width, dtype):
            return held.tile([P, width], dtype, name=name, align_bytes=64)

        def tiles(name, count, width, dtype):
            return [sbuf(f"{name}{i}", width, dtype) for i in range(count)]

        def placed(name, width, dtype, offset):
            return shared.tile([P, width], dtype, name=name, align_bytes=64, offset=offset)

        banks = [psum.tile([P, BANK], F32, name=f"bank{i}") for i in range(8)]

        idx = held.tile([P, S // PER_COLUMN], U16, name="idx")
        idx2 = held.tile([P, S // PER_COLUMN], U16, name="idx2")
        idx3 = held.tile([P, M // PER_COLUMN], U16, name="idx3")

        table = [placed(f"table{a}", T, I32, TABLE_AT[a]) for a in range(K_PASSES)]
        table_scales = placed("table_scales", T, U8, TABLE_SCALES_AT)
        picked = [tiles(f"picked{a}_", HALVES, BANK, U32) for a in range(K_PASSES)]
        picked_scales = tiles("picked_scales", K_PASSES, S, U8)

        def win_raw_at(lo, hi, a):
            return WIN_RAW_AT + 4 * PASS * (K_PASSES * lo + a * (hi - lo))

        win_raw = [
            [
                placed(f"win_raw{lo}_{a}", PASS * (hi - lo), F32, win_raw_at(lo, hi, a))
                if hi <= TILES_PER_PASS
                else sbuf(f"win_raw{lo}_{a}", PASS * (hi - lo), F32)
                for a in range(K_PASSES)
            ]
            for lo, hi in WIN_CHUNKS
        ]
        second_quarter = placed("second_quarter", QUARTER, F32, win_raw_at(*WIN_CHUNKS[1], K_PASSES - 1))
        first_staged = placed("first_staged", BANK, F32, win_raw_at(*WIN_CHUNKS[0], K_PASSES - 1))
        woven_weights = placed("woven_weights", PACK * S, F32, WIN_RAW_AT)
        landing = [
            placed(f"landing{first}", PACK * count, F32, WIN_RAW_AT + 4 * PACK * first) for first, count in POLL_CHUNKS
        ]
        win_bf = placed("win_bf", K_PASSES * PASS, BF16, WIN_BF_AT)
        win_codes = [sbuf("win_codes0", K_PASSES * P, U32)] + [
            placed(f"win_codes{u}", K_PASSES * P, U32, WIN_CODES_AT + KIB * u) for u in range(1, ROW_TILES)
        ]
        win_scales = tiles("win_scales", ROW_TILES, K_PASSES * P, U8)
        weg_codes = [sbuf(f"weg_codes{lo}", K_PASSES * 2 * P * (hi - lo), U8) for lo, hi in WEG_CHUNKS]
        weg_sc = [sbuf(f"weg_sc{lo}", K_PASSES * P * (hi - lo), U8) for lo, hi in WEG_CHUNKS]
        wal_codes = sbuf("wal_codes", R_PASSES * N, I32)
        wal_sc = sbuf("wal_sc", R_PASSES * N, U8)
        slot_weights = sbuf("slot_weights", S, F32)
        baseline = tiles("baseline", TILES_PER_PASS, M, F32)
        woven_baseline = [placed(f"woven_baseline{t}", M, F32, TABLE_AT[1] + 4 * M * t) for t in range(PACK)]
        pages = tiles("page", PACK, T2, F32)
        readings = [placed(f"readings{t}", S, F32, READINGS_AT + 4 * S * t) for t in range(PACK)]
        spare_reading = sbuf("spare_reading", BANK, F32)
        polled = tiles("polled", TILES_PER_PASS, M, F32)
        ingress = tiles("ingress", SLOTS, BANK, F32)
        drained = tiles("drained", SLOTS, BANK, F32)
        turned = tiles("turned", BANK // P, BANK, F32)
        z_rows = tiles("z_rows", 4, PASS, BF16)
        z_bf = tiles("z_bf", QUARTERS, QUARTER * PACK, BF16)
        z_codes = [
            [sbuf("z_codes0_0", QUARTER, U32)]
            + [placed(f"z_codes0_{q}", QUARTER, U32, WIN_RAW_AT + LATE_Z_CODES_AT[q - 1]) for q in range(1, QUARTERS)],
            [sbuf(f"z_codes1_{first}", count, U32) for first, count in POLL_CHUNKS],
        ]
        z_scales = [
            tiles("z_scales0_", QUARTERS, QUARTER, U8),
            [sbuf(f"z_scales1_{first}", count, U8) for first, count in POLL_CHUNKS],
        ]
        results_at = [TABLE_AT[0] + 4 * BANK * i for i in range(len(banks))]
        results_at[2:4] = [WIN_RAW_AT + 4 * PACK * POLL_CHUNKS[2][0] + 4 * BANK * g for g in range(2)]
        results = [placed(f"result{i}", BANK, F32, at) for i, at in enumerate(results_at)]
        vectors = sbuf("vectors", P, F32)
        first_drain = sbuf("first_drain", 1, F32)
        minus_first_drain = sbuf("minus_first_drain", 1, F32)
        minus_drain = sbuf("minus_drain", ROW_TILES, F32)
        bias_col = sbuf("bias_col", N_TILES, F32)
        identity = sbuf("identity", P, F32)

        nc.gpsimd.memset(table_scales[:].bitcast(I32), 0)
        nc.gpsimd.memset(weg_sc[0][:].bitcast(I32), 0)
        nc.gpsimd.memset(picked_scales[1][:].bitcast(I32), 0)
        nc.gpsimd.memset(weg_sc[1][:].bitcast(I32), 0)
        nc.gpsimd.memset(vectors[:], 0.0)
        nc.gpsimd.memset(wal_sc[:].bitcast(I32), 0)
        make_identity(nc, identity[:])
        nc.gpsimd.memset(pages[PACK - 1][:].bitcast(I32), 0)
        for page in pages[: PACK - 1]:
            nc.vector.memset(page[:, 0 : T2 // 2 - 1].bitcast(I32), 0)
            nc.vector.memset(page[:, T2 // 2 - 1 : T2].bitcast(I32), 0)

        def load_scales(scale_tile, scales):
            for quad in range(QUADS):
                nc.sync.dma_start(
                    out=scale_tile[QUAD * quad : QUAD * quad + 4, :].bitcast(I32).rearrange("q (a c) -> q a c", a=2),
                    in_=scales[:, 4 * quad : 4 * quad + 4, :].bitcast(I32).rearrange("a q c -> q a c"),
                )

        def load_table(a, part):
            nc.sync.dma_start(out=table[a][:, part], in_=tab_words[a].rearrange("p t i -> p (t i)").bitcast(I32)[:, part])

        def load_win(chunk):
            lo, hi = WIN_CHUNKS[chunk]
            for a in range(K_PASSES):
                nc.sync.dma_start(
                    out=win_raw[chunk][a][:].rearrange("p (i r) -> p i r", i=PACK),
                    in_=win[a * PASS : (a + 1) * PASS, lo * P : hi * P].rearrange("(p i) r -> p i r", i=PACK),
                )

        def load_weg(chunk):
            lo, hi = WEG_CHUNKS[chunk]
            nc.sync.dma_start(
                out=weg_codes[chunk][:].bitcast(I32).rearrange("p (a c) -> p a c", a=K_PASSES),
                in_=weg_words[:, :, 2 * lo * P : 2 * hi * P].bitcast(I32).rearrange("a p c -> p a c"),
            )

        def load_weg_scales(chunk):
            lo, hi = WEG_CHUNKS[chunk]
            load_scales(weg_sc[chunk], weg_scales[:, :, lo * P : hi * P])

        def load_base(u):
            nc.sync.dma_start(out=baseline[u][:], in_=base[u * P : (u + 1) * P, :])

        nc.sync.dma_start(idx[:], offs)
        load_table(0, slice(0, T // 2))
        nc.sync.dma_start(out=first_drain[:], in_=drain[0:P].rearrange("(p o) -> p o", o=1))
        nc.sync.dma_start(idx2[:], offs2)
        for r in range(4):
            nc.sync.dma_start(
                out=table_scales[r:P:PASS_SHIFT, :].bitcast(I32),
                in_=tab_scales.bitcast(I32).rearrange("a (q r) c -> r q a c", r=4)[r],
            )
        load_table(0, slice(T // 2, T))
        load_table(1, slice(0, T))
        load_weg_scales(0)
        load_weg(0)
        load_win(0)
        nc.sync.dma_start(out=slot_weights[:, 0:QUARTER], in_=wgs[:, 0:QUARTER])
        load_win(1)
        nc.sync.dma_start(out=vectors[0:ROW_TILES, :], in_=drain.rearrange("(u p) -> u p", p=P))
        nc.sync.dma_start(out=vectors[ROW_TILES : ROW_TILES + N_TILES, :], in_=bias.rearrange("(c p) -> c p", p=P))
        nc.sync.dma_start(out=slot_weights[:, QUARTER:S], in_=wgs[:, QUARTER:S])
        load_win(2)
        nc.sync.dma_start(idx3[:], offs3)
        load_base(0)
        load_weg(1)
        load_weg_scales(1)
        load_win(3)
        load_win(4)
        for u in range(1, TILES_PER_PASS):
            load_base(u)
        nc.sync.dma_start(
            out=wal_codes[:].rearrange("p (b c) -> p b c", b=R_PASSES),
            in_=wal_words.rearrange("b p c i -> p b (c i)").bitcast(I32),
        )
        load_scales(wal_sc, wal_scales)

        def entries(offsets, first, count):
            return offsets[:, first // PER_COLUMN : (first + count) // PER_COLUMN]

        def chunk_of(chunks, u):
            return [c for c, (lo, hi) in enumerate(chunks) if lo <= u < hi][0]

        def columns(c):
            return slice(c * P, (c + 1) * P)

        def halves(half):
            return slice(half * BANK, (half + 1) * BANK)

        def cast_win(u, a, staged):
            chunk = chunk_of(WIN_CHUNKS, u)
            first = (u - WIN_CHUNKS[chunk][0]) * P
            lines = slice(first // LINE, (first + P) // LINE)
            nc.scalar.copy(
                staged[:, a * PASS : (a + 1) * PASS].rearrange("p (c e i) -> p c i e", i=PACK, e=LINE),
                win_raw[chunk][a][:].rearrange("p (i c e) -> p c i e", i=PACK, e=LINE)[:, lines, :, :],
            )

        def quantize_win(u, staged):
            for a in range(K_PASSES):
                cast_win(u, a, staged)
            nc.vector.quantize_mx(out=win_codes[u][:].bitcast(FP8X4), scales=win_scales[u][:], in_=staged)

        def gather_words(a, half):
            nc.vector.tensor_copy(picked[a][half][:], table[a][:].bitcast(U32).indirect(entries(idx, half * BANK, BANK)))

        def ingress_pass(u, a, half, bank, at, count):
            nc.tensor.matmul_mx(
                out=bank[:, 0:count],
                lhsT=win_codes[u][:, columns(a)].bitcast(FP8X4),
                lhsT_scale=win_scales[u][:, columns(a)],
                rhs=picked[a][half][:, at : at + count].bitcast(FP8X4),
                rhs_scale=picked_scales[a][:, half * BANK + at : half * BANK + at + count],
                start=a == 0,
                stop=a == K_PASSES - 1,
            )

        def egress_pass(u, a, half, bank, at, count):
            chunk = chunk_of(WEG_CHUNKS, u)
            lo, hi = WEG_CHUNKS[chunk]
            first = 2 * P * (a * (hi - lo) + u - lo)
            width = BANK if count == BANK else P
            for lo_port in range(0, count, width):
                port = at + lo_port
                nc.tensor.matmul_mx(
                    out=bank[:, lo_port : lo_port + width],
                    lhsT=weg_codes[chunk][:, first : first + 2 * P].bitcast(FP4X4),
                    lhsT_scale=weg_sc[chunk][:, first // 2 : first // 2 + P],
                    rhs=picked[a][half][:, port : port + width].bitcast(FP8X4),
                    rhs_scale=picked_scales[a][:, half * BANK + port : half * BANK + port + width],
                    start=a == 0 and lo_port == 0,
                    stop=a == K_PASSES - 1 and lo_port + width == count,
                )

        def project(u, half, pair):
            for a in range(K_PASSES):
                ingress_pass(u, a, half, pair[0], 0, BANK)
                egress_pass(u, a, half, pair[1], 0, BANK)

        def scatter(t, first, count, values, weights):
            nc.vector.tensor_tensor(pages[t][:].indirect(entries(idx2, first, count)), values, weights, ALU.mult)

        def poll(t, first, count, dst, base_rows):
            nc.vector.tensor_tensor(
                dst, pages[t][:].indirect(entries(idx3, first, count)), base_rows[:, first : first + count], ALU.subtract
            )

        def quantize_z(b, i, staged):
            nc.vector.quantize_mx(out=z_codes[b][i][:].bitcast(FP8X4), scales=z_scales[b][i][:], in_=staged)

        nc.scalar.activation(minus_first_drain[:], first_drain[:], ACT.Copy, scale=-1.0)
        nc.vector.tensor_copy(picked_scales[0][:], table_scales[:].indirect(idx[:]))
        nc.scalar.dma_start(
            out=picked_scales[1][0:MOVED_ROWS, :].bitcast(I32), in_=picked_scales[0][PASS_SHIFT:P, :].bitcast(I32)
        )
        for half in range(HALVES):
            gather_words(0, half)
        for half in range(HALVES):
            gather_words(1, half)
        for a in range(K_PASSES):
            cast_win(0, a, win_bf[:])
            nc.vector.quantize_mx(
                out=win_codes[0][:, columns(a)].bitcast(FP8X4),
                scales=win_scales[0][:, columns(a)],
                in_=win_bf[:, a * PASS : (a + 1) * PASS],
            )

        def first_products(half, pair, staged, at, count):
            for a in range(K_PASSES):
                egress_pass(0, a, half, pair[1], at, count)
            nc.scalar.activation(staged, pair[1][:, 0:count], ACT.Copy, scale=minus_first_drain[:])
            for a in range(K_PASSES):
                ingress_pass(0, a, half, pair[0], at, count)

        def first_difference(pair, staged, difference, count):
            nc.vector.tensor_tensor(difference, pair[0][:, 0:count], staged, ALU.add)

        low, high = slice(0, QUARTER), slice(QUARTER, BANK)
        first_products(0, banks[0:2], first_staged[:, low], 0, QUARTER)
        first_products(0, banks[2:4], first_staged[:, high], QUARTER, QUARTER)
        first_difference(banks[0:2], first_staged[:, low], ingress[3][:, low], QUARTER)
        first_difference(banks[2:4], first_staged[:, high], drained[2][:, low], QUARTER)
        nc.scalar.activation(drained[3][:, low], ingress[3][:, low], ACT.Abs)
        second_pair = (banks[2], banks[0])
        first_products(1, second_pair, ingress[3][:], 0, BANK)
        scatter(0, 0, QUARTER, drained[3][:, low], slot_weights[:, low])
        quantize_win(1, first_staged[:].bitcast(BF16))
        nc.scalar.activation(second_quarter[:], drained[2][:, low], ACT.Abs)
        first_difference(second_pair, ingress[3][:], drained[3][:], BANK)
        scatter(0, QUARTER, QUARTER, second_quarter[:], slot_weights[:, high])
        nc.tensor.transpose(banks[1][:, 0:P], vectors[:], identity[:])
        nc.scalar.activation(minus_drain[:], banks[1][:, 0:ROW_TILES], ACT.Copy, scale=-1.0)
        nc.scalar.copy(bias_col[:], banks[1][:, ROW_TILES : ROW_TILES + N_TILES])
        quantize_win(2, drained[2][:].bitcast(BF16))
        nc.scalar.activation(readings[0][:, halves(1)], drained[3][:], ACT.Abs)
        scatter(0, BANK, BANK, readings[0][:, halves(1)], slot_weights[:, halves(1)])

        def staged_products(u, half, pair, staged_ingress, staged_drained):
            project(u, half, pair)
            nc.scalar.copy(staged_ingress, pair[0][:])
            nc.scalar.activation(staged_drained, pair[1][:], ACT.Copy, scale=minus_drain[:, u : u + 1])

        def add_turned(dst, staged_ingress, staged_drained):
            for term, staged in enumerate((staged_ingress, staged_drained)):
                nc.tensor.matmul(dst, staged, identity[:], start=term == 0, stop=term == 1, is_transpose=True)

        plain_ingress = {
            1: [ingress[0][:], ingress[1][:]],
            2: [z_bf[half][:].bitcast(F32) for half in range(HALVES)],
            3: [ingress[0][:], ingress[1][:]],
        }
        plain_drained = {1: drained[0:2], 2: drained[2:4], 3: drained[0:2]}
        plain_turned = {
            1: [polled[1][:, halves(half)] for half in range(HALVES)],
            2: [turned[2][:], turned[3][:]],
            3: [turned[0][:], turned[1][:]],
        }
        product_banks = {1: (banks[6:8], banks[6:8]), 2: (banks[0:2], banks[2:4]), 3: (banks[0:2], banks[2:4])}
        difference_banks = banks[4:6]
        return_banks = {1: banks[2:4], 2: banks[6:8], 3: banks[6:8]}

        def plain_products(u, half):
            staged_products(u, half, product_banks[u][half], plain_ingress[u][half], plain_drained[u][half][:])

        def plain_difference(u, half):
            bank = difference_banks[half]
            for c in range(BANK // P):
                add_turned(bank[:, columns(c)], plain_ingress[u][half][:, columns(c)], plain_drained[u][half][:, columns(c)])
            nc.scalar.activation(plain_turned[u][half], bank[:], ACT.Abs)

        def plain_reading(u, half):
            bank = return_banks[u][half]
            for c in range(BANK // P):
                nc.tensor.transpose(bank[:, columns(c)], plain_turned[u][half][:, columns(c)], identity[:])
            nc.scalar.copy(readings[u][:, halves(half)], bank[:])

        def both_halves(step, u):
            for half in range(HALVES):
                step(u, half)

        def poll_plain(u):
            poll(u, 0, M, polled[u][:], baseline[u])

        def woven_slot(v):
            return (v + 2) % SLOTS

        def woven_products(half, v):
            pair = banks[2 * (v % 2) : 2 * (v % 2) + 2]
            staged_products(TILES_PER_PASS + v, half, pair, ingress[woven_slot(v)][:], drained[woven_slot(v)][:])

        def woven_difference(c):
            bank = difference_banks[c % 2]
            for v in range(TILES_PER_PASS):
                add_turned(bank[:, columns(v)], ingress[woven_slot(v)][:, columns(c)], drained[woven_slot(v)][:, columns(c)])
            nc.scalar.activation(
                turned[c][:].rearrange("j (t p) -> j t p", t=PACK), bank[:].rearrange("j (p t) -> j t p", t=PACK), ACT.Abs
            )

        elsewhere = {(0, 0): polled[3][:, 0:QUARTER], (0, PACK - 1): spare_reading[:]}

        def woven_reading(half, t, at=0, count=BANK):
            bank = banks[6 + t % 2]
            for c in range(at // P, (at + count) // P):
                nc.tensor.transpose(bank[:, columns(c)], turned[c][:, columns(t)], identity[:])
            first = half * BANK + at
            values = elsewhere.get((first, t), readings[t][:, first : first + count])
            nc.scalar.copy(values, bank[:, at : at + count])
            scatter(t, first, count, values, woven_weights[:, t * S + first : t * S + first + count])

        def turn_plain_z(q):
            word_bank = banks[6 + q % 2]
            rows = [z_rows[(2 * q + c) % len(z_rows)] for c in range(QUARTER // P)]
            for c in range(QUARTER // P):
                for v in range(TILES_PER_PASS):
                    nc.tensor.transpose(difference_banks[c][:, columns(v)], polled[v][:, columns(2 * q + c)], identity[:])
                nc.scalar.activation(
                    rows[c][:].rearrange("m (w p e) -> m w p e", w=2, e=2),
                    difference_banks[c][:].rearrange("m (p w e) -> m w p e", w=2, e=2),
                    ACT.Copy,
                    scale=-1.0,
                )
            for c in range(QUARTER // P):
                for w in range(2):
                    nc.tensor.transpose(word_bank[:, columns(2 * c + w)], rows[c][:].bitcast(F32)[:, columns(w)], identity[:])
            nc.scalar.copy(
                z_bf[q][:].bitcast(F32).rearrange("p (c m w) -> p c m w", c=2, w=2),
                word_bank[:].rearrange("p (c w m) -> p c m w", c=2, w=2),
            )

        plain_products(1, 0)
        plain_difference(1, 0)
        plain_products(1, 1)
        quantize_win(3, drained[3][:].bitcast(BF16))
        poll_plain(0)
        plain_reading(1, 0)
        scatter(1, 0, BANK, readings[1][:, halves(0)], slot_weights[:, halves(0)])
        plain_difference(1, 1)
        plain_reading(1, 1)
        scatter(1, BANK, BANK, readings[1][:, halves(1)], slot_weights[:, halves(1)])
        both_halves(plain_products, 2)
        for v in (0, 1):
            quantize_win(TILES_PER_PASS + v, polled[1][:, halves(v)].bitcast(BF16))
        poll_plain(1)
        both_halves(plain_difference, 2)
        both_halves(plain_reading, 2)
        scatter(2, 0, S, readings[2][:], slot_weights[:])
        for v in (2, 3):
            quantize_win(TILES_PER_PASS + v, polled[2][:, halves(v - 2)].bitcast(BF16))
        poll_plain(2)
        for quad in range(QUADS):
            nc.sync.dma_start(
                out=woven_weights[QUAD * quad : QUAD * (quad + 1), :], in_=wgs.rearrange("(p t) j -> p (t j)", t=PACK)
            )
        for t in range(PACK):
            nc.sync.dma_start(out=woven_baseline[t][:], in_=base[PASS:H, :].rearrange("(p t) m -> p t m", t=PACK)[:, t, :])
        both_halves(plain_products, 3)
        both_halves(plain_difference, 3)
        for v in (0, 1):
            woven_products(0, v)
        both_halves(plain_reading, 3)
        scatter(3, 0, S, readings[3][:], slot_weights[:])
        for v in (2, 3):
            woven_products(0, v)
        for q in range(2):
            for c in (2 * q, 2 * q + 1):
                woven_difference(c)
            for t in (0, 1):
                woven_reading(0, t, q * QUARTER, QUARTER)
                if (q, t) == (0, 0):
                    poll_plain(3)
        for t in range(PACK):
            if t > 1:
                woven_reading(0, t)
            woven_products(1, t)
        for c in range(BANK // P):
            woven_difference(c)
        for t in range(PACK):
            woven_reading(1, t)
            turn_plain_z(t)

        sums = [banks[6:8], banks[4:6], banks[0:2], banks[2:3], [banks[3], banks[6]]]

        def alarm_pass(b, i, score_tiles=range(N_TILES)):
            first, count = POLL_CHUNKS[i]
            per_bank = N_TILES // len(sums[i])
            source, at = (first // QUARTER, first % QUARTER) if b == 0 else (i, 0)
            for c in score_tiles:
                nc.tensor.matmul_mx(
                    out=sums[i][c // per_bank][:, (c % per_bank) * count : (c % per_bank + 1) * count],
                    lhsT=wal_codes[:, b * N + c * P : b * N + (c + 1) * P].bitcast(FP8X4),
                    lhsT_scale=wal_sc[:, b * N + c * P : b * N + (c + 1) * P],
                    rhs=z_codes[b][source][:, at : at + count].bitcast(FP8X4),
                    rhs_scale=z_scales[b][source][:, at : at + count],
                    start=b == 0 and c % per_bank == 0,
                    stop=b == R_PASSES - 1 and c % per_bank == per_bank - 1,
                )

        def finish(i):
            first, count = POLL_CHUNKS[i]
            per_bank = N_TILES // len(sums[i])
            alarm_pass(1, i)
            for g, bank in enumerate(sums[i]):
                result = results[(2 * i + g) % len(results)]
                used = slice(0, per_bank * count)
                if (i, g) in EMPTIED_BY_VECTOR:
                    nc.vector.tensor_tensor(
                        result[:, used].rearrange("p (c m) -> p c m", c=per_bank),
                        bank[:, used].rearrange("p (c m) -> p c m", c=per_bank),
                        bias_col[:, per_bank * g : per_bank * (g + 1)].unsqueeze(2).to_broadcast([P, per_bank, count]),
                        ALU.add,
                    )
                else:
                    for c in range(per_bank):
                        part = slice(c * count, (c + 1) * count)
                        column = bias_col[:, per_bank * g + c : per_bank * g + c + 1]
                        nc.scalar.activation(result[:, part], bank[:, part], ACT.Identity, bias=column)
                scores = slice(per_bank * g * P, per_bank * (g + 1) * P)
                nc.sync.dma_start(
                    out=out[scores, first : first + count].rearrange("(c p) m -> p c m", p=P),
                    in_=result[:, used].rearrange("p (c m) -> p c m", c=per_bank),
                )

        woven_bf = [landing[i + 2][:].bitcast(BF16)[:, 0 : PACK * QUARTER] for i in range(3)] + [z_bf[1][:, 0:PASS], z_bf[2][:, 0:PASS]]
        last = len(POLL_CHUNKS) - 1
        quantize_z(0, 0, z_bf[0][:])
        alarm_pass(0, 0)
        for i, (first, count) in enumerate(POLL_CHUNKS):
            for t in range(PACK):
                poll(t, first, count, landing[i][:, t * count : (t + 1) * count], woven_baseline[t])
            dst = woven_bf[i].rearrange("p (c e t) -> p c t e", t=PACK, e=LINE)
            src = landing[i][:].rearrange("p (t c e) -> p c t e", t=PACK, e=LINE)
            if count < QUARTER:
                nc.vector.tensor_scalar_mul(dst, src, -1.0)
            else:
                nc.scalar.activation(dst, src, ACT.Copy, scale=-1.0)
            quantize_z(1, i, woven_bf[i])
            if i < last - 1:
                finish(i)
            for q in {0: (1,), 1: (2, 3)}.get(i, ()):
                quantize_z(0, q, z_bf[q][:])
                for j in range(len(POLL_CHUNKS)):
                    if POLL_CHUNKS[j][0] // QUARTER == q:
                        alarm_pass(0, j)
        finish(last - 1)
        finish(last)
